import numpy as np
import ml_dtypes


def mxq(x, axis, fmt="e4m3"):
    dtype, down = {"e4m3": (ml_dtypes.float8_e4m3fn, 7), "e5m2": (ml_dtypes.float8_e5m2, 14)}[fmt]
    v = np.moveaxis(np.asarray(x, np.float32).astype(ml_dtypes.bfloat16).astype(np.float64), axis, -1)
    blocks = v.reshape(v.shape[:-1] + (-1, 32))
    amax = np.abs(blocks).max(-1, keepdims=True)
    byte = np.maximum(np.where(amax > 0, np.frexp(amax)[1] - 1 + 127, 0) - down, 1)
    scale = np.exp2(byte - 127.0)
    codes = (blocks / scale).astype(np.float32).astype(dtype).astype(np.float64)
    return np.moveaxis((codes * scale).reshape(v.shape), -1, axis)


WIDE = False


def mx_kscale(k):
    if not WIDE:
        return np.ones(k)
    levels = np.array([10, -10, 5, -5, 0])
    if k % 512:
        return np.exp2(np.random.permutation(np.resize(levels, k // 32))).repeat(32)
    a = np.empty((k // 512, 16))
    for p in range(k // 512):
        a[p, :8] = np.random.permutation(np.resize(levels, 8))
        for g in range(8):
            far = levels[np.abs(levels - a[p, g]) >= 10]
            a[p, g + 8] = far[np.random.randint(len(far))]
    return np.exp2(a.ravel()).repeat(32)


def f64(x):
    return np.asarray(x).astype(np.float64)


def striped(idx):
    return np.tile(idx.reshape(-1, 16).T, (8, 1)).astype(np.uint16)


def unstriped(offs):
    return offs[:16].T.reshape(-1).astype(np.int64)


def striped8(idx):
    return np.concatenate([x.reshape(-1, 16).T for x in idx]).astype(np.uint16)


def runs(offs, k):
    lists = np.stack([offs[16 * r : 16 * r + 16].T.reshape(-1) for r in range(8)]).astype(np.int64)
    return lists[np.arange(k) % 512 // 64]


def pack_weight(w):
    k, n = w.shape
    w = f64(np.asarray(w, np.float32).astype(ml_dtypes.bfloat16)).reshape(k // 32, 32, n)
    amax = np.abs(w).max(1)
    byte = np.clip(np.where(amax > 0, np.frexp(amax)[1] - 1 + 127 - 7, 1), 1, 254)
    scaled = (w * np.exp2(127.0 - byte)[:, None, :]).reshape(k, n).astype(np.float32)
    words = np.ascontiguousarray(scaled.reshape(k // 512, 128, 4, n).transpose(0, 1, 3, 2)).astype(ml_dtypes.float8_e4m3fn).view(np.uint8)
    return words, np.ascontiguousarray(byte.astype(np.uint8).reshape(k // 512, 16, n))


def unpack_weight(words, scales):
    g, p, n, _ = words.shape
    vals = np.ascontiguousarray(words).view(ml_dtypes.float8_e4m3fn).astype(np.float64) * np.repeat(np.exp2(scales.astype(np.float64) - 127.0), 8, axis=1)[..., None]
    return vals.transpose(0, 1, 3, 2).reshape(g * 512, n)


def sigmoid(v):
    return 1.0 / (1.0 + np.exp(-np.maximum(v, -700.0)))


K, T, S, N, G, H = 512, 2048, 512, 512, 2048, 512


def setup_inputs():
    n = np.random.standard_normal
    s = mx_kscale(K)[:, None]
    u = mx_kscale(H)
    packed_xT = pack_weight(n((K, T)) * s)
    packed_dT = pack_weight(n((K, G)) / s)
    return {
        "x_words": packed_xT[0],
        "x_scales": packed_xT[1],
        "d_words": packed_dT[0],
        "d_scales": packed_dT[1],
        "kb": (0.5 * n((H, 1))).astype(np.float32),
        "gn": (np.random.uniform(0.5, 1.5, (H, 1)) * u[:, None]).astype(np.float32),
        "w1": (n((H, N)) / np.sqrt(H) / u[:, None]).astype(np.float32),
        "offs": striped(np.random.permutation(T)[:S]),
        "kidx": striped8(np.random.randint(0, G, (8, H))),
    }


def reference(x_words, x_scales, d_words, d_scales, kb, gn, w1, offs, kidx):
    d_kidx = unpack_weight(d_words, d_scales)[np.arange(K)[:, None], runs(kidx, K)]
    xq = unpack_weight(x_words, x_scales)[:, unstriped(offs)]
    s = 0.0625 * (d_kidx.T @ xq) + f64(kb)
    z = f64(gn) * sigmoid(s)
    return mxq(f64(w1), 0, "e4m3").T @ mxq(z, 0, "e4m3")

@@ -1,0 +1,168 @@
+from contextlib import ExitStack
+
+import concourse.mybir as mybir
+
+K, T, S, N, G, H = 512, 2048, 512, 512, 2048, 512
+FLOPS = 2 * K * H * S + 2 * H * N * S
+
+F32 = mybir.dt.float32
+BF16 = mybir.dt.bfloat16
+U32 = mybir.dt.uint32
+I32 = mybir.dt.int32
+U16 = mybir.dt.uint16
+U8 = mybir.dt.uint8
+FP8X4 = mybir.dt.float8_e4m3fn_x4
+SIGMOID = mybir.ActivationFunctionType.Sigmoid
+MULT = mybir.AluOpType.mult
+
+P = 128
+PACK = 4
+CHUNK = 128
+HALF = 256
+
+
+def tile_picked_sigattn_sigmoid_p_kernel(
+    tc, x_words, x_scales, d_words, d_scales, kb, gn, w1, offs, kidx, out
+):
+    nc = tc.nc
+    with ExitStack() as ctx:
+        keep = ctx.enter_context(tc.tile_pool(name="keep", bufs=1))
+        psum = ctx.enter_context(tc.psum_pool(name="psum", bufs=1))
+
+        kidx_sb = keep.tile([P, H // 16], U16, name="kidx_sb")
+        offs_sb = keep.tile([P, S // 16], U16, name="offs_sb")
+        d_table = keep.tile([P, G], U32, name="d_table", align_bytes=64)
+        x_table = keep.tile([P, T], U32, name="x_table", align_bytes=64)
+        w_raw = keep.tile([P, PACK, N], F32, name="w_raw", align_bytes=64)
+        d_scale_table = keep.tile([P, G], U8, name="d_scale_table", align_bytes=64)
+        x_scale_table = keep.tile([P, T], U8, name="x_scale_table", align_bytes=64)
+        planes = keep.tile([P, H + S], U8, name="planes", align_bytes=64)
+        warm_in = keep.tile([P, 8], F32, name="warm_in")
+        warm_out = keep.tile([P, 8], F32, name="warm_out")
+        kb_sb = keep.tile([P, PACK], F32, name="kb_sb")
+        gn_sb = keep.tile([P, PACK], F32, name="gn_sb")
+
+        nc.gpsimd.memset(d_scale_table[:].bitcast(I32), 0)
+        nc.vector.memset(x_scale_table[:].bitcast(I32), 0)
+        nc.vector.memset(warm_in[:], 0.0)
+        nc.vector.memset(planes[:].bitcast(I32), 0)
+
+        nc.sync.dma_start(kidx_sb[:], kidx)
+        nc.sync.dma_start(offs_sb[:], offs)
+        nc.sync.dma_start(d_scale_table[0:P:8, :].bitcast(I32), d_scales[0].bitcast(I32))
+        nc.sync.dma_start(x_scale_table[0:P:8, :].bitcast(I32), x_scales[0].bitcast(I32))
+        nc.sync.dma_start(d_table[:].bitcast(I32), d_words[0].rearrange("p c r -> p (c r)").bitcast(I32))
+        nc.sync.dma_start(w_raw[:], w1.rearrange("(p j) m -> p j m", j=PACK))
+        nc.sync.dma_start(x_table[:].bitcast(I32), x_words[0].rearrange("p c r -> p (c r)").bitcast(I32))
+        nc.scalar.dma_start(kb_sb[:], kb.rearrange("(p t) o -> p (t o)", t=PACK))
+        nc.scalar.dma_start(gn_sb[:], gn.rearrange("(p t) o -> p (t o)", t=PACK))
+        nc.scalar.activation(warm_out[:], warm_in[:], SIGMOID)
+
+        d_scale_picked = keep.tile([P, H], U8, name="d_scale_picked", align_bytes=64)
+        x_scale_picked = keep.tile([P, S], U8, name="x_scale_picked", align_bytes=64)
+        rows = keep.tile([P, H + S], U8, name="rows", align_bytes=64)
+        nc.vector.tensor_copy(d_scale_picked[:], d_scale_table[:].indirect(kidx_sb[:]))
+        nc.vector.tensor_copy(x_scale_picked[:], x_scale_table[:].indirect(offs_sb[:]))
+        nc.vector.tensor_copy(
+            rows[:, 0:H].rearrange("p (t m) -> p m t", t=PACK),
+            d_scale_picked[:].rearrange("p (m t) -> p m t", t=PACK),
+        )
+        nc.vector.tensor_copy(rows[:, H : H + S].bitcast(I32), x_scale_picked[:].bitcast(I32))
+        for r in range(4):
+            nc.scalar.dma_start(planes[r:P:32, :].bitcast(I32), rows[8 * r : P : 32, :].bitcast(I32))
+
+        d_picked = keep.tile([P, H], U32, name="d_picked", align_bytes=64)
+        keys = keep.tile([P, H], U32, name="keys", align_bytes=64)
+        nc.vector.tensor_copy(d_picked[:], d_table[:].indirect(kidx_sb[:]))
+        nc.vector.tensor_copy(
+            keys[:].rearrange("p (t c i) -> p c t i", t=PACK, i=4),
+            d_picked[:].rearrange("p (c i t) -> p c t i", t=PACK, i=4),
+        )
+
+        w_codes = keep.tile([P, N], U32, name="w_codes", align_bytes=64)
+        w_scales = keep.tile([P, N], U8, name="w_scales", align_bytes=64)
+        for h in range(2):
+            cols = slice(h * HALF, (h + 1) * HALF)
+            w_grouped = keep.tile([P, HALF * PACK], BF16, name="w_grouped%d" % h, align_bytes=64)
+            dst = w_grouped[:].rearrange("p (c i j) -> p c j i", i=4, j=PACK)
+            src = w_raw[:, :, cols].rearrange("p j (c i) -> p c j i", i=4)
+            if h == 0:
+                nc.vector.tensor_copy(dst, src)
+            else:
+                nc.scalar.copy(dst, src)
+            nc.vector.quantize_mx(out=w_codes[:, cols].bitcast(FP8X4), scales=w_scales[:, cols], in_=w_grouped[:])
+
+        queries = []
+        for h in range(2):
+            q = keep.tile([P, HALF], U32, name="queries%d" % h, align_bytes=64)
+            nc.vector.tensor_copy(q[:], x_table[:].indirect(offs_sb[:, h * 16 : (h + 1) * 16]))
+            queries.append(q)
+
+        chunks = S // CHUNK
+        sig = {}
+        zq = {}
+
+        def scores(c):
+            sig[c] = keep.tile([P, PACK, CHUNK], F32, name="sig%d" % c, align_bytes=64)
+            h, o = divmod(c * CHUNK, HALF)
+            for pair in range(2):
+                bank = psum.tile([P, 2, CHUNK], F32, name="score", tag="score", bufs=4)
+                for u in range(2):
+                    t = 2 * pair + u
+                    nc.tensor.matmul_mx(
+                        out=bank[:, u, :],
+                        lhsT=keys[:, t * P : (t + 1) * P].bitcast(FP8X4),
+                        lhsT_scale=planes[:, t * P : (t + 1) * P],
+                        rhs=queries[h][:, o : o + CHUNK].bitcast(FP8X4),
+                        rhs_scale=planes[:, H + c * CHUNK : H + (c + 1) * CHUNK],
+                        start=True,
+                        stop=True,
+                    )
+                for u in range(2):
+                    t = 2 * pair + u
+                    nc.scalar.activation(sig[c][:, t, :], bank[:, u, :], SIGMOID, bias=kb_sb[:, t : t + 1], scale=0.0625)
+
+        def weigh(c):
+            z = keep.tile([P, CHUNK * PACK], BF16, name="z%d" % c, align_bytes=64)
+            nc.vector.tensor_tensor(
+                z[:].rearrange("p (c i t) -> p c t i", i=4, t=PACK),
+                sig[c][:].rearrange("p t (c i) -> p c t i", i=4),
+                gn_sb[:].unsqueeze(1).unsqueeze(3).broadcast_to([P, CHUNK // 4, PACK, 4]),
+                MULT,
+            )
+            zq[c] = z
+
+        def finish(c):
+            z_codes = keep.tile([P, CHUNK], U32, name="z_codes%d" % c, align_bytes=64)
+            z_scales = keep.tile([P, CHUNK], U8, name="z_scales%d" % c, align_bytes=64)
+            nc.vector.quantize_mx(out=z_codes[:].bitcast(FP8X4), scales=z_scales[:], in_=zq[c][:])
+            for pair in range(2):
+                bank = psum.tile([P, 2, CHUNK], F32, name="acc", tag="acc", bufs=4)
+                for u in range(2):
+                    a = 2 * pair + u
+                    nc.tensor.matmul_mx(
+                        out=bank[:, u, :],
+                        lhsT=w_codes[:, a * P : (a + 1) * P].bitcast(FP8X4),
+                        lhsT_scale=w_scales[:, a * P : (a + 1) * P],
+                        rhs=z_codes[:].bitcast(FP8X4),
+                        rhs_scale=z_scales[:],
+                        start=True,
+                        stop=True,
+                    )
+                res = keep.tile([P, 2, CHUNK], F32, name="res%d_%d" % (c, pair), align_bytes=64)
+                if c == chunks - 1 and pair == 1:
+                    nc.vector.tensor_copy(res[:], bank[:])
+                else:
+                    nc.scalar.copy(res[:], bank[:])
+                nc.sync.dma_start(
+                    out.rearrange("(a p) j -> p a j", p=P)[:, 2 * pair : 2 * pair + 2, c * CHUNK : (c + 1) * CHUNK],
+                    res[:],
+                )
+
+        for c in range(chunks):
+            scores(c)
+        weigh(0)
+        for c in range(1, chunks):
+            weigh(c)
+            finish(c - 1)
+        finish(chunks - 1)

@@ -33,43 +33,47 @@ def tile_picked_sigattn_sigmoid_p_kernel(
         offs_sb = keep.tile([P, S // 16], U16, name="offs_sb")
         d_table = keep.tile([P, G], U32, name="d_table", align_bytes=64)
         x_table = keep.tile([P, T], U32, name="x_table", align_bytes=64)
-        w_raw = keep.tile([P, PACK, N], F32, name="w_raw", align_bytes=64)
+        w_raw = [keep.tile([P, PACK, HALF], F32, name="w_raw%d" % h, align_bytes=64) for h in range(2)]
         d_scale_table = keep.tile([P, G], U8, name="d_scale_table", align_bytes=64)
         x_scale_table = keep.tile([P, T], U8, name="x_scale_table", align_bytes=64)
-        planes = keep.tile([P, H + S], U8, name="planes", align_bytes=64)
+        key_scales = keep.tile([P, H], U8, name="key_scales", align_bytes=64)
         warm_in = keep.tile([P, 8], F32, name="warm_in")
         warm_out = keep.tile([P, 8], F32, name="warm_out")
         kb_sb = keep.tile([P, PACK], F32, name="kb_sb")
         gn_sb = keep.tile([P, PACK], F32, name="gn_sb")
 
-        nc.gpsimd.memset(d_scale_table[:].bitcast(I32), 0)
+        nc.vector.memset(d_scale_table[:].bitcast(I32), 0)
         nc.vector.memset(x_scale_table[:].bitcast(I32), 0)
         nc.vector.memset(warm_in[:], 0.0)
-        nc.vector.memset(planes[:].bitcast(I32), 0)
+        nc.vector.memset(key_scales[:].bitcast(I32), 0)
 
+        w_rows = w1.rearrange("(p j) m -> p j m", j=PACK)
         nc.sync.dma_start(kidx_sb[:], kidx)
+        nc.scalar.dma_start(d_scale_table[0:P:8, :].bitcast(I32), d_scales[0].bitcast(I32))
         nc.sync.dma_start(offs_sb[:], offs)
-        nc.sync.dma_start(d_scale_table[0:P:8, :].bitcast(I32), d_scales[0].bitcast(I32))
-        nc.sync.dma_start(x_scale_table[0:P:8, :].bitcast(I32), x_scales[0].bitcast(I32))
         nc.sync.dma_start(d_table[:].bitcast(I32), d_words[0].rearrange("p c r -> p (c r)").bitcast(I32))
-        nc.sync.dma_start(w_raw[:], w1.rearrange("(p j) m -> p j m", j=PACK))
+        for q in range(4):
+            nc.scalar.dma_start(
+                x_scale_table[32 * q : 32 * q + 4, :].bitcast(I32), x_scales[0, 4 * q : 4 * q + 4, :].bitcast(I32)
+            )
+        nc.sync.dma_start(w_raw[0][:], w_rows[:, :, 0:HALF])
         nc.sync.dma_start(x_table[:].bitcast(I32), x_words[0].rearrange("p c r -> p (c r)").bitcast(I32))
-        nc.scalar.dma_start(kb_sb[:], kb.rearrange("(p t) o -> p (t o)", t=PACK))
-        nc.scalar.dma_start(gn_sb[:], gn.rearrange("(p t) o -> p (t o)", t=PACK))
+        nc.sync.dma_start(w_raw[1][:], w_rows[:, :, HALF:N])
         nc.scalar.activation(warm_out[:], warm_in[:], SIGMOID)
+        nc.gpsimd.dma_start(kb_sb[:], kb.rearrange("(p t) o -> p (t o)", t=PACK))
+        nc.gpsimd.dma_start(gn_sb[:], gn.rearrange("(p t) o -> p (t o)", t=PACK))
 
         d_scale_picked = keep.tile([P, H], U8, name="d_scale_picked", align_bytes=64)
-        x_scale_picked = keep.tile([P, S], U8, name="x_scale_picked", align_bytes=64)
-        rows = keep.tile([P, H + S], U8, name="rows", align_bytes=64)
+        query_scales = keep.tile([P, S], U8, name="query_scales", align_bytes=64)
+        rows = keep.tile([P, H], U8, name="rows", align_bytes=64)
         nc.vector.tensor_copy(d_scale_picked[:], d_scale_table[:].indirect(kidx_sb[:]))
-        nc.vector.tensor_copy(x_scale_picked[:], x_scale_table[:].indirect(offs_sb[:]))
         nc.vector.tensor_copy(
-            rows[:, 0:H].rearrange("p (t m) -> p m t", t=PACK),
+            rows[:].rearrange("p (t m) -> p m t", t=PACK),
             d_scale_picked[:].rearrange("p (m t) -> p m t", t=PACK),
         )
-        nc.vector.tensor_copy(rows[:, H : H + S].bitcast(I32), x_scale_picked[:].bitcast(I32))
         for r in range(4):
-            nc.scalar.dma_start(planes[r:P:32, :].bitcast(I32), rows[8 * r : P : 32, :].bitcast(I32))
+            nc.scalar.dma_start(key_scales[r:P:32, :].bitcast(I32), rows[8 * r : P : 32, :].bitcast(I32))
+        nc.vector.tensor_copy(query_scales[:], x_scale_table[:].indirect(offs_sb[:]))
 
         d_picked = keep.tile([P, H], U32, name="d_picked", align_bytes=64)
         keys = keep.tile([P, H], U32, name="keys", align_bytes=64)
@@ -79,24 +83,25 @@ def tile_picked_sigattn_sigmoid_p_kernel(
             d_picked[:].rearrange("p (c i t) -> p c t i", t=PACK, i=4),
         )
 
-        w_codes = keep.tile([P, N], U32, name="w_codes", align_bytes=64)
-        w_scales = keep.tile([P, N], U8, name="w_scales", align_bytes=64)
-        for h in range(2):
-            cols = slice(h * HALF, (h + 1) * HALF)
+        w_codes = [keep.tile([P, HALF], U32, name="w_codes%d" % h, align_bytes=64) for h in range(2)]
+        w_scales = [keep.tile([P, HALF], U8, name="w_scales%d" % h, align_bytes=64) for h in range(2)]
+
+        def weights(h, copy):
             w_grouped = keep.tile([P, HALF * PACK], BF16, name="w_grouped%d" % h, align_bytes=64)
-            dst = w_grouped[:].rearrange("p (c i j) -> p c j i", i=4, j=PACK)
-            src = w_raw[:, :, cols].rearrange("p j (c i) -> p c j i", i=4)
-            if h == 0:
-                nc.vector.tensor_copy(dst, src)
-            else:
-                nc.scalar.copy(dst, src)
-            nc.vector.quantize_mx(out=w_codes[:, cols].bitcast(FP8X4), scales=w_scales[:, cols], in_=w_grouped[:])
+            copy(
+                w_grouped[:].rearrange("p (c i j) -> p c j i", i=4, j=PACK),
+                w_raw[h][:].rearrange("p j (c i) -> p c j i", i=4),
+            )
+            nc.vector.quantize_mx(out=w_codes[h][:].bitcast(FP8X4), scales=w_scales[h][:], in_=w_grouped[:])
+
+        weights(0, nc.scalar.copy)
 
         queries = []
         for h in range(2):
             q = keep.tile([P, HALF], U32, name="queries%d" % h, align_bytes=64)
             nc.vector.tensor_copy(q[:], x_table[:].indirect(offs_sb[:, h * 16 : (h + 1) * 16]))
             queries.append(q)
+        weights(1, nc.vector.tensor_copy)
 
         chunks = S // CHUNK
         sig = {}
@@ -112,9 +117,9 @@ def tile_picked_sigattn_sigmoid_p_kernel(
                     nc.tensor.matmul_mx(
                         out=bank[:, u, :],
                         lhsT=keys[:, t * P : (t + 1) * P].bitcast(FP8X4),
-                        lhsT_scale=planes[:, t * P : (t + 1) * P],
+                        lhsT_scale=key_scales[:, t * P : (t + 1) * P],
                         rhs=queries[h][:, o : o + CHUNK].bitcast(FP8X4),
-                        rhs_scale=planes[:, H + c * CHUNK : H + (c + 1) * CHUNK],
+                        rhs_scale=query_scales[:, c * CHUNK : (c + 1) * CHUNK],
                         start=True,
                         stop=True,
                     )
@@ -136,26 +141,27 @@ def tile_picked_sigattn_sigmoid_p_kernel(
             z_codes = keep.tile([P, CHUNK], U32, name="z_codes%d" % c, align_bytes=64)
             z_scales = keep.tile([P, CHUNK], U8, name="z_scales%d" % c, align_bytes=64)
             nc.vector.quantize_mx(out=z_codes[:].bitcast(FP8X4), scales=z_scales[:], in_=zq[c][:])
-            for pair in range(2):
-                bank = psum.tile([P, 2, CHUNK], F32, name="acc", tag="acc", bufs=4)
-                for u in range(2):
-                    a = 2 * pair + u
+            groups = [(0, 2), (2, 4)]
+            for lo, hi in groups:
+                bank = psum.tile([P, hi - lo, CHUNK], F32, name="acc", tag="acc", bufs=4)
+                for a in range(lo, hi):
+                    h, o = divmod(a * P, HALF)
                     nc.tensor.matmul_mx(
-                        out=bank[:, u, :],
-                        lhsT=w_codes[:, a * P : (a + 1) * P].bitcast(FP8X4),
-                        lhsT_scale=w_scales[:, a * P : (a + 1) * P],
+                        out=bank[:, a - lo, :],
+                        lhsT=w_codes[h][:, o : o + P].bitcast(FP8X4),
+                        lhsT_scale=w_scales[h][:, o : o + P],
                         rhs=z_codes[:].bitcast(FP8X4),
                         rhs_scale=z_scales[:],
                         start=True,
                         stop=True,
                     )
-                res = keep.tile([P, 2, CHUNK], F32, name="res%d_%d" % (c, pair), align_bytes=64)
-                if c == chunks - 1 and pair == 1:
+                res = keep.tile([P, hi - lo, CHUNK], F32, name="res%d_%d" % (c, lo), align_bytes=64)
+                if lo > 0 and c >= chunks - 2:
                     nc.vector.tensor_copy(res[:], bank[:])
                 else:
                     nc.scalar.copy(res[:], bank[:])
                 nc.sync.dma_start(
-                    out.rearrange("(a p) j -> p a j", p=P)[:, 2 * pair : 2 * pair + 2, c * CHUNK : (c + 1) * CHUNK],
+                    out.rearrange("(a p) j -> p a j", p=P)[:, lo:hi, c * CHUNK : (c + 1) * CHUNK],
                     res[:],
                 )
 

@@ -33,10 +33,10 @@ def tile_picked_sigattn_sigmoid_p_kernel(
         offs_sb = keep.tile([P, S // 16], U16, name="offs_sb")
         d_table = keep.tile([P, G], U32, name="d_table", align_bytes=64)
         x_table = keep.tile([P, T], U32, name="x_table", align_bytes=64)
-        w_raw = [keep.tile([P, PACK, HALF], F32, name="w_raw%d" % h, align_bytes=64) for h in range(2)]
+        w_raw = [keep.tile([P, PACK, HALF], F32, name="w_raw0", align_bytes=64)]
         d_scale_table = keep.tile([P, G], U8, name="d_scale_table", align_bytes=64)
         x_scale_table = keep.tile([P, T], U8, name="x_scale_table", align_bytes=64)
-        key_scales = keep.tile([P, H], U8, name="key_scales", align_bytes=64)
+        planes = keep.tile([P, H + S], U8, name="planes", align_bytes=64)
         warm_in = keep.tile([P, 8], F32, name="warm_in")
         warm_out = keep.tile([P, 8], F32, name="warm_out")
         kb_sb = keep.tile([P, PACK], F32, name="kb_sb")
@@ -45,35 +45,32 @@ def tile_picked_sigattn_sigmoid_p_kernel(
         nc.vector.memset(d_scale_table[:].bitcast(I32), 0)
         nc.vector.memset(x_scale_table[:].bitcast(I32), 0)
         nc.vector.memset(warm_in[:], 0.0)
-        nc.vector.memset(key_scales[:].bitcast(I32), 0)
 
         w_rows = w1.rearrange("(p j) m -> p j m", j=PACK)
         nc.sync.dma_start(kidx_sb[:], kidx)
-        nc.scalar.dma_start(d_scale_table[0:P:8, :].bitcast(I32), d_scales[0].bitcast(I32))
         nc.sync.dma_start(offs_sb[:], offs)
-        nc.sync.dma_start(d_table[:].bitcast(I32), d_words[0].rearrange("p c r -> p (c r)").bitcast(I32))
-        for q in range(4):
-            nc.scalar.dma_start(
-                x_scale_table[32 * q : 32 * q + 4, :].bitcast(I32), x_scales[0, 4 * q : 4 * q + 4, :].bitcast(I32)
-            )
+        nc.sync.dma_start(d_scale_table[0:P:8, :].bitcast(I32), d_scales[0].bitcast(I32))
         nc.sync.dma_start(w_raw[0][:], w_rows[:, :, 0:HALF])
+        nc.sync.dma_start(x_scale_table[0:P:8, :].bitcast(I32), x_scales[0].bitcast(I32))
+        nc.sync.dma_start(d_table[:].bitcast(I32), d_words[0].rearrange("p c r -> p (c r)").bitcast(I32))
         nc.sync.dma_start(x_table[:].bitcast(I32), x_words[0].rearrange("p c r -> p (c r)").bitcast(I32))
-        nc.sync.dma_start(w_raw[1][:], w_rows[:, :, HALF:N])
+        nc.sync.dma_start(kb_sb[:], kb.rearrange("(p t) o -> p (t o)", t=PACK))
+        nc.sync.dma_start(gn_sb[:], gn.rearrange("(p t) o -> p (t o)", t=PACK))
         nc.scalar.activation(warm_out[:], warm_in[:], SIGMOID)
-        nc.gpsimd.dma_start(kb_sb[:], kb.rearrange("(p t) o -> p (t o)", t=PACK))
-        nc.gpsimd.dma_start(gn_sb[:], gn.rearrange("(p t) o -> p (t o)", t=PACK))
 
         d_scale_picked = keep.tile([P, H], U8, name="d_scale_picked", align_bytes=64)
-        query_scales = keep.tile([P, S], U8, name="query_scales", align_bytes=64)
-        rows = keep.tile([P, H], U8, name="rows", align_bytes=64)
+        x_scale_picked = keep.tile([P, S], U8, name="x_scale_picked", tag="late", align_bytes=64)
         nc.vector.tensor_copy(d_scale_picked[:], d_scale_table[:].indirect(kidx_sb[:]))
+        nc.vector.tensor_copy(x_scale_picked[:], x_scale_table[:].indirect(offs_sb[:]))
         nc.vector.tensor_copy(
-            rows[:].rearrange("p (t m) -> p m t", t=PACK),
+            planes[:, 0:H].rearrange("p (t m) -> p m t", t=PACK),
             d_scale_picked[:].rearrange("p (m t) -> p m t", t=PACK),
         )
-        for r in range(4):
-            nc.scalar.dma_start(key_scales[r:P:32, :].bitcast(I32), rows[8 * r : P : 32, :].bitcast(I32))
-        nc.vector.tensor_copy(query_scales[:], x_scale_table[:].indirect(offs_sb[:]))
+        nc.vector.tensor_copy(planes[:, H : H + S].bitcast(I32), x_scale_picked[:].bitcast(I32))
+        for r in range(1, 4):
+            nc.sync.dma_start(planes[r:P:32, :].bitcast(I32), planes[8 * r : P : 32, :].bitcast(I32))
+        w_raw.append(keep.tile([P, PACK, HALF], F32, name="w_raw1", tag="late", align_bytes=64))
+        nc.sync.dma_start(w_raw[1][:], w_rows[:, :, HALF:N])
 
         d_picked = keep.tile([P, H], U32, name="d_picked", align_bytes=64)
         keys = keep.tile([P, H], U32, name="keys", align_bytes=64)
@@ -106,6 +103,7 @@ def tile_picked_sigattn_sigmoid_p_kernel(
         chunks = S // CHUNK
         sig = {}
         zq = {}
+        z_all = keep.tile([P, S * PACK], BF16, name="z_all", tag="late", align_bytes=64)
 
         def scores(c):
             sig[c] = keep.tile([P, PACK, CHUNK], F32, name="sig%d" % c, align_bytes=64)
@@ -117,9 +115,9 @@ def tile_picked_sigattn_sigmoid_p_kernel(
                     nc.tensor.matmul_mx(
                         out=bank[:, u, :],
                         lhsT=keys[:, t * P : (t + 1) * P].bitcast(FP8X4),
-                        lhsT_scale=key_scales[:, t * P : (t + 1) * P],
+                        lhsT_scale=planes[:, t * P : (t + 1) * P],
                         rhs=queries[h][:, o : o + CHUNK].bitcast(FP8X4),
-                        rhs_scale=query_scales[:, c * CHUNK : (c + 1) * CHUNK],
+                        rhs_scale=planes[:, H + c * CHUNK : H + (c + 1) * CHUNK],
                         start=True,
                         stop=True,
                     )
@@ -128,9 +126,9 @@ def tile_picked_sigattn_sigmoid_p_kernel(
                     nc.scalar.activation(sig[c][:, t, :], bank[:, u, :], SIGMOID, bias=kb_sb[:, t : t + 1], scale=0.0625)
 
         def weigh(c):
-            z = keep.tile([P, CHUNK * PACK], BF16, name="z%d" % c, align_bytes=64)
+            z = z_all[:, c * CHUNK * PACK : (c + 1) * CHUNK * PACK]
             nc.vector.tensor_tensor(
-                z[:].rearrange("p (c i t) -> p c t i", i=4, t=PACK),
+                z.rearrange("p (c i t) -> p c t i", i=4, t=PACK),
                 sig[c][:].rearrange("p t (c i) -> p c t i", i=4),
                 gn_sb[:].unsqueeze(1).unsqueeze(3).broadcast_to([P, CHUNK // 4, PACK, 4]),
                 MULT,
@@ -140,7 +138,7 @@ def tile_picked_sigattn_sigmoid_p_kernel(
         def finish(c):
             z_codes = keep.tile([P, CHUNK], U32, name="z_codes%d" % c, align_bytes=64)
             z_scales = keep.tile([P, CHUNK], U8, name="z_scales%d" % c, align_bytes=64)
-            nc.vector.quantize_mx(out=z_codes[:].bitcast(FP8X4), scales=z_scales[:], in_=zq[c][:])
+            nc.vector.quantize_mx(out=z_codes[:].bitcast(FP8X4), scales=z_scales[:], in_=zq[c])
             groups = [(0, 2), (2, 4)]
             for lo, hi in groups:
                 bank = psum.tile([P, hi - lo, CHUNK], F32, name="acc", tag="acc", bufs=4)

@@ -19,6 +19,7 @@ P = 128
 PACK = 4
 CHUNK = 128
 HALF = 256
+LEAD = 384
 
 
 def tile_picked_sigattn_sigmoid_p_kernel(
@@ -31,12 +32,10 @@ def tile_picked_sigattn_sigmoid_p_kernel(
 
         kidx_sb = keep.tile([P, H // 16], U16, name="kidx_sb")
         offs_sb = keep.tile([P, S // 16], U16, name="offs_sb")
-        d_table = keep.tile([P, G], U32, name="d_table", align_bytes=64)
+        d_table = keep.tile([P, G], U32, name="d_table", tag="after_keys", align_bytes=64)
         x_table = keep.tile([P, T], U32, name="x_table", align_bytes=64)
-        w_raw = [keep.tile([P, PACK, HALF], F32, name="w_raw0", align_bytes=64)]
         d_scale_table = keep.tile([P, G], U8, name="d_scale_table", align_bytes=64)
-        x_scale_table = keep.tile([P, T], U8, name="x_scale_table", align_bytes=64)
-        planes = keep.tile([P, H + S], U8, name="planes", align_bytes=64)
+        x_scale_table = keep.tile([P, T], U8, name="x_scale_table", tag="after_scales", align_bytes=64)
         warm_in = keep.tile([P, 8], F32, name="warm_in")
         warm_out = keep.tile([P, 8], F32, name="warm_out")
         kb_sb = keep.tile([P, PACK], F32, name="kb_sb")
@@ -47,21 +46,46 @@ def tile_picked_sigattn_sigmoid_p_kernel(
         nc.vector.memset(warm_in[:], 0.0)
 
         w_rows = w1.rearrange("(p j) m -> p j m", j=PACK)
+        pieces = [(0, 256), (256, 512)]
+        w_raw, w_codes, w_scales, w_grouped = {}, {}, {}, {}
+
+        def load_w(n, tag):
+            lo, hi = pieces[n]
+            w_raw[n] = keep.tile([P, PACK, hi - lo], F32, name="w_raw%d" % n, tag=tag, align_bytes=64)
+            nc.sync.dma_start(w_raw[n][:], w_rows[:, :, lo:hi])
+
+        def cast_w(n, copy):
+            lo, hi = pieces[n]
+            w_grouped[n] = keep.tile([P, (hi - lo) * PACK], BF16, name="w_grouped%d" % n, align_bytes=64)
+            copy(
+                w_grouped[n][:].rearrange("p (c i j) -> p c j i", i=4, j=PACK),
+                w_raw[n][:].rearrange("p j (c i) -> p c j i", i=4),
+            )
+
+        def quantise_w(n, tag):
+            lo, hi = pieces[n]
+            w_codes[n] = keep.tile([P, hi - lo], U32, name="w_codes%d" % n, tag=tag, align_bytes=64)
+            w_scales[n] = keep.tile([P, hi - lo], U8, name="w_scales%d" % n, align_bytes=64)
+            nc.vector.quantize_mx(out=w_codes[n][:].bitcast(FP8X4), scales=w_scales[n][:], in_=w_grouped[n][:])
+
+        d_src = d_words[0].rearrange("p c r -> p (c r)").bitcast(I32)
         nc.sync.dma_start(kidx_sb[:], kidx)
-        nc.sync.dma_start(offs_sb[:], offs)
+        nc.sync.dma_start(d_table[:, 0:LEAD].bitcast(I32), d_src[:, 0:LEAD])
         nc.sync.dma_start(d_scale_table[0:P:8, :].bitcast(I32), d_scales[0].bitcast(I32))
-        nc.sync.dma_start(w_raw[0][:], w_rows[:, :, 0:HALF])
+        load_w(0, "w_raw0")
+        nc.sync.dma_start(offs_sb[:], offs)
         nc.sync.dma_start(x_scale_table[0:P:8, :].bitcast(I32), x_scales[0].bitcast(I32))
-        nc.sync.dma_start(d_table[:].bitcast(I32), d_words[0].rearrange("p c r -> p (c r)").bitcast(I32))
+        nc.sync.dma_start(d_table[:, LEAD:G].bitcast(I32), d_src[:, LEAD:G])
         nc.sync.dma_start(x_table[:].bitcast(I32), x_words[0].rearrange("p c r -> p (c r)").bitcast(I32))
         nc.sync.dma_start(kb_sb[:], kb.rearrange("(p t) o -> p (t o)", t=PACK))
         nc.sync.dma_start(gn_sb[:], gn.rearrange("(p t) o -> p (t o)", t=PACK))
         nc.scalar.activation(warm_out[:], warm_in[:], SIGMOID)
 
         d_scale_picked = keep.tile([P, H], U8, name="d_scale_picked", align_bytes=64)
-        x_scale_picked = keep.tile([P, S], U8, name="x_scale_picked", tag="late", align_bytes=64)
+        x_scale_picked = keep.tile([P, S], U8, name="x_scale_picked", tag="after_moves", align_bytes=64)
         nc.vector.tensor_copy(d_scale_picked[:], d_scale_table[:].indirect(kidx_sb[:]))
         nc.vector.tensor_copy(x_scale_picked[:], x_scale_table[:].indirect(offs_sb[:]))
+        planes = keep.tile([P, H + S], U8, name="planes", tag="after_scales", align_bytes=64)
         nc.vector.tensor_copy(
             planes[:, 0:H].rearrange("p (t m) -> p m t", t=PACK),
             d_scale_picked[:].rearrange("p (m t) -> p m t", t=PACK),
@@ -69,104 +93,102 @@ def tile_picked_sigattn_sigmoid_p_kernel(
         nc.vector.tensor_copy(planes[:, H : H + S].bitcast(I32), x_scale_picked[:].bitcast(I32))
         for r in range(1, 4):
             nc.sync.dma_start(planes[r:P:32, :].bitcast(I32), planes[8 * r : P : 32, :].bitcast(I32))
-        w_raw.append(keep.tile([P, PACK, HALF], F32, name="w_raw1", tag="late", align_bytes=64))
-        nc.sync.dma_start(w_raw[1][:], w_rows[:, :, HALF:N])
+        load_w(1, "after_moves")
 
         d_picked = keep.tile([P, H], U32, name="d_picked", align_bytes=64)
         keys = keep.tile([P, H], U32, name="keys", align_bytes=64)
         nc.vector.tensor_copy(d_picked[:], d_table[:].indirect(kidx_sb[:]))
+        cast_w(0, nc.scalar.copy)
+        quantise_w(0, "after_keys")
         nc.vector.tensor_copy(
             keys[:].rearrange("p (t c i) -> p c t i", t=PACK, i=4),
             d_picked[:].rearrange("p (c i t) -> p c t i", t=PACK, i=4),
         )
-
-        w_codes = [keep.tile([P, HALF], U32, name="w_codes%d" % h, align_bytes=64) for h in range(2)]
-        w_scales = [keep.tile([P, HALF], U8, name="w_scales%d" % h, align_bytes=64) for h in range(2)]
-
-        def weights(h, copy):
-            w_grouped = keep.tile([P, HALF * PACK], BF16, name="w_grouped%d" % h, align_bytes=64)
-            copy(
-                w_grouped[:].rearrange("p (c i j) -> p c j i", i=4, j=PACK),
-                w_raw[h][:].rearrange("p j (c i) -> p c j i", i=4),
-            )
-            nc.vector.quantize_mx(out=w_codes[h][:].bitcast(FP8X4), scales=w_scales[h][:], in_=w_grouped[:])
-
-        weights(0, nc.scalar.copy)
 
         queries = []
         for h in range(2):
             q = keep.tile([P, HALF], U32, name="queries%d" % h, align_bytes=64)
             nc.vector.tensor_copy(q[:], x_table[:].indirect(offs_sb[:, h * 16 : (h + 1) * 16]))
             queries.append(q)
-        weights(1, nc.vector.tensor_copy)
+        cast_w(1, nc.vector.tensor_copy)
+        z_all = keep.tile([P, S * PACK], BF16, name="z_all", tag="after_moves", align_bytes=64)
 
         chunks = S // CHUNK
         sig = {}
         zq = {}
-        z_all = keep.tile([P, S * PACK], BF16, name="z_all", tag="late", align_bytes=64)
+        codes = {}
 
-        def scores(c):
-            sig[c] = keep.tile([P, PACK, CHUNK], F32, name="sig%d" % c, align_bytes=64)
-            h, o = divmod(c * CHUNK, HALF)
-            for pair in range(2):
-                bank = psum.tile([P, 2, CHUNK], F32, name="score", tag="score", bufs=4)
-                for u in range(2):
-                    t = 2 * pair + u
+        def scores(lo, width, per_bank):
+            tile = keep.tile([P, PACK, width], F32, name="sig%d" % lo, align_bytes=64)
+            for c in range(lo // CHUNK, (lo + width) // CHUNK):
+                sig[c] = tile[:, :, c * CHUNK - lo : (c + 1) * CHUNK - lo]
+            h, o = divmod(lo, HALF)
+            for first in range(0, PACK, per_bank):
+                bank = psum.tile([P, per_bank, width], F32, name="score", tag="bank", bufs=8)
+                for u in range(per_bank):
+                    t = first + u
                     nc.tensor.matmul_mx(
                         out=bank[:, u, :],
                         lhsT=keys[:, t * P : (t + 1) * P].bitcast(FP8X4),
                         lhsT_scale=planes[:, t * P : (t + 1) * P],
-                        rhs=queries[h][:, o : o + CHUNK].bitcast(FP8X4),
-                        rhs_scale=planes[:, H + c * CHUNK : H + (c + 1) * CHUNK],
+                        rhs=queries[h][:, o : o + width].bitcast(FP8X4),
+                        rhs_scale=planes[:, H + lo : H + lo + width],
                         start=True,
                         stop=True,
                     )
-                for u in range(2):
-                    t = 2 * pair + u
-                    nc.scalar.activation(sig[c][:, t, :], bank[:, u, :], SIGMOID, bias=kb_sb[:, t : t + 1], scale=0.0625)
+                for u in range(per_bank):
+                    t = first + u
+                    nc.scalar.activation(tile[:, t, :], bank[:, u, :], SIGMOID, bias=kb_sb[:, t : t + 1], scale=0.0625)
 
         def weigh(c):
             z = z_all[:, c * CHUNK * PACK : (c + 1) * CHUNK * PACK]
             nc.vector.tensor_tensor(
                 z.rearrange("p (c i t) -> p c t i", i=4, t=PACK),
-                sig[c][:].rearrange("p t (c i) -> p c t i", i=4),
+                sig[c].rearrange("p t (c i) -> p c t i", i=4),
                 gn_sb[:].unsqueeze(1).unsqueeze(3).broadcast_to([P, CHUNK // 4, PACK, 4]),
                 MULT,
             )
             zq[c] = z
 
-        def finish(c):
+        def quantise_z(c):
             z_codes = keep.tile([P, CHUNK], U32, name="z_codes%d" % c, align_bytes=64)
             z_scales = keep.tile([P, CHUNK], U8, name="z_scales%d" % c, align_bytes=64)
             nc.vector.quantize_mx(out=z_codes[:].bitcast(FP8X4), scales=z_scales[:], in_=zq[c])
-            groups = [(0, 2), (2, 4)]
-            for lo, hi in groups:
-                bank = psum.tile([P, hi - lo, CHUNK], F32, name="acc", tag="acc", bufs=4)
-                for a in range(lo, hi):
-                    h, o = divmod(a * P, HALF)
-                    nc.tensor.matmul_mx(
-                        out=bank[:, a - lo, :],
-                        lhsT=w_codes[h][:, o : o + P].bitcast(FP8X4),
-                        lhsT_scale=w_scales[h][:, o : o + P],
-                        rhs=z_codes[:].bitcast(FP8X4),
-                        rhs_scale=z_scales[:],
-                        start=True,
-                        stop=True,
-                    )
-                res = keep.tile([P, hi - lo, CHUNK], F32, name="res%d_%d" % (c, lo), align_bytes=64)
-                if lo > 0 and c >= chunks - 2:
-                    nc.vector.tensor_copy(res[:], bank[:])
-                else:
-                    nc.scalar.copy(res[:], bank[:])
-                nc.sync.dma_start(
-                    out.rearrange("(a p) j -> p a j", p=P)[:, lo:hi, c * CHUNK : (c + 1) * CHUNK],
-                    res[:],
-                )
+            codes[c] = (z_codes, z_scales)
 
-        for c in range(chunks):
-            scores(c)
+        def finish(c, h, copy):
+            z_codes, z_scales = codes[c]
+            bank = psum.tile([P, 2, CHUNK], F32, name="acc", tag="bank", bufs=8)
+            for u in range(2):
+                n, o = h, u * P
+                nc.tensor.matmul_mx(
+                    out=bank[:, u, :],
+                    lhsT=w_codes[n][:, o : o + P].bitcast(FP8X4),
+                    lhsT_scale=w_scales[n][:, o : o + P],
+                    rhs=z_codes[:].bitcast(FP8X4),
+                    rhs_scale=z_scales[:],
+                    start=True,
+                    stop=True,
+                )
+            res = keep.tile([P, 2, CHUNK], F32, name="res%d_%d" % (c, h), align_bytes=64)
+            copy(res[:], bank[:])
+            nc.sync.dma_start(
+                out.rearrange("(a p) j -> p a j", p=P)[:, 2 * h : 2 * h + 2, c * CHUNK : (c + 1) * CHUNK],
+                res[:],
+            )
+
+        scores(0, CHUNK, 1)
+        for c in range(1, chunks):
+            scores(c * CHUNK, CHUNK, 2)
         weigh(0)
+        quantise_w(1, "w_codes1")
         for c in range(1, chunks):
             weigh(c)
-            finish(c - 1)
-        finish(chunks - 1)
+            quantise_z(c - 1)
+            if c < chunks - 1:
+                finish(c - 1, 0, nc.scalar.copy)
+                finish(c - 1, 1, nc.scalar.copy)
+        quantise_z(chunks - 1)
+        for c in (2, 3):
+            finish(c, 0, nc.scalar.copy)
+            finish(c, 1, nc.vector.tensor_copy)

@@ -115,8 +115,6 @@ def tile_picked_sigattn_sigmoid_p_kernel(
 
         chunks = S // CHUNK
         sig = {}
-        zq = {}
-        codes = {}
 
         def scores(lo, width, per_bank):
             tile = keep.tile([P, PACK, width], F32, name="sig%d" % lo, align_bytes=64)
@@ -148,47 +146,47 @@ def tile_picked_sigattn_sigmoid_p_kernel(
                 gn_sb[:].unsqueeze(1).unsqueeze(3).broadcast_to([P, CHUNK // 4, PACK, 4]),
                 MULT,
             )
-            zq[c] = z
 
-        def quantise_z(c):
-            z_codes = keep.tile([P, CHUNK], U32, name="z_codes%d" % c, align_bytes=64)
-            z_scales = keep.tile([P, CHUNK], U8, name="z_scales%d" % c, align_bytes=64)
-            nc.vector.quantize_mx(out=z_codes[:].bitcast(FP8X4), scales=z_scales[:], in_=zq[c])
-            codes[c] = (z_codes, z_scales)
+        z_codes = keep.tile([P, S], U32, name="z_codes", align_bytes=64)
+        z_scales = keep.tile([P, S], U8, name="z_scales", align_bytes=64)
 
-        def finish(c, h, copy):
-            z_codes, z_scales = codes[c]
-            bank = psum.tile([P, 2, CHUNK], F32, name="acc", tag="bank", bufs=8)
-            for u in range(2):
-                n, o = h, u * P
+        def quantise_z(lo, width):
+            nc.vector.quantize_mx(
+                out=z_codes[:, lo : lo + width].bitcast(FP8X4),
+                scales=z_scales[:, lo : lo + width],
+                in_=z_all[:, lo * PACK : (lo + width) * PACK],
+            )
+
+        def finish(lo, width, first, tiles, copy):
+            cols = slice(lo, lo + width)
+            bank = psum.tile([P, tiles, width], F32, name="acc", tag="bank", bufs=8)
+            for u in range(tiles):
+                n, o = divmod((first + u) * P, HALF)
                 nc.tensor.matmul_mx(
                     out=bank[:, u, :],
                     lhsT=w_codes[n][:, o : o + P].bitcast(FP8X4),
                     lhsT_scale=w_scales[n][:, o : o + P],
-                    rhs=z_codes[:].bitcast(FP8X4),
-                    rhs_scale=z_scales[:],
+                    rhs=z_codes[:, cols].bitcast(FP8X4),
+                    rhs_scale=z_scales[:, cols],
                     start=True,
                     stop=True,
                 )
-            res = keep.tile([P, 2, CHUNK], F32, name="res%d_%d" % (c, h), align_bytes=64)
+            res = keep.tile([P, tiles, width], F32, name="res%d_%d" % (lo, first), align_bytes=64)
             copy(res[:], bank[:])
-            nc.sync.dma_start(
-                out.rearrange("(a p) j -> p a j", p=P)[:, 2 * h : 2 * h + 2, c * CHUNK : (c + 1) * CHUNK],
-                res[:],
-            )
+            nc.sync.dma_start(out.rearrange("(a p) j -> p a j", p=P)[:, first : first + tiles, cols], res[:])
 
         scores(0, CHUNK, 1)
         for c in range(1, chunks):
             scores(c * CHUNK, CHUNK, 2)
         weigh(0)
+        weigh(1)
         quantise_w(1, "w_codes1")
-        for c in range(1, chunks):
-            weigh(c)
-            quantise_z(c - 1)
-            if c < chunks - 1:
-                finish(c - 1, 0, nc.scalar.copy)
-                finish(c - 1, 1, nc.scalar.copy)
-        quantise_z(chunks - 1)
-        for c in (2, 3):
-            finish(c, 0, nc.scalar.copy)
-            finish(c, 1, nc.vector.tensor_copy)
+        quantise_z(0, HALF)
+        for a in range(N // P):
+            finish(0, HALF, a, 1, nc.scalar.copy)
+        weigh(2)
+        weigh(3)
+        quantise_z(2 * CHUNK, CHUNK)
+        quantise_z(3 * CHUNK, CHUNK)
+        for a in range(N // P):
+            finish(HALF, HALF, a, 1, nc.scalar.copy if a % 2 else nc.vector.tensor_copy)

@@ -17,9 +17,12 @@ MULT = mybir.AluOpType.mult
 
 P = 128
 PACK = 4
+RUN = 4
 CHUNK = 128
 HALF = 256
-LEAD = 384
+LIST_HALF = HALF // 16
+LEAD = 448
+BANKS = 8
 
 
 def tile_picked_sigattn_sigmoid_p_kernel(
@@ -28,6 +31,7 @@ def tile_picked_sigattn_sigmoid_p_kernel(
     nc = tc.nc
     with ExitStack() as ctx:
         keep = ctx.enter_context(tc.tile_pool(name="keep", bufs=1))
+        late = ctx.enter_context(tc.tile_pool(name="late", bufs=1))
         psum = ctx.enter_context(tc.psum_pool(name="psum", bufs=1))
 
         kidx_sb = keep.tile([P, H // 16], U16, name="kidx_sb")
@@ -39,50 +43,41 @@ def tile_picked_sigattn_sigmoid_p_kernel(
         warm_in = keep.tile([P, 8], F32, name="warm_in")
         warm_out = keep.tile([P, 8], F32, name="warm_out")
         kb_sb = keep.tile([P, PACK], F32, name="kb_sb")
-        gn_sb = keep.tile([P, PACK], F32, name="gn_sb")
 
         nc.vector.memset(d_scale_table[:].bitcast(I32), 0)
         nc.vector.memset(x_scale_table[:].bitcast(I32), 0)
         nc.vector.memset(warm_in[:], 0.0)
 
         w_rows = w1.rearrange("(p j) m -> p j m", j=PACK)
-        pieces = [(0, 256), (256, 512)]
-        w_raw, w_codes, w_scales, w_grouped = {}, {}, {}, {}
+        w_codes, w_scales, w_grouped = {}, {}, {}
 
-        def load_w(n, tag):
-            lo, hi = pieces[n]
-            w_raw[n] = keep.tile([P, PACK, hi - lo], F32, name="w_raw%d" % n, tag=tag, align_bytes=64)
-            nc.sync.dma_start(w_raw[n][:], w_rows[:, :, lo:hi])
-
-        def cast_w(n, copy):
-            lo, hi = pieces[n]
-            w_grouped[n] = keep.tile([P, (hi - lo) * PACK], BF16, name="w_grouped%d" % n, align_bytes=64)
+        def cast_w(h, raw, copy):
+            w_grouped[h] = keep.tile([P, HALF * PACK], BF16, name="w_grouped%d" % h, align_bytes=64)
             copy(
-                w_grouped[n][:].rearrange("p (c i j) -> p c j i", i=4, j=PACK),
-                w_raw[n][:].rearrange("p j (c i) -> p c j i", i=4),
+                w_grouped[h][:].rearrange("p (c i j) -> p c j i", i=RUN, j=PACK),
+                raw[:].rearrange("p j (c i) -> p c j i", i=RUN),
             )
 
-        def quantise_w(n, tag):
-            lo, hi = pieces[n]
-            w_codes[n] = keep.tile([P, hi - lo], U32, name="w_codes%d" % n, tag=tag, align_bytes=64)
-            w_scales[n] = keep.tile([P, hi - lo], U8, name="w_scales%d" % n, align_bytes=64)
-            nc.vector.quantize_mx(out=w_codes[n][:].bitcast(FP8X4), scales=w_scales[n][:], in_=w_grouped[n][:])
+        def quantise_w(h, tag):
+            w_codes[h] = keep.tile([P, HALF], U32, name="w_codes%d" % h, tag=tag, align_bytes=64)
+            w_scales[h] = keep.tile([P, HALF], U8, name="w_scales%d" % h, align_bytes=64)
+            nc.vector.quantize_mx(out=w_codes[h][:].bitcast(FP8X4), scales=w_scales[h][:], in_=w_grouped[h][:])
 
         d_src = d_words[0].rearrange("p c r -> p (c r)").bitcast(I32)
-        nc.sync.dma_start(kidx_sb[:], kidx)
         nc.sync.dma_start(d_table[:, 0:LEAD].bitcast(I32), d_src[:, 0:LEAD])
+        nc.sync.dma_start(kidx_sb[:], kidx)
         nc.sync.dma_start(d_scale_table[0:P:8, :].bitcast(I32), d_scales[0].bitcast(I32))
-        load_w(0, "w_raw0")
+        w_raw0 = keep.tile([P, PACK, HALF], F32, name="w_raw0", align_bytes=64)
+        nc.sync.dma_start(w_raw0[:], w_rows[:, :, 0:HALF])
         nc.sync.dma_start(offs_sb[:], offs)
         nc.sync.dma_start(x_scale_table[0:P:8, :].bitcast(I32), x_scales[0].bitcast(I32))
         nc.sync.dma_start(d_table[:, LEAD:G].bitcast(I32), d_src[:, LEAD:G])
         nc.sync.dma_start(x_table[:].bitcast(I32), x_words[0].rearrange("p c r -> p (c r)").bitcast(I32))
         nc.sync.dma_start(kb_sb[:], kb.rearrange("(p t) o -> p (t o)", t=PACK))
-        nc.sync.dma_start(gn_sb[:], gn.rearrange("(p t) o -> p (t o)", t=PACK))
         nc.scalar.activation(warm_out[:], warm_in[:], SIGMOID)
 
         d_scale_picked = keep.tile([P, H], U8, name="d_scale_picked", align_bytes=64)
-        x_scale_picked = keep.tile([P, S], U8, name="x_scale_picked", tag="after_moves", align_bytes=64)
+        x_scale_picked = late.tile([P, S], U8, name="x_scale_picked", align_bytes=64, offset=0)
         nc.vector.tensor_copy(d_scale_picked[:], d_scale_table[:].indirect(kidx_sb[:]))
         nc.vector.tensor_copy(x_scale_picked[:], x_scale_table[:].indirect(offs_sb[:]))
         planes = keep.tile([P, H + S], U8, name="planes", tag="after_scales", align_bytes=64)
@@ -93,57 +88,65 @@ def tile_picked_sigattn_sigmoid_p_kernel(
         nc.vector.tensor_copy(planes[:, H : H + S].bitcast(I32), x_scale_picked[:].bitcast(I32))
         for r in range(1, 4):
             nc.sync.dma_start(planes[r:P:32, :].bitcast(I32), planes[8 * r : P : 32, :].bitcast(I32))
-        load_w(1, "after_moves")
 
-        d_picked = keep.tile([P, H], U32, name="d_picked", align_bytes=64)
+        w_raw1 = late.tile([P, PACK, HALF], F32, name="w_raw1", align_bytes=64, offset=64)
+        nc.sync.dma_start(w_raw1[:, 0 : PACK - 1, :], w_rows[:, 0 : PACK - 1, HALF:N])
+        nc.sync.dma_start(w_raw1[:, PACK - 1 : PACK, :], w_rows[:, PACK - 1 : PACK, HALF:N])
+        gn_sb = late.tile([P, PACK], F32, name="gn_sb", align_bytes=64, offset=0)
+        nc.sync.dma_start(gn_sb[:], gn.rearrange("(p t) o -> p (t o)", t=PACK))
+
         keys = keep.tile([P, H], U32, name="keys", align_bytes=64)
-        nc.vector.tensor_copy(d_picked[:], d_table[:].indirect(kidx_sb[:]))
-        cast_w(0, nc.scalar.copy)
+        d_picked = [keep.tile([P, HALF], U32, name="d_picked%d" % h, align_bytes=64) for h in range(2)]
+        for h in range(2):
+            nc.vector.tensor_copy(d_picked[h][:], d_table[:].indirect(kidx_sb[:, h * LIST_HALF : (h + 1) * LIST_HALF]))
+
+        def deal_keys(h):
+            nc.vector.tensor_copy(
+                keys[:].rearrange("p (t g c i) -> p g c t i", t=PACK, g=2, i=RUN)[:, h],
+                d_picked[h][:].rearrange("p (c i t) -> p c t i", t=PACK, i=RUN),
+            )
+
+        deal_keys(0)
+        cast_w(0, w_raw0, nc.scalar.copy)
         quantise_w(0, "after_keys")
-        nc.vector.tensor_copy(
-            keys[:].rearrange("p (t c i) -> p c t i", t=PACK, i=4),
-            d_picked[:].rearrange("p (c i t) -> p c t i", t=PACK, i=4),
-        )
+        deal_keys(1)
 
         queries = []
         for h in range(2):
             q = keep.tile([P, HALF], U32, name="queries%d" % h, align_bytes=64)
-            nc.vector.tensor_copy(q[:], x_table[:].indirect(offs_sb[:, h * 16 : (h + 1) * 16]))
+            nc.vector.tensor_copy(q[:], x_table[:].indirect(offs_sb[:, h * LIST_HALF : (h + 1) * LIST_HALF]))
             queries.append(q)
-        cast_w(1, nc.vector.tensor_copy)
-        z_all = keep.tile([P, S * PACK], BF16, name="z_all", tag="after_moves", align_bytes=64)
+        cast_w(1, w_raw1, nc.vector.tensor_copy)
 
-        chunks = S // CHUNK
+        z = keep.tile([P, S * PACK], BF16, name="z", align_bytes=64)
         sig = {}
 
-        def scores(lo, width, per_bank):
-            tile = keep.tile([P, PACK, width], F32, name="sig%d" % lo, align_bytes=64)
-            for c in range(lo // CHUNK, (lo + width) // CHUNK):
-                sig[c] = tile[:, :, c * CHUNK - lo : (c + 1) * CHUNK - lo]
+        def scores(c, per_bank):
+            sig[c] = keep.tile([P, PACK, CHUNK], F32, name="sig%d" % c, align_bytes=64)
+            lo = c * CHUNK
             h, o = divmod(lo, HALF)
             for first in range(0, PACK, per_bank):
-                bank = psum.tile([P, per_bank, width], F32, name="score", tag="bank", bufs=8)
+                bank = psum.tile([P, per_bank, CHUNK], F32, name="score", tag="bank", bufs=BANKS)
                 for u in range(per_bank):
                     t = first + u
                     nc.tensor.matmul_mx(
                         out=bank[:, u, :],
                         lhsT=keys[:, t * P : (t + 1) * P].bitcast(FP8X4),
                         lhsT_scale=planes[:, t * P : (t + 1) * P],
-                        rhs=queries[h][:, o : o + width].bitcast(FP8X4),
-                        rhs_scale=planes[:, H + lo : H + lo + width],
+                        rhs=queries[h][:, o : o + CHUNK].bitcast(FP8X4),
+                        rhs_scale=planes[:, H + lo : H + lo + CHUNK],
                         start=True,
                         stop=True,
                     )
                 for u in range(per_bank):
                     t = first + u
-                    nc.scalar.activation(tile[:, t, :], bank[:, u, :], SIGMOID, bias=kb_sb[:, t : t + 1], scale=0.0625)
+                    nc.scalar.activation(sig[c][:, t, :], bank[:, u, :], SIGMOID, bias=kb_sb[:, t : t + 1], scale=0.0625)
 
         def weigh(c):
-            z = z_all[:, c * CHUNK * PACK : (c + 1) * CHUNK * PACK]
             nc.vector.tensor_tensor(
-                z.rearrange("p (c i t) -> p c t i", i=4, t=PACK),
-                sig[c].rearrange("p t (c i) -> p c t i", i=4),
-                gn_sb[:].unsqueeze(1).unsqueeze(3).broadcast_to([P, CHUNK // 4, PACK, 4]),
+                z[:, c * CHUNK * PACK : (c + 1) * CHUNK * PACK].rearrange("p (c i t) -> p c t i", i=RUN, t=PACK),
+                sig[c][:].rearrange("p t (c i) -> p c t i", i=RUN),
+                gn_sb[:].unsqueeze(1).unsqueeze(3).broadcast_to([P, CHUNK // RUN, PACK, RUN]),
                 MULT,
             )
 
@@ -154,39 +157,40 @@ def tile_picked_sigattn_sigmoid_p_kernel(
             nc.vector.quantize_mx(
                 out=z_codes[:, lo : lo + width].bitcast(FP8X4),
                 scales=z_scales[:, lo : lo + width],
-                in_=z_all[:, lo * PACK : (lo + width) * PACK],
+                in_=z[:, lo * PACK : (lo + width) * PACK],
             )
 
-        def finish(lo, width, first, tiles, copy):
-            cols = slice(lo, lo + width)
-            bank = psum.tile([P, tiles, width], F32, name="acc", tag="bank", bufs=8)
-            for u in range(tiles):
-                n, o = divmod((first + u) * P, HALF)
-                nc.tensor.matmul_mx(
-                    out=bank[:, u, :],
-                    lhsT=w_codes[n][:, o : o + P].bitcast(FP8X4),
-                    lhsT_scale=w_scales[n][:, o : o + P],
-                    rhs=z_codes[:, cols].bitcast(FP8X4),
-                    rhs_scale=z_scales[:, cols],
-                    start=True,
-                    stop=True,
-                )
-            res = keep.tile([P, tiles, width], F32, name="res%d_%d" % (lo, first), align_bytes=64)
+        def finish(lo, a, copy):
+            cols = slice(lo, lo + HALF)
+            h, o = divmod(a * P, HALF)
+            bank = psum.tile([P, HALF], F32, name="acc", tag="bank", bufs=BANKS)
+            nc.tensor.matmul_mx(
+                out=bank[:],
+                lhsT=w_codes[h][:, o : o + P].bitcast(FP8X4),
+                lhsT_scale=w_scales[h][:, o : o + P],
+                rhs=z_codes[:, cols].bitcast(FP8X4),
+                rhs_scale=z_scales[:, cols],
+                start=True,
+                stop=True,
+            )
+            res = keep.tile([P, HALF], F32, name="res%d_%d" % (lo, a), align_bytes=64)
             copy(res[:], bank[:])
-            nc.sync.dma_start(out.rearrange("(a p) j -> p a j", p=P)[:, first : first + tiles, cols], res[:])
+            nc.sync.dma_start(out[a * P : (a + 1) * P, cols], res[:])
 
-        scores(0, CHUNK, 1)
-        for c in range(1, chunks):
-            scores(c * CHUNK, CHUNK, 2)
+        scores(0, 1)
+        for c in range(1, S // CHUNK):
+            scores(c, 2)
+
         weigh(0)
         weigh(1)
         quantise_w(1, "w_codes1")
         quantise_z(0, HALF)
         for a in range(N // P):
-            finish(0, HALF, a, 1, nc.scalar.copy)
+            finish(0, a, nc.scalar.copy)
+
         weigh(2)
         weigh(3)
         quantise_z(2 * CHUNK, CHUNK)
         quantise_z(3 * CHUNK, CHUNK)
         for a in range(N // P):
-            finish(HALF, HALF, a, 1, nc.scalar.copy if a % 2 else nc.vector.tensor_copy)
+            finish(HALF, a, nc.scalar.copy if a % 2 else nc.vector.tensor_copy)

@@ -42,7 +42,6 @@ def tile_picked_sigattn_sigmoid_p_kernel(
         x_scale_table = keep.tile([P, T], U8, name="x_scale_table", tag="after_scales", align_bytes=64)
         warm_in = keep.tile([P, 8], F32, name="warm_in")
         warm_out = keep.tile([P, 8], F32, name="warm_out")
-        kb_sb = keep.tile([P, PACK], F32, name="kb_sb")
 
         nc.vector.memset(d_scale_table[:].bitcast(I32), 0)
         nc.vector.memset(x_scale_table[:].bitcast(I32), 0)
@@ -67,13 +66,12 @@ def tile_picked_sigattn_sigmoid_p_kernel(
         nc.sync.dma_start(d_table[:, 0:LEAD].bitcast(I32), d_src[:, 0:LEAD])
         nc.sync.dma_start(kidx_sb[:], kidx)
         nc.sync.dma_start(d_scale_table[0:P:8, :].bitcast(I32), d_scales[0].bitcast(I32))
-        w_raw0 = keep.tile([P, PACK, HALF], F32, name="w_raw0", align_bytes=64)
-        nc.sync.dma_start(w_raw0[:], w_rows[:, :, 0:HALF])
         nc.sync.dma_start(offs_sb[:], offs)
         nc.sync.dma_start(x_scale_table[0:P:8, :].bitcast(I32), x_scales[0].bitcast(I32))
         nc.sync.dma_start(d_table[:, LEAD:G].bitcast(I32), d_src[:, LEAD:G])
         nc.sync.dma_start(x_table[:].bitcast(I32), x_words[0].rearrange("p c r -> p (c r)").bitcast(I32))
-        nc.sync.dma_start(kb_sb[:], kb.rearrange("(p t) o -> p (t o)", t=PACK))
+        w_raw0 = keep.tile([P, PACK, HALF], F32, name="w_raw0", tag="after_cast", align_bytes=64)
+        nc.sync.dma_start(w_raw0[:], w_rows[:, :, 0:HALF])
         nc.scalar.activation(warm_out[:], warm_in[:], SIGMOID)
 
         d_scale_picked = keep.tile([P, H], U8, name="d_scale_picked", align_bytes=64)
@@ -89,11 +87,12 @@ def tile_picked_sigattn_sigmoid_p_kernel(
         for r in range(1, 4):
             nc.sync.dma_start(planes[r:P:32, :].bitcast(I32), planes[8 * r : P : 32, :].bitcast(I32))
 
-        w_raw1 = late.tile([P, PACK, HALF], F32, name="w_raw1", align_bytes=64, offset=64)
-        nc.sync.dma_start(w_raw1[:, 0 : PACK - 1, :], w_rows[:, 0 : PACK - 1, HALF:N])
-        nc.sync.dma_start(w_raw1[:, PACK - 1 : PACK, :], w_rows[:, PACK - 1 : PACK, HALF:N])
-        gn_sb = late.tile([P, PACK], F32, name="gn_sb", align_bytes=64, offset=0)
+        kb_sb = late.tile([P, PACK], F32, name="kb_sb", align_bytes=32, offset=0)
+        nc.sync.dma_start(kb_sb[:], kb.rearrange("(p t) o -> p (t o)", t=PACK))
+        gn_sb = late.tile([P, PACK], F32, name="gn_sb", align_bytes=32, offset=32)
         nc.sync.dma_start(gn_sb[:], gn.rearrange("(p t) o -> p (t o)", t=PACK))
+        w_raw1 = late.tile([P, PACK, HALF], F32, name="w_raw1", align_bytes=64, offset=64)
+        nc.sync.dma_start(w_raw1[:], w_rows[:, :, HALF:N])
 
         keys = keep.tile([P, H], U32, name="keys", align_bytes=64)
         d_picked = [keep.tile([P, HALF], U32, name="d_picked%d" % h, align_bytes=64) for h in range(2)]
@@ -107,8 +106,6 @@ def tile_picked_sigattn_sigmoid_p_kernel(
             )
 
         deal_keys(0)
-        cast_w(0, w_raw0, nc.scalar.copy)
-        quantise_w(0, "after_keys")
         deal_keys(1)
 
         queries = []
@@ -116,9 +113,9 @@ def tile_picked_sigattn_sigmoid_p_kernel(
             q = keep.tile([P, HALF], U32, name="queries%d" % h, align_bytes=64)
             nc.vector.tensor_copy(q[:], x_table[:].indirect(offs_sb[:, h * LIST_HALF : (h + 1) * LIST_HALF]))
             queries.append(q)
-        cast_w(1, w_raw1, nc.vector.tensor_copy)
+        cast_w(0, w_raw0, nc.vector.tensor_copy)
 
-        z = keep.tile([P, S * PACK], BF16, name="z", align_bytes=64)
+        z = keep.tile([P, S * PACK], BF16, name="z", tag="after_cast", align_bytes=64)
         sig = {}
 
         def scores(c, per_bank):
@@ -183,12 +180,15 @@ def tile_picked_sigattn_sigmoid_p_kernel(
 
         weigh(0)
         weigh(1)
-        quantise_w(1, "w_codes1")
+        quantise_w(0, "w_codes0")
         quantise_z(0, HALF)
-        for a in range(N // P):
+        for a in range(2):
             finish(0, a, nc.scalar.copy)
-
+        cast_w(1, w_raw1, nc.vector.tensor_copy)
         weigh(2)
+        quantise_w(1, "w_codes1")
+        for a in range(2, 4):
+            finish(0, a, nc.scalar.copy)
         weigh(3)
         quantise_z(2 * CHUNK, CHUNK)
         quantise_z(3 * CHUNK, CHUNK)

@@ -22,6 +22,7 @@ CHUNK = 128
 HALF = 256
 LIST_HALF = HALF // 16
 LEAD = 448
+MID = 960
 BANKS = 8
 
 
@@ -36,7 +37,7 @@ def tile_picked_sigattn_sigmoid_p_kernel(
 
         kidx_sb = keep.tile([P, H // 16], U16, name="kidx_sb")
         offs_sb = keep.tile([P, S // 16], U16, name="offs_sb")
-        d_table = keep.tile([P, G], U32, name="d_table", tag="after_keys", align_bytes=64)
+        d_table = keep.tile([P, G], U32, name="d_table", align_bytes=64)
         x_table = keep.tile([P, T], U32, name="x_table", align_bytes=64)
         d_scale_table = keep.tile([P, G], U8, name="d_scale_table", align_bytes=64)
         x_scale_table = keep.tile([P, T], U8, name="x_scale_table", tag="after_scales", align_bytes=64)
@@ -50,12 +51,14 @@ def tile_picked_sigattn_sigmoid_p_kernel(
         w_rows = w1.rearrange("(p j) m -> p j m", j=PACK)
         w_codes, w_scales, w_grouped = {}, {}, {}
 
-        def cast_w(h, raw, copy):
+        def cast_w(h, raw, copies):
             w_grouped[h] = keep.tile([P, HALF * PACK], BF16, name="w_grouped%d" % h, align_bytes=64)
-            copy(
-                w_grouped[h][:].rearrange("p (c i j) -> p c j i", i=RUN, j=PACK),
-                raw[:].rearrange("p j (c i) -> p c j i", i=RUN),
-            )
+            width = HALF // len(copies)
+            for k, copy in enumerate(copies):
+                copy(
+                    w_grouped[h][:, k * width * PACK : (k + 1) * width * PACK].rearrange("p (c i j) -> p c j i", i=RUN, j=PACK),
+                    raw[:, :, k * width : (k + 1) * width].rearrange("p j (c i) -> p c j i", i=RUN),
+                )
 
         def quantise_w(h, tag):
             w_codes[h] = keep.tile([P, HALF], U32, name="w_codes%d" % h, tag=tag, align_bytes=64)
@@ -66,11 +69,12 @@ def tile_picked_sigattn_sigmoid_p_kernel(
         nc.sync.dma_start(d_table[:, 0:LEAD].bitcast(I32), d_src[:, 0:LEAD])
         nc.sync.dma_start(kidx_sb[:], kidx)
         nc.sync.dma_start(d_scale_table[0:P:8, :].bitcast(I32), d_scales[0].bitcast(I32))
+        nc.sync.dma_start(d_table[:, LEAD:MID].bitcast(I32), d_src[:, LEAD:MID])
         nc.sync.dma_start(offs_sb[:], offs)
         nc.sync.dma_start(x_scale_table[0:P:8, :].bitcast(I32), x_scales[0].bitcast(I32))
-        nc.sync.dma_start(d_table[:, LEAD:G].bitcast(I32), d_src[:, LEAD:G])
+        nc.sync.dma_start(d_table[:, MID:G].bitcast(I32), d_src[:, MID:G])
         nc.sync.dma_start(x_table[:].bitcast(I32), x_words[0].rearrange("p c r -> p (c r)").bitcast(I32))
-        w_raw0 = keep.tile([P, PACK, HALF], F32, name="w_raw0", tag="after_cast", align_bytes=64)
+        w_raw0 = keep.tile([P, PACK, HALF], F32, name="w_raw0", align_bytes=64)
         nc.sync.dma_start(w_raw0[:], w_rows[:, :, 0:HALF])
         nc.scalar.activation(warm_out[:], warm_in[:], SIGMOID)
 
@@ -89,10 +93,11 @@ def tile_picked_sigattn_sigmoid_p_kernel(
 
         kb_sb = late.tile([P, PACK], F32, name="kb_sb", align_bytes=32, offset=0)
         nc.sync.dma_start(kb_sb[:], kb.rearrange("(p t) o -> p (t o)", t=PACK))
+        w_raw1 = late.tile([P, PACK, HALF], F32, name="w_raw1", align_bytes=64, offset=64)
+        nc.sync.dma_start(w_raw1[:, 0 : PACK - 1, :], w_rows[:, 0 : PACK - 1, HALF:N])
+        nc.sync.dma_start(w_raw1[:, PACK - 1 : PACK, :], w_rows[:, PACK - 1 : PACK, HALF:N])
         gn_sb = late.tile([P, PACK], F32, name="gn_sb", align_bytes=32, offset=32)
         nc.sync.dma_start(gn_sb[:], gn.rearrange("(p t) o -> p (t o)", t=PACK))
-        w_raw1 = late.tile([P, PACK, HALF], F32, name="w_raw1", align_bytes=64, offset=64)
-        nc.sync.dma_start(w_raw1[:], w_rows[:, :, HALF:N])
 
         keys = keep.tile([P, H], U32, name="keys", align_bytes=64)
         d_picked = [keep.tile([P, HALF], U32, name="d_picked%d" % h, align_bytes=64) for h in range(2)]
@@ -108,20 +113,22 @@ def tile_picked_sigattn_sigmoid_p_kernel(
         deal_keys(0)
         deal_keys(1)
 
-        queries = []
+        queries = keep.tile([P, S], U32, name="queries", align_bytes=64)
         for h in range(2):
-            q = keep.tile([P, HALF], U32, name="queries%d" % h, align_bytes=64)
-            nc.vector.tensor_copy(q[:], x_table[:].indirect(offs_sb[:, h * LIST_HALF : (h + 1) * LIST_HALF]))
-            queries.append(q)
-        cast_w(0, w_raw0, nc.vector.tensor_copy)
+            nc.vector.tensor_copy(
+                queries[:, h * HALF : (h + 1) * HALF],
+                x_table[:].indirect(offs_sb[:, h * LIST_HALF : (h + 1) * LIST_HALF]),
+            )
+        cast_w(0, w_raw0, (nc.scalar.copy, nc.vector.tensor_copy))
+        quantise_w(0, "w_codes0")
+        cast_w(1, w_raw1, (nc.vector.tensor_copy,))
 
-        z = keep.tile([P, S * PACK], BF16, name="z", tag="after_cast", align_bytes=64)
+        z = keep.tile([P, S * PACK], BF16, name="z", align_bytes=64)
         sig = {}
 
         def scores(c, per_bank):
             sig[c] = keep.tile([P, PACK, CHUNK], F32, name="sig%d" % c, align_bytes=64)
             lo = c * CHUNK
-            h, o = divmod(lo, HALF)
             for first in range(0, PACK, per_bank):
                 bank = psum.tile([P, per_bank, CHUNK], F32, name="score", tag="bank", bufs=BANKS)
                 for u in range(per_bank):
@@ -130,7 +137,7 @@ def tile_picked_sigattn_sigmoid_p_kernel(
                         out=bank[:, u, :],
                         lhsT=keys[:, t * P : (t + 1) * P].bitcast(FP8X4),
                         lhsT_scale=planes[:, t * P : (t + 1) * P],
-                        rhs=queries[h][:, o : o + CHUNK].bitcast(FP8X4),
+                        rhs=queries[:, lo : lo + CHUNK].bitcast(FP8X4),
                         rhs_scale=planes[:, H + lo : H + lo + CHUNK],
                         start=True,
                         stop=True,
@@ -176,19 +183,28 @@ def tile_picked_sigattn_sigmoid_p_kernel(
 
         scores(0, 1)
         for c in range(1, S // CHUNK):
-            scores(c, 2)
+            scores(c, 1)
+
+        for t in range(2):
+            idle = psum.tile([P, S], F32, name="idle", tag="bank", bufs=BANKS)
+            nc.tensor.matmul_mx(
+                out=idle[:],
+                lhsT=keys[:, t * P : (t + 1) * P].bitcast(FP8X4),
+                lhsT_scale=planes[:, t * P : (t + 1) * P],
+                rhs=queries[:].bitcast(FP8X4),
+                rhs_scale=planes[:, H : H + S],
+                start=True,
+                stop=True,
+            )
 
         weigh(0)
         weigh(1)
-        quantise_w(0, "w_codes0")
-        quantise_z(0, HALF)
-        for a in range(2):
-            finish(0, a, nc.scalar.copy)
-        cast_w(1, w_raw1, nc.vector.tensor_copy)
-        weigh(2)
         quantise_w(1, "w_codes1")
-        for a in range(2, 4):
+        quantise_z(0, HALF)
+        for a in range(N // P):
             finish(0, a, nc.scalar.copy)
+
+        weigh(2)
         weigh(3)
         quantise_z(2 * CHUNK, CHUNK)
         quantise_z(3 * CHUNK, CHUNK)

@@ -40,25 +40,27 @@ def tile_picked_sigattn_sigmoid_p_kernel(
         d_table = keep.tile([P, G], U32, name="d_table", align_bytes=64)
         x_table = keep.tile([P, T], U32, name="x_table", align_bytes=64)
         d_scale_table = keep.tile([P, G], U8, name="d_scale_table", align_bytes=64)
-        x_scale_table = keep.tile([P, T], U8, name="x_scale_table", tag="after_scales", align_bytes=64)
+        x_scale_table = late.tile([P, T], U8, name="x_scale_table", align_bytes=64, offset=4032)
+        rows = keep.tile([P, H + S], U8, name="rows", align_bytes=64)
         warm_in = keep.tile([P, 8], F32, name="warm_in")
         warm_out = keep.tile([P, 8], F32, name="warm_out")
 
         nc.vector.memset(d_scale_table[:].bitcast(I32), 0)
         nc.vector.memset(x_scale_table[:].bitcast(I32), 0)
         nc.vector.memset(warm_in[:], 0.0)
+        nc.vector.memset(rows[:].bitcast(I32), 0)
 
         w_rows = w1.rearrange("(p j) m -> p j m", j=PACK)
         w_codes, w_scales, w_grouped = {}, {}, {}
 
-        def cast_w(h, raw, copies):
+        for h in range(2):
             w_grouped[h] = keep.tile([P, HALF * PACK], BF16, name="w_grouped%d" % h, align_bytes=64)
-            width = HALF // len(copies)
-            for k, copy in enumerate(copies):
-                copy(
-                    w_grouped[h][:, k * width * PACK : (k + 1) * width * PACK].rearrange("p (c i j) -> p c j i", i=RUN, j=PACK),
-                    raw[:, :, k * width : (k + 1) * width].rearrange("p j (c i) -> p c j i", i=RUN),
-                )
+
+        def cast_w(h, raw, lo, width, copy):
+            copy(
+                w_grouped[h][:, lo * PACK : (lo + width) * PACK].rearrange("p (c i j) -> p c j i", i=RUN, j=PACK),
+                raw[:, :, lo : lo + width].rearrange("p j (c i) -> p c j i", i=RUN),
+            )
 
         def quantise_w(h, tag):
             w_codes[h] = keep.tile([P, HALF], U32, name="w_codes%d" % h, tag=tag, align_bytes=64)
@@ -74,30 +76,22 @@ def tile_picked_sigattn_sigmoid_p_kernel(
         nc.sync.dma_start(x_scale_table[0:P:8, :].bitcast(I32), x_scales[0].bitcast(I32))
         nc.sync.dma_start(d_table[:, MID:G].bitcast(I32), d_src[:, MID:G])
         nc.sync.dma_start(x_table[:].bitcast(I32), x_words[0].rearrange("p c r -> p (c r)").bitcast(I32))
-        w_raw0 = keep.tile([P, PACK, HALF], F32, name="w_raw0", align_bytes=64)
-        nc.sync.dma_start(w_raw0[:], w_rows[:, :, 0:HALF])
         nc.scalar.activation(warm_out[:], warm_in[:], SIGMOID)
 
-        d_scale_picked = keep.tile([P, H], U8, name="d_scale_picked", align_bytes=64)
-        x_scale_picked = late.tile([P, S], U8, name="x_scale_picked", align_bytes=64, offset=0)
-        nc.vector.tensor_copy(d_scale_picked[:], d_scale_table[:].indirect(kidx_sb[:]))
-        nc.vector.tensor_copy(x_scale_picked[:], x_scale_table[:].indirect(offs_sb[:]))
-        planes = keep.tile([P, H + S], U8, name="planes", tag="after_scales", align_bytes=64)
-        nc.vector.tensor_copy(
-            planes[:, 0:H].rearrange("p (t m) -> p m t", t=PACK),
-            d_scale_picked[:].rearrange("p (m t) -> p m t", t=PACK),
-        )
-        nc.vector.tensor_copy(planes[:, H : H + S].bitcast(I32), x_scale_picked[:].bitcast(I32))
-        for r in range(1, 4):
-            nc.sync.dma_start(planes[r:P:32, :].bitcast(I32), planes[8 * r : P : 32, :].bitcast(I32))
+        picked = keep.tile([P, H + S], U8, name="picked", tag="after_moves", align_bytes=64)
+        nc.vector.tensor_copy(picked[:, 0:H], d_scale_table[:].indirect(kidx_sb[:]))
+        nc.vector.tensor_copy(picked[:, H : H + S], x_scale_table[:].indirect(offs_sb[:]))
+        for r in range(4):
+            nc.sync.dma_start(rows[r:P:32, :].bitcast(I32), picked[8 * r : P : 32, :].bitcast(I32))
 
-        kb_sb = late.tile([P, PACK], F32, name="kb_sb", align_bytes=32, offset=0)
+        w_raw0 = late.tile([P, PACK, HALF], F32, name="w_raw0", align_bytes=64, offset=0)
+        nc.sync.dma_start(w_raw0[:], w_rows[:, :, 0:HALF])
+        kb_sb = late.tile([P, PACK], F32, name="kb_sb", align_bytes=32, offset=4096)
         nc.sync.dma_start(kb_sb[:], kb.rearrange("(p t) o -> p (t o)", t=PACK))
-        w_raw1 = late.tile([P, PACK, HALF], F32, name="w_raw1", align_bytes=64, offset=64)
-        nc.sync.dma_start(w_raw1[:, 0 : PACK - 1, :], w_rows[:, 0 : PACK - 1, HALF:N])
-        nc.sync.dma_start(w_raw1[:, PACK - 1 : PACK, :], w_rows[:, PACK - 1 : PACK, HALF:N])
-        gn_sb = late.tile([P, PACK], F32, name="gn_sb", align_bytes=32, offset=32)
+        gn_sb = late.tile([P, PACK], F32, name="gn_sb", align_bytes=32, offset=4128)
         nc.sync.dma_start(gn_sb[:], gn.rearrange("(p t) o -> p (t o)", t=PACK))
+        w_raw1 = late.tile([P, PACK, HALF], F32, name="w_raw1", align_bytes=64, offset=4160)
+        nc.sync.dma_start(w_raw1[:], w_rows[:, :, HALF:N])
 
         keys = keep.tile([P, H], U32, name="keys", align_bytes=64)
         d_picked = [keep.tile([P, HALF], U32, name="d_picked%d" % h, align_bytes=64) for h in range(2)]
@@ -113,15 +107,19 @@ def tile_picked_sigattn_sigmoid_p_kernel(
         deal_keys(0)
         deal_keys(1)
 
-        queries = keep.tile([P, S], U32, name="queries", align_bytes=64)
-        for h in range(2):
-            nc.vector.tensor_copy(
-                queries[:, h * HALF : (h + 1) * HALF],
-                x_table[:].indirect(offs_sb[:, h * LIST_HALF : (h + 1) * LIST_HALF]),
-            )
-        cast_w(0, w_raw0, (nc.scalar.copy, nc.vector.tensor_copy))
+        queries = [
+            keep.tile([P, HALF], U32, name="queries0", align_bytes=64),
+            keep.tile([P, HALF], U32, name="queries1", tag="after_moves", align_bytes=64),
+        ]
+        key_scales = keep.tile([P, H], U8, name="key_scales", align_bytes=64)
+        nc.vector.tensor_copy(queries[0][:], x_table[:].indirect(offs_sb[:, 0:LIST_HALF]))
+        nc.vector.tensor_copy(
+            key_scales[:].rearrange("p (t m) -> p m t", t=PACK),
+            rows[:, 0:H].rearrange("p (m t) -> p m t", t=PACK),
+        )
+        nc.vector.tensor_copy(queries[1][:], x_table[:].indirect(offs_sb[:, LIST_HALF : 2 * LIST_HALF]))
+        cast_w(0, w_raw0, 0, HALF, nc.vector.tensor_copy)
         quantise_w(0, "w_codes0")
-        cast_w(1, w_raw1, (nc.vector.tensor_copy,))
 
         z = keep.tile([P, S * PACK], BF16, name="z", align_bytes=64)
         sig = {}
@@ -129,6 +127,7 @@ def tile_picked_sigattn_sigmoid_p_kernel(
         def scores(c, per_bank):
             sig[c] = keep.tile([P, PACK, CHUNK], F32, name="sig%d" % c, align_bytes=64)
             lo = c * CHUNK
+            h, o = divmod(lo, HALF)
             for first in range(0, PACK, per_bank):
                 bank = psum.tile([P, per_bank, CHUNK], F32, name="score", tag="bank", bufs=BANKS)
                 for u in range(per_bank):
@@ -136,9 +135,9 @@ def tile_picked_sigattn_sigmoid_p_kernel(
                     nc.tensor.matmul_mx(
                         out=bank[:, u, :],
                         lhsT=keys[:, t * P : (t + 1) * P].bitcast(FP8X4),
-                        lhsT_scale=planes[:, t * P : (t + 1) * P],
-                        rhs=queries[:, lo : lo + CHUNK].bitcast(FP8X4),
-                        rhs_scale=planes[:, H + lo : H + lo + CHUNK],
+                        lhsT_scale=key_scales[:, t * P : (t + 1) * P],
+                        rhs=queries[h][:, o : o + CHUNK].bitcast(FP8X4),
+                        rhs_scale=rows[:, H + lo : H + lo + CHUNK],
                         start=True,
                         stop=True,
                     )
@@ -182,7 +181,9 @@ def tile_picked_sigattn_sigmoid_p_kernel(
             nc.sync.dma_start(out[a * P : (a + 1) * P, cols], res[:])
 
         scores(0, 1)
-        for c in range(1, S // CHUNK):
+        scores(1, 1)
+        cast_w(1, w_raw1, P, P, nc.scalar.copy)
+        for c in range(2, S // CHUNK):
             scores(c, 1)
 
         for t in range(2):
@@ -190,14 +191,15 @@ def tile_picked_sigattn_sigmoid_p_kernel(
             nc.tensor.matmul_mx(
                 out=idle[:],
                 lhsT=keys[:, t * P : (t + 1) * P].bitcast(FP8X4),
-                lhsT_scale=planes[:, t * P : (t + 1) * P],
-                rhs=queries[:].bitcast(FP8X4),
-                rhs_scale=planes[:, H : H + S],
+                lhsT_scale=key_scales[:, t * P : (t + 1) * P],
+                rhs=keys[:].bitcast(FP8X4),
+                rhs_scale=key_scales[:],
                 start=True,
                 stop=True,
             )
 
         weigh(0)
+        cast_w(1, w_raw1, 0, P, nc.vector.tensor_copy)
         weigh(1)
         quantise_w(1, "w_codes1")
         quantise_z(0, HALF)

@@ -62,10 +62,16 @@ def tile_picked_sigattn_sigmoid_p_kernel(
                 raw[:, :, lo : lo + width].rearrange("p j (c i) -> p c j i", i=RUN),
             )
 
-        def quantise_w(h, tag):
-            w_codes[h] = keep.tile([P, HALF], U32, name="w_codes%d" % h, tag=tag, align_bytes=64)
+        for h in range(2):
+            w_codes[h] = keep.tile([P, HALF], U32, name="w_codes%d" % h, align_bytes=64)
             w_scales[h] = keep.tile([P, HALF], U8, name="w_scales%d" % h, align_bytes=64)
-            nc.vector.quantize_mx(out=w_codes[h][:].bitcast(FP8X4), scales=w_scales[h][:], in_=w_grouped[h][:])
+
+        def quantise_w(h, lo, width):
+            nc.vector.quantize_mx(
+                out=w_codes[h][:, lo : lo + width].bitcast(FP8X4),
+                scales=w_scales[h][:, lo : lo + width],
+                in_=w_grouped[h][:, lo * PACK : (lo + width) * PACK],
+            )
 
         d_src = d_words[0].rearrange("p c r -> p (c r)").bitcast(I32)
         nc.sync.dma_start(d_table[:, 0:LEAD].bitcast(I32), d_src[:, 0:LEAD])
@@ -82,7 +88,8 @@ def tile_picked_sigattn_sigmoid_p_kernel(
         nc.vector.tensor_copy(picked[:, 0:H], d_scale_table[:].indirect(kidx_sb[:]))
         nc.vector.tensor_copy(picked[:, H : H + S], x_scale_table[:].indirect(offs_sb[:]))
         for r in range(4):
-            nc.sync.dma_start(rows[r:P:32, :].bitcast(I32), picked[8 * r : P : 32, :].bitcast(I32))
+            queue = nc.scalar if r % 2 else nc.sync
+            queue.dma_start(rows[r:P:32, :].bitcast(I32), picked[8 * r : P : 32, :].bitcast(I32))
 
         w_raw0 = late.tile([P, PACK, HALF], F32, name="w_raw0", align_bytes=64, offset=0)
         nc.sync.dma_start(w_raw0[:], w_rows[:, :, 0:HALF])
@@ -113,13 +120,16 @@ def tile_picked_sigattn_sigmoid_p_kernel(
         ]
         key_scales = keep.tile([P, H], U8, name="key_scales", align_bytes=64)
         nc.vector.tensor_copy(queries[0][:], x_table[:].indirect(offs_sb[:, 0:LIST_HALF]))
-        nc.vector.tensor_copy(
-            key_scales[:].rearrange("p (t m) -> p m t", t=PACK),
-            rows[:, 0:H].rearrange("p (m t) -> p m t", t=PACK),
-        )
+        for tiles in (slice(0, 1), slice(1, PACK)):
+            nc.vector.tensor_copy(
+                key_scales[:].rearrange("p (t m) -> p m t", t=PACK)[:, :, tiles],
+                rows[:, 0:H].rearrange("p (m t) -> p m t", t=PACK)[:, :, tiles],
+            )
         nc.vector.tensor_copy(queries[1][:], x_table[:].indirect(offs_sb[:, LIST_HALF : 2 * LIST_HALF]))
-        cast_w(0, w_raw0, 0, HALF, nc.vector.tensor_copy)
-        quantise_w(0, "w_codes0")
+        for lo in range(0, HALF, P):
+            cast_w(0, w_raw0, lo, P, nc.vector.tensor_copy)
+        for lo in range(0, HALF, P):
+            quantise_w(0, lo, P)
 
         z = keep.tile([P, S * PACK], BF16, name="z", align_bytes=64)
         sig = {}
@@ -201,7 +211,7 @@ def tile_picked_sigattn_sigmoid_p_kernel(
         weigh(0)
         cast_w(1, w_raw1, 0, P, nc.vector.tensor_copy)
         weigh(1)
-        quantise_w(1, "w_codes1")
+        quantise_w(1, 0, HALF)
         quantise_z(0, HALF)
         for a in range(N // P):
             finish(0, a, nc.scalar.copy)

@@ -1,6 +1,7 @@
 from contextlib import ExitStack
 
 import concourse.mybir as mybir
+from concourse.masks import make_identity
 
 K, T, S, N, G, H = 512, 2048, 512, 512, 2048, 512
 FLOPS = 2 * K * H * S + 2 * H * N * S
@@ -20,7 +21,6 @@ PACK = 4
 RUN = 4
 CHUNK = 128
 HALF = 256
-LIST_HALF = HALF // 16
 LEAD = 448
 MID = 960
 BANKS = 8
@@ -44,34 +44,16 @@ def tile_picked_sigattn_sigmoid_p_kernel(
         rows = keep.tile([P, H + S], U8, name="rows", align_bytes=64)
         warm_in = keep.tile([P, 8], F32, name="warm_in")
         warm_out = keep.tile([P, 8], F32, name="warm_out")
+        key_rows = keep.tile([P, H], F32, name="key_rows", align_bytes=64)
+        ident = keep.tile([P, P], F32, name="ident", align_bytes=64)
 
         nc.vector.memset(d_scale_table[:].bitcast(I32), 0)
         nc.vector.memset(x_scale_table[:].bitcast(I32), 0)
         nc.vector.memset(warm_in[:], 0.0)
+        nc.vector.memset(key_rows[:], 0.0)
         nc.vector.memset(rows[:].bitcast(I32), 0)
-
-        w_rows = w1.rearrange("(p j) m -> p j m", j=PACK)
-        w_codes, w_scales, w_grouped = {}, {}, {}
-
-        for h in range(2):
-            w_grouped[h] = keep.tile([P, HALF * PACK], BF16, name="w_grouped%d" % h, align_bytes=64)
-
-        def cast_w(h, raw, lo, width, copy):
-            copy(
-                w_grouped[h][:, lo * PACK : (lo + width) * PACK].rearrange("p (c i j) -> p c j i", i=RUN, j=PACK),
-                raw[:, :, lo : lo + width].rearrange("p j (c i) -> p c j i", i=RUN),
-            )
-
-        for h in range(2):
-            w_codes[h] = keep.tile([P, HALF], U32, name="w_codes%d" % h, align_bytes=64)
-            w_scales[h] = keep.tile([P, HALF], U8, name="w_scales%d" % h, align_bytes=64)
-
-        def quantise_w(h, lo, width):
-            nc.vector.quantize_mx(
-                out=w_codes[h][:, lo : lo + width].bitcast(FP8X4),
-                scales=w_scales[h][:, lo : lo + width],
-                in_=w_grouped[h][:, lo * PACK : (lo + width) * PACK],
-            )
+        nc.vector.memset(ident[:], 0.0)
+        make_identity(nc, ident[:], nomemset=True)
 
         d_src = d_words[0].rearrange("p c r -> p (c r)").bitcast(I32)
         nc.sync.dma_start(d_table[:, 0:LEAD].bitcast(I32), d_src[:, 0:LEAD])
@@ -81,144 +63,145 @@ def tile_picked_sigattn_sigmoid_p_kernel(
         nc.sync.dma_start(offs_sb[:], offs)
         nc.sync.dma_start(x_scale_table[0:P:8, :].bitcast(I32), x_scales[0].bitcast(I32))
         nc.sync.dma_start(d_table[:, MID:G].bitcast(I32), d_src[:, MID:G])
+        nc.sync.dma_start(key_rows[0:1, :], kb.rearrange("h o -> o h"))
+        nc.sync.dma_start(key_rows[1:2, :], gn.rearrange("h o -> o h"))
         nc.sync.dma_start(x_table[:].bitcast(I32), x_words[0].rearrange("p c r -> p (c r)").bitcast(I32))
         nc.scalar.activation(warm_out[:], warm_in[:], SIGMOID)
 
-        picked = keep.tile([P, H + S], U8, name="picked", tag="after_moves", align_bytes=64)
+        turned = psum.tile([P, PACK, P], F32, name="turned", tag="bank", bufs=BANKS)
+        for t in range(PACK):
+            nc.tensor.transpose(turned[:, t, :], key_rows[:, t:H:PACK], ident[:])
+        key_cols = keep.tile([P, 2, PACK], F32, name="key_cols", align_bytes=32)
+        nc.scalar.copy(key_cols[:], turned[:, :, 0:2].rearrange("p t r -> p r t"))
+
+        picked = late.tile([P, H + S], U8, name="picked", align_bytes=64, offset=9600)
         nc.vector.tensor_copy(picked[:, 0:H], d_scale_table[:].indirect(kidx_sb[:]))
         nc.vector.tensor_copy(picked[:, H : H + S], x_scale_table[:].indirect(offs_sb[:]))
         for r in range(4):
             queue = nc.scalar if r % 2 else nc.sync
             queue.dma_start(rows[r:P:32, :].bitcast(I32), picked[8 * r : P : 32, :].bitcast(I32))
 
-        w_raw0 = late.tile([P, PACK, HALF], F32, name="w_raw0", align_bytes=64, offset=0)
-        nc.sync.dma_start(w_raw0[:], w_rows[:, :, 0:HALF])
-        kb_sb = late.tile([P, PACK], F32, name="kb_sb", align_bytes=32, offset=4096)
-        nc.sync.dma_start(kb_sb[:], kb.rearrange("(p t) o -> p (t o)", t=PACK))
-        gn_sb = late.tile([P, PACK], F32, name="gn_sb", align_bytes=32, offset=4128)
-        nc.sync.dma_start(gn_sb[:], gn.rearrange("(p t) o -> p (t o)", t=PACK))
-        w_raw1 = late.tile([P, PACK, HALF], F32, name="w_raw1", align_bytes=64, offset=4160)
-        nc.sync.dma_start(w_raw1[:], w_rows[:, :, HALF:N])
+        w_rows = w1.rearrange("(p j) m -> p j m", j=PACK)
+        w_raw = [late.tile([P, PACK, HALF], F32, name="w_raw%d" % h, align_bytes=64, offset=4096 * h) for h in range(2)]
+        for h in range(2):
+            nc.sync.dma_start(w_raw[h][:], w_rows[:, :, h * HALF : (h + 1) * HALF])
 
         keys = keep.tile([P, H], U32, name="keys", align_bytes=64)
         d_picked = [keep.tile([P, HALF], U32, name="d_picked%d" % h, align_bytes=64) for h in range(2)]
         for h in range(2):
-            nc.vector.tensor_copy(d_picked[h][:], d_table[:].indirect(kidx_sb[:, h * LIST_HALF : (h + 1) * LIST_HALF]))
-
-        def deal_keys(h):
+            nc.vector.tensor_copy(d_picked[h][:], d_table[:].indirect(kidx_sb[:, h * 16 : (h + 1) * 16]))
+        for h in range(2):
             nc.vector.tensor_copy(
                 keys[:].rearrange("p (t g c i) -> p g c t i", t=PACK, g=2, i=RUN)[:, h],
                 d_picked[h][:].rearrange("p (c i t) -> p c t i", t=PACK, i=RUN),
             )
 
-        deal_keys(0)
-        deal_keys(1)
-
-        queries = [
-            keep.tile([P, HALF], U32, name="queries0", align_bytes=64),
-            keep.tile([P, HALF], U32, name="queries1", tag="after_moves", align_bytes=64),
-        ]
+        queries = [keep.tile([P, CHUNK], U32, name="queries0", align_bytes=64)]
+        queries.append(late.tile([P, CHUNK], U32, name="queries1", align_bytes=64, offset=9152))
+        queries.append(late.tile([P, HALF], U32, name="queries2", align_bytes=64, offset=10560))
         key_scales = keep.tile([P, H], U8, name="key_scales", align_bytes=64)
-        nc.vector.tensor_copy(queries[0][:], x_table[:].indirect(offs_sb[:, 0:LIST_HALF]))
+        nc.vector.tensor_copy(queries[0][:], x_table[:].indirect(offs_sb[:, 0:8]))
         for tiles in (slice(0, 1), slice(1, PACK)):
             nc.vector.tensor_copy(
                 key_scales[:].rearrange("p (t m) -> p m t", t=PACK)[:, :, tiles],
                 rows[:, 0:H].rearrange("p (m t) -> p m t", t=PACK)[:, :, tiles],
             )
-        nc.vector.tensor_copy(queries[1][:], x_table[:].indirect(offs_sb[:, LIST_HALF : 2 * LIST_HALF]))
-        for lo in range(0, HALF, P):
-            cast_w(0, w_raw0, lo, P, nc.vector.tensor_copy)
-        for lo in range(0, HALF, P):
-            quantise_w(0, lo, P)
+        nc.vector.tensor_copy(queries[1][:], x_table[:].indirect(offs_sb[:, 8:16]))
+        nc.vector.tensor_copy(queries[2][:], x_table[:].indirect(offs_sb[:, 16:32]))
 
-        z = keep.tile([P, S * PACK], BF16, name="z", align_bytes=64)
-        sig = {}
+        sig = {
+            0: late.tile([P, PACK, CHUNK], F32, name="sig0", align_bytes=64, offset=12544),
+            CHUNK: keep.tile([P, PACK, CHUNK], F32, name="sig1", align_bytes=64),
+            HALF: keep.tile([P, PACK, HALF], F32, name="sig2", align_bytes=64),
+        }
 
-        def scores(c, per_bank):
-            sig[c] = keep.tile([P, PACK, CHUNK], F32, name="sig%d" % c, align_bytes=64)
-            lo = c * CHUNK
-            h, o = divmod(lo, HALF)
-            for first in range(0, PACK, per_bank):
-                bank = psum.tile([P, per_bank, CHUNK], F32, name="score", tag="bank", bufs=BANKS)
-                for u in range(per_bank):
-                    t = first + u
-                    nc.tensor.matmul_mx(
-                        out=bank[:, u, :],
-                        lhsT=keys[:, t * P : (t + 1) * P].bitcast(FP8X4),
-                        lhsT_scale=key_scales[:, t * P : (t + 1) * P],
-                        rhs=queries[h][:, o : o + CHUNK].bitcast(FP8X4),
-                        rhs_scale=rows[:, H + lo : H + lo + CHUNK],
-                        start=True,
-                        stop=True,
-                    )
-                for u in range(per_bank):
-                    t = first + u
-                    nc.scalar.activation(sig[c][:, t, :], bank[:, u, :], SIGMOID, bias=kb_sb[:, t : t + 1], scale=0.0625)
+        def scores(lo, width):
+            moving = queries[lo // CHUNK][:]
+            for t in range(PACK):
+                bank = psum.tile([P, width], F32, name="score", tag="bank", bufs=BANKS)
+                nc.tensor.matmul_mx(
+                    out=bank[:],
+                    lhsT=keys[:, t * P : (t + 1) * P].bitcast(FP8X4),
+                    lhsT_scale=key_scales[:, t * P : (t + 1) * P],
+                    rhs=moving.bitcast(FP8X4),
+                    rhs_scale=rows[:, H + lo : H + lo + width],
+                    start=True,
+                    stop=True,
+                )
+                nc.scalar.activation(sig[lo][:, t, :], bank[:], SIGMOID, bias=key_cols[:, 0, t : t + 1], scale=0.0625)
 
-        def weigh(c):
-            nc.vector.tensor_tensor(
-                z[:, c * CHUNK * PACK : (c + 1) * CHUNK * PACK].rearrange("p (c i t) -> p c t i", i=RUN, t=PACK),
-                sig[c][:].rearrange("p t (c i) -> p c t i", i=RUN),
-                gn_sb[:].unsqueeze(1).unsqueeze(3).broadcast_to([P, CHUNK // RUN, PACK, RUN]),
-                MULT,
-            )
-
+        z_first = keep.tile([P, HALF * PACK], BF16, name="z_first", align_bytes=64)
+        z_second = keep.tile([P, HALF * PACK], BF16, name="z_second", align_bytes=64)
+        w_codes = keep.tile([P, N], U32, name="w_codes", align_bytes=64)
+        w_scales = keep.tile([P, N], U8, name="w_scales", align_bytes=64)
         z_codes = keep.tile([P, S], U32, name="z_codes", align_bytes=64)
         z_scales = keep.tile([P, S], U8, name="z_scales", align_bytes=64)
 
-        def quantise_z(lo, width):
-            nc.vector.quantize_mx(
-                out=z_codes[:, lo : lo + width].bitcast(FP8X4),
-                scales=z_scales[:, lo : lo + width],
-                in_=z[:, lo * PACK : (lo + width) * PACK],
-            )
-
-        def finish(lo, a, copy):
-            cols = slice(lo, lo + HALF)
+        def cast(dst, a, copy):
             h, o = divmod(a * P, HALF)
-            bank = psum.tile([P, HALF], F32, name="acc", tag="bank", bufs=BANKS)
-            nc.tensor.matmul_mx(
-                out=bank[:],
-                lhsT=w_codes[h][:, o : o + P].bitcast(FP8X4),
-                lhsT_scale=w_scales[h][:, o : o + P],
-                rhs=z_codes[:, cols].bitcast(FP8X4),
-                rhs_scale=z_scales[:, cols],
-                start=True,
-                stop=True,
+            copy(dst[:].rearrange("p (c i j) -> p c j i", i=RUN, j=PACK), w_raw[h][:, :, o : o + P].rearrange("p j (c i) -> p c j i", i=RUN))
+
+        def quantise(codes, scales, lo, width, src):
+            nc.vector.quantize_mx(out=codes[:, lo : lo + width].bitcast(FP8X4), scales=scales[:, lo : lo + width], in_=src)
+
+        def weigh(lo, width):
+            h, o = divmod(lo, HALF)
+            z = z_second if h else z_first
+            nc.vector.tensor_tensor(
+                z[:, o * PACK : (o + width) * PACK].rearrange("p (c i t) -> p c t i", i=RUN, t=PACK),
+                sig[min(lo, HALF)][:, :, h * o : h * o + width].rearrange("p t (c i) -> p c t i", i=RUN),
+                key_cols[:, 1, :].unsqueeze(1).unsqueeze(3).broadcast_to([P, width // RUN, PACK, RUN]),
+                MULT,
             )
-            res = keep.tile([P, HALF], F32, name="res%d_%d" % (lo, a), align_bytes=64)
+
+        def finish(lo, width, first, count, copy):
+            cols = slice(lo, lo + width)
+            bank = psum.tile([P, count, width], F32, name="acc", tag="bank", bufs=BANKS)
+            for u in range(count):
+                a = first + u
+                nc.tensor.matmul_mx(
+                    out=bank[:, u, :],
+                    lhsT=w_codes[:, a * P : (a + 1) * P].bitcast(FP8X4),
+                    lhsT_scale=w_scales[:, a * P : (a + 1) * P],
+                    rhs=z_codes[:, cols].bitcast(FP8X4),
+                    rhs_scale=z_scales[:, cols],
+                    start=True,
+                    stop=True,
+                )
+            res = keep.tile([P, count, width], F32, name="res%d_%d" % (lo, first), align_bytes=64)
             copy(res[:], bank[:])
-            nc.sync.dma_start(out[a * P : (a + 1) * P, cols], res[:])
+            nc.sync.dma_start(out[first * P : (first + count) * P, cols].rearrange("(a p) c -> p a c", p=P), res[:])
 
-        scores(0, 1)
-        scores(1, 1)
-        cast_w(1, w_raw1, P, P, nc.scalar.copy)
-        for c in range(2, S // CHUNK):
-            scores(c, 1)
+        w_cast = [
+            keep.tile([P, P * PACK], BF16, name="w_cast0", align_bytes=64),
+            keep.tile([P, P * PACK], BF16, name="w_cast1", align_bytes=64),
+            late.tile([P, P * PACK], BF16, name="w_cast2", align_bytes=64, offset=12544),
+            late.tile([P, P * PACK], BF16, name="w_cast3", align_bytes=64, offset=11520),
+        ]
+        scores(0, CHUNK)
+        scores(CHUNK, CHUNK)
+        scores(HALF, HALF)
+        cast(w_cast[3], 3, nc.scalar.copy)
 
-        for t in range(2):
-            idle = psum.tile([P, S], F32, name="idle", tag="bank", bufs=BANKS)
-            nc.tensor.matmul_mx(
-                out=idle[:],
-                lhsT=keys[:, t * P : (t + 1) * P].bitcast(FP8X4),
-                lhsT_scale=key_scales[:, t * P : (t + 1) * P],
-                rhs=keys[:].bitcast(FP8X4),
-                rhs_scale=key_scales[:],
-                start=True,
-                stop=True,
-            )
-
-        weigh(0)
-        cast_w(1, w_raw1, 0, P, nc.vector.tensor_copy)
-        weigh(1)
-        quantise_w(1, 0, HALF)
-        quantise_z(0, HALF)
-        for a in range(N // P):
-            finish(0, a, nc.scalar.copy)
-
-        weigh(2)
-        weigh(3)
-        quantise_z(2 * CHUNK, CHUNK)
-        quantise_z(3 * CHUNK, CHUNK)
-        for a in range(N // P):
-            finish(HALF, a, nc.scalar.copy if a % 2 else nc.vector.tensor_copy)
+        for a in range(2):
+            cast(w_cast[a], a, nc.vector.tensor_copy)
+        for a in range(2):
+            quantise(w_codes, w_scales, a * P, P, w_cast[a][:])
+        weigh(0, CHUNK)
+        weigh(CHUNK, CHUNK)
+        cast(w_cast[2], 2, nc.vector.tensor_copy)
+        quantise(z_codes, z_scales, 0, HALF, z_first[:])
+        for a in range(2):
+            finish(0, HALF, a, 1, nc.scalar.copy)
+        weigh(HALF, CHUNK)
+        for a in range(2, 4):
+            quantise(w_codes, w_scales, a * P, P, w_cast[a][:])
+        quantise(z_codes, z_scales, HALF, CHUNK, z_second[:, 0 : CHUNK * PACK])
+        for a in range(2, 4):
+            finish(0, HALF, a, 1, nc.scalar.copy)
+        weigh(HALF + CHUNK, CHUNK)
+        finish(HALF, CHUNK, 0, 2, nc.vector.tensor_copy)
+        finish(HALF, CHUNK, 2, 2, nc.scalar.copy)
+        quantise(z_codes, z_scales, HALF + CHUNK, CHUNK, z_second[:, CHUNK * PACK : HALF * PACK])
+        finish(HALF + CHUNK, CHUNK, 0, 2, nc.scalar.copy)
+        finish(HALF + CHUNK, CHUNK, 2, 2, nc.vector.tensor_copy)

@@ -1,7 +1,6 @@
 from contextlib import ExitStack
 
 import concourse.mybir as mybir
-from concourse.masks import make_identity
 
 K, T, S, N, G, H = 512, 2048, 512, 512, 2048, 512
 FLOPS = 2 * K * H * S + 2 * H * N * S
@@ -44,16 +43,11 @@ def tile_picked_sigattn_sigmoid_p_kernel(
         rows = keep.tile([P, H + S], U8, name="rows", align_bytes=64)
         warm_in = keep.tile([P, 8], F32, name="warm_in")
         warm_out = keep.tile([P, 8], F32, name="warm_out")
-        key_rows = keep.tile([P, H], F32, name="key_rows", align_bytes=64)
-        ident = keep.tile([P, P], F32, name="ident", align_bytes=64)
 
         nc.vector.memset(d_scale_table[:].bitcast(I32), 0)
         nc.vector.memset(x_scale_table[:].bitcast(I32), 0)
         nc.vector.memset(warm_in[:], 0.0)
-        nc.vector.memset(key_rows[:], 0.0)
         nc.vector.memset(rows[:].bitcast(I32), 0)
-        nc.vector.memset(ident[:], 0.0)
-        make_identity(nc, ident[:], nomemset=True)
 
         d_src = d_words[0].rearrange("p c r -> p (c r)").bitcast(I32)
         nc.sync.dma_start(d_table[:, 0:LEAD].bitcast(I32), d_src[:, 0:LEAD])
@@ -63,16 +57,8 @@ def tile_picked_sigattn_sigmoid_p_kernel(
         nc.sync.dma_start(offs_sb[:], offs)
         nc.sync.dma_start(x_scale_table[0:P:8, :].bitcast(I32), x_scales[0].bitcast(I32))
         nc.sync.dma_start(d_table[:, MID:G].bitcast(I32), d_src[:, MID:G])
-        nc.sync.dma_start(key_rows[0:1, :], kb.rearrange("h o -> o h"))
-        nc.sync.dma_start(key_rows[1:2, :], gn.rearrange("h o -> o h"))
         nc.sync.dma_start(x_table[:].bitcast(I32), x_words[0].rearrange("p c r -> p (c r)").bitcast(I32))
         nc.scalar.activation(warm_out[:], warm_in[:], SIGMOID)
-
-        turned = psum.tile([P, PACK, P], F32, name="turned", tag="bank", bufs=BANKS)
-        for t in range(PACK):
-            nc.tensor.transpose(turned[:, t, :], key_rows[:, t:H:PACK], ident[:])
-        key_cols = keep.tile([P, 2, PACK], F32, name="key_cols", align_bytes=32)
-        nc.scalar.copy(key_cols[:], turned[:, :, 0:2].rearrange("p t r -> p r t"))
 
         picked = late.tile([P, H + S], U8, name="picked", align_bytes=64, offset=9600)
         nc.vector.tensor_copy(picked[:, 0:H], d_scale_table[:].indirect(kidx_sb[:]))
@@ -82,9 +68,13 @@ def tile_picked_sigattn_sigmoid_p_kernel(
             queue.dma_start(rows[r:P:32, :].bitcast(I32), picked[8 * r : P : 32, :].bitcast(I32))
 
         w_rows = w1.rearrange("(p j) m -> p j m", j=PACK)
-        w_raw = [late.tile([P, PACK, HALF], F32, name="w_raw%d" % h, align_bytes=64, offset=4096 * h) for h in range(2)]
-        for h in range(2):
-            nc.sync.dma_start(w_raw[h][:], w_rows[:, :, h * HALF : (h + 1) * HALF])
+        w_raw = [late.tile([P, PACK, HALF], F32, name="w_raw%d" % h, align_bytes=64, offset=4160 * h) for h in range(2)]
+        kb_sb = late.tile([P, PACK], F32, name="kb_sb", align_bytes=32, offset=4096)
+        gn_sb = late.tile([P, PACK], F32, name="gn_sb", align_bytes=32, offset=4128)
+        nc.sync.dma_start(w_raw[0][:], w_rows[:, :, 0:HALF])
+        nc.sync.dma_start(kb_sb[:], kb.rearrange("(p t) o -> p (t o)", t=PACK))
+        nc.sync.dma_start(gn_sb[:], gn.rearrange("(p t) o -> p (t o)", t=PACK))
+        nc.sync.dma_start(w_raw[1][:], w_rows[:, :, HALF:N])
 
         keys = keep.tile([P, H], U32, name="keys", align_bytes=64)
         d_picked = [keep.tile([P, HALF], U32, name="d_picked%d" % h, align_bytes=64) for h in range(2)]
@@ -96,18 +86,18 @@ def tile_picked_sigattn_sigmoid_p_kernel(
                 d_picked[h][:].rearrange("p (c i t) -> p c t i", t=PACK, i=RUN),
             )
 
-        queries = [keep.tile([P, CHUNK], U32, name="queries0", align_bytes=64)]
-        queries.append(late.tile([P, CHUNK], U32, name="queries1", align_bytes=64, offset=9152))
-        queries.append(late.tile([P, HALF], U32, name="queries2", align_bytes=64, offset=10560))
+        queries = [
+            keep.tile([P, HALF], U32, name="queries0", align_bytes=64),
+            late.tile([P, HALF], U32, name="queries1", align_bytes=64, offset=10560),
+        ]
         key_scales = keep.tile([P, H], U8, name="key_scales", align_bytes=64)
-        nc.vector.tensor_copy(queries[0][:], x_table[:].indirect(offs_sb[:, 0:8]))
+        nc.vector.tensor_copy(queries[0][:], x_table[:].indirect(offs_sb[:, 0:16]))
         for tiles in (slice(0, 1), slice(1, PACK)):
             nc.vector.tensor_copy(
                 key_scales[:].rearrange("p (t m) -> p m t", t=PACK)[:, :, tiles],
                 rows[:, 0:H].rearrange("p (m t) -> p m t", t=PACK)[:, :, tiles],
             )
-        nc.vector.tensor_copy(queries[1][:], x_table[:].indirect(offs_sb[:, 8:16]))
-        nc.vector.tensor_copy(queries[2][:], x_table[:].indirect(offs_sb[:, 16:32]))
+        nc.vector.tensor_copy(queries[1][:], x_table[:].indirect(offs_sb[:, 16:32]))
 
         sig = {
             0: late.tile([P, PACK, CHUNK], F32, name="sig0", align_bytes=64, offset=12544),
@@ -116,7 +106,7 @@ def tile_picked_sigattn_sigmoid_p_kernel(
         }
 
         def scores(lo, width):
-            moving = queries[lo // CHUNK][:]
+            moving = queries[lo // HALF][:, lo % HALF : lo % HALF + width]
             for t in range(PACK):
                 bank = psum.tile([P, width], F32, name="score", tag="bank", bufs=BANKS)
                 nc.tensor.matmul_mx(
@@ -128,10 +118,10 @@ def tile_picked_sigattn_sigmoid_p_kernel(
                     start=True,
                     stop=True,
                 )
-                nc.scalar.activation(sig[lo][:, t, :], bank[:], SIGMOID, bias=key_cols[:, 0, t : t + 1], scale=0.0625)
+                nc.scalar.activation(sig[lo][:, t, :], bank[:], SIGMOID, bias=kb_sb[:, t : t + 1], scale=0.0625)
 
         z_first = keep.tile([P, HALF * PACK], BF16, name="z_first", align_bytes=64)
-        z_second = keep.tile([P, HALF * PACK], BF16, name="z_second", align_bytes=64)
+        z_second = late.tile([P, HALF * PACK], BF16, name="z_second", align_bytes=64, offset=14592)
         w_codes = keep.tile([P, N], U32, name="w_codes", align_bytes=64)
         w_scales = keep.tile([P, N], U8, name="w_scales", align_bytes=64)
         z_codes = keep.tile([P, S], U32, name="z_codes", align_bytes=64)
@@ -150,11 +140,11 @@ def tile_picked_sigattn_sigmoid_p_kernel(
             nc.vector.tensor_tensor(
                 z[:, o * PACK : (o + width) * PACK].rearrange("p (c i t) -> p c t i", i=RUN, t=PACK),
                 sig[min(lo, HALF)][:, :, h * o : h * o + width].rearrange("p t (c i) -> p c t i", i=RUN),
-                key_cols[:, 1, :].unsqueeze(1).unsqueeze(3).broadcast_to([P, width // RUN, PACK, RUN]),
+                gn_sb[:].unsqueeze(1).unsqueeze(3).broadcast_to([P, width // RUN, PACK, RUN]),
                 MULT,
             )
 
-        def finish(lo, width, first, count, copy):
+        def finish(lo, width, first, count, copy, offset=None):
             cols = slice(lo, lo + width)
             bank = psum.tile([P, count, width], F32, name="acc", tag="bank", bufs=BANKS)
             for u in range(count):
@@ -168,7 +158,8 @@ def tile_picked_sigattn_sigmoid_p_kernel(
                     start=True,
                     stop=True,
                 )
-            res = keep.tile([P, count, width], F32, name="res%d_%d" % (lo, first), align_bytes=64)
+            pool = keep if offset is None else late
+            res = pool.tile([P, count, width], F32, name="res%d_%d" % (lo, first), align_bytes=64, offset=offset)
             copy(res[:], bank[:])
             nc.sync.dma_start(out[first * P : (first + count) * P, cols].rearrange("(a p) c -> p a c", p=P), res[:])
 
@@ -199,9 +190,11 @@ def tile_picked_sigattn_sigmoid_p_kernel(
         quantise(z_codes, z_scales, HALF, CHUNK, z_second[:, 0 : CHUNK * PACK])
         for a in range(2, 4):
             finish(0, HALF, a, 1, nc.scalar.copy)
-        weigh(HALF + CHUNK, CHUNK)
-        finish(HALF, CHUNK, 0, 2, nc.vector.tensor_copy)
-        finish(HALF, CHUNK, 2, 2, nc.scalar.copy)
-        quantise(z_codes, z_scales, HALF + CHUNK, CHUNK, z_second[:, CHUNK * PACK : HALF * PACK])
+        for o in (CHUNK, CHUNK + CHUNK // 2):
+            weigh(HALF + o, CHUNK // 2)
+        for o in (CHUNK, CHUNK + CHUNK // 2):
+            quantise(z_codes, z_scales, HALF + o, CHUNK // 2, z_second[:, o * PACK : (o + CHUNK // 2) * PACK])
+        finish(HALF, CHUNK, 0, 2, nc.scalar.copy)
+        finish(HALF, CHUNK, 2, 2, nc.vector.tensor_copy, 14592 + 1024)
         finish(HALF + CHUNK, CHUNK, 0, 2, nc.scalar.copy)
         finish(HALF + CHUNK, CHUNK, 2, 2, nc.vector.tensor_copy)

@@ -121,7 +121,7 @@ def tile_picked_sigattn_sigmoid_p_kernel(
                 nc.scalar.activation(sig[lo][:, t, :], bank[:], SIGMOID, bias=kb_sb[:, t : t + 1], scale=0.0625)
 
         z_first = keep.tile([P, HALF * PACK], BF16, name="z_first", align_bytes=64)
-        z_second = late.tile([P, HALF * PACK], BF16, name="z_second", align_bytes=64, offset=14592)
+        z_second = keep.tile([P, HALF * PACK], BF16, name="z_second", align_bytes=64)
         w_codes = keep.tile([P, N], U32, name="w_codes", align_bytes=64)
         w_scales = keep.tile([P, N], U8, name="w_scales", align_bytes=64)
         z_codes = keep.tile([P, S], U32, name="z_codes", align_bytes=64)
@@ -144,24 +144,26 @@ def tile_picked_sigattn_sigmoid_p_kernel(
                 MULT,
             )
 
-        def finish(lo, width, first, count, copy, offset=None):
+        def product(a, lo, width):
             cols = slice(lo, lo + width)
-            bank = psum.tile([P, count, width], F32, name="acc", tag="bank", bufs=BANKS)
-            for u in range(count):
-                a = first + u
-                nc.tensor.matmul_mx(
-                    out=bank[:, u, :],
-                    lhsT=w_codes[:, a * P : (a + 1) * P].bitcast(FP8X4),
-                    lhsT_scale=w_scales[:, a * P : (a + 1) * P],
-                    rhs=z_codes[:, cols].bitcast(FP8X4),
-                    rhs_scale=z_scales[:, cols],
-                    start=True,
-                    stop=True,
-                )
-            pool = keep if offset is None else late
-            res = pool.tile([P, count, width], F32, name="res%d_%d" % (lo, first), align_bytes=64, offset=offset)
-            copy(res[:], bank[:])
-            nc.sync.dma_start(out[first * P : (first + count) * P, cols].rearrange("(a p) c -> p a c", p=P), res[:])
+            bank = psum.tile([P, width], F32, name="acc", tag="bank", bufs=BANKS)
+            nc.tensor.matmul_mx(
+                out=bank[:],
+                lhsT=w_codes[:, a * P : (a + 1) * P].bitcast(FP8X4),
+                lhsT_scale=w_scales[:, a * P : (a + 1) * P],
+                rhs=z_codes[:, cols].bitcast(FP8X4),
+                rhs_scale=z_scales[:, cols],
+                start=True,
+                stop=True,
+            )
+            return bank
+
+        def finish(lo, a, banks, copy):
+            res = keep.tile([P, HALF], F32, name="res%d_%d" % (lo, a), align_bytes=64)
+            width = HALF // len(banks)
+            for u, bank in enumerate(banks):
+                copy(res[:, u * width : (u + 1) * width], bank[:])
+            nc.sync.dma_start(out[a * P : (a + 1) * P, lo : lo + HALF], res[:])
 
         w_cast = [
             keep.tile([P, P * PACK], BF16, name="w_cast0", align_bytes=64),
@@ -182,19 +184,18 @@ def tile_picked_sigattn_sigmoid_p_kernel(
         weigh(CHUNK, CHUNK)
         cast(w_cast[2], 2, nc.vector.tensor_copy)
         quantise(z_codes, z_scales, 0, HALF, z_first[:])
-        for a in range(2):
-            finish(0, HALF, a, 1, nc.scalar.copy)
+        quantise(w_codes, w_scales, 2 * P, P, w_cast[2][:])
+        for a in range(3):
+            finish(0, a, [product(a, 0, HALF)], nc.scalar.copy)
         weigh(HALF, CHUNK)
-        for a in range(2, 4):
-            quantise(w_codes, w_scales, a * P, P, w_cast[a][:])
-        quantise(z_codes, z_scales, HALF, CHUNK, z_second[:, 0 : CHUNK * PACK])
-        for a in range(2, 4):
-            finish(0, HALF, a, 1, nc.scalar.copy)
-        for o in (CHUNK, CHUNK + CHUNK // 2):
-            weigh(HALF + o, CHUNK // 2)
-        for o in (CHUNK, CHUNK + CHUNK // 2):
-            quantise(z_codes, z_scales, HALF + o, CHUNK // 2, z_second[:, o * PACK : (o + CHUNK // 2) * PACK])
-        finish(HALF, CHUNK, 0, 2, nc.scalar.copy)
-        finish(HALF, CHUNK, 2, 2, nc.vector.tensor_copy, 14592 + 1024)
-        finish(HALF + CHUNK, CHUNK, 0, 2, nc.scalar.copy)
-        finish(HALF + CHUNK, CHUNK, 2, 2, nc.vector.tensor_copy)
+        quantise(w_codes, w_scales, 3 * P, P, w_cast[3][:])
+        finish(0, 3, [product(3, 0, HALF)], nc.scalar.copy)
+        weigh(HALF + CHUNK, CHUNK)
+        banks = {}
+        for o in (0, CHUNK):
+            quantise(z_codes, z_scales, HALF + o, CHUNK, z_second[:, o * PACK : (o + CHUNK) * PACK])
+            for a in range(2):
+                banks[a, o] = product(a, HALF + o, CHUNK)
+        for a in range(4):
+            parts = [banks[a, 0], banks[a, CHUNK]] if a < 2 else [product(a, HALF, HALF)]
+            finish(HALF, a, parts, nc.scalar.copy if a % 2 else nc.vector.tensor_copy)

@@ -1,6 +1,7 @@
 from contextlib import ExitStack
 
 import concourse.mybir as mybir
+from concourse.masks import make_identity
 
 K, T, S, N, G, H = 512, 2048, 512, 512, 2048, 512
 FLOPS = 2 * K * H * S + 2 * H * N * S
@@ -14,6 +15,7 @@ U8 = mybir.dt.uint8
 FP8X4 = mybir.dt.float8_e4m3fn_x4
 SIGMOID = mybir.ActivationFunctionType.Sigmoid
 MULT = mybir.AluOpType.mult
+ADD = mybir.AluOpType.add
 
 P = 128
 PACK = 4
@@ -22,7 +24,7 @@ CHUNK = 128
 HALF = 256
 LEAD = 448
 MID = 960
-BANKS = 8
+BANKS = 7
 
 
 def tile_picked_sigattn_sigmoid_p_kernel(
@@ -37,17 +39,22 @@ def tile_picked_sigattn_sigmoid_p_kernel(
         kidx_sb = keep.tile([P, H // 16], U16, name="kidx_sb")
         offs_sb = keep.tile([P, S // 16], U16, name="offs_sb")
         d_table = keep.tile([P, G], U32, name="d_table", align_bytes=64)
-        x_table = keep.tile([P, T], U32, name="x_table", align_bytes=64)
+        x_table = late.tile([P, T], U32, name="x_table", align_bytes=64, offset=12544)
         d_scale_table = keep.tile([P, G], U8, name="d_scale_table", align_bytes=64)
         x_scale_table = late.tile([P, T], U8, name="x_scale_table", align_bytes=64, offset=4032)
         rows = keep.tile([P, H + S], U8, name="rows", align_bytes=64)
+        gn_row = keep.tile([P, H], F32, name="gn_row", align_bytes=64)
+        identity = keep.tile([P, P], F32, name="identity", align_bytes=64)
         warm_in = keep.tile([P, 8], F32, name="warm_in")
         warm_out = keep.tile([P, 8], F32, name="warm_out")
 
         nc.vector.memset(d_scale_table[:].bitcast(I32), 0)
         nc.vector.memset(x_scale_table[:].bitcast(I32), 0)
         nc.vector.memset(warm_in[:], 0.0)
+        nc.vector.memset(gn_row[:], 0.0)
         nc.vector.memset(rows[:].bitcast(I32), 0)
+        nc.vector.memset(identity[:], 0.0)
+        make_identity(nc, identity[:], nomemset=True)
 
         d_src = d_words[0].rearrange("p c r -> p (c r)").bitcast(I32)
         nc.sync.dma_start(d_table[:, 0:LEAD].bitcast(I32), d_src[:, 0:LEAD])
@@ -57,8 +64,13 @@ def tile_picked_sigattn_sigmoid_p_kernel(
         nc.sync.dma_start(offs_sb[:], offs)
         nc.sync.dma_start(x_scale_table[0:P:8, :].bitcast(I32), x_scales[0].bitcast(I32))
         nc.sync.dma_start(d_table[:, MID:G].bitcast(I32), d_src[:, MID:G])
+        nc.sync.dma_start(gn_row[0:1, :], gn.rearrange("h o -> o h"))
         nc.sync.dma_start(x_table[:].bitcast(I32), x_words[0].rearrange("p c r -> p (c r)").bitcast(I32))
         nc.scalar.activation(warm_out[:], warm_in[:], SIGMOID)
+
+        gn_bank = psum.tile([P, P + PACK], F32, name="gn_bank")
+        for t in range(PACK):
+            nc.tensor.transpose(gn_bank[:, t : t + P], gn_row[:, t:H:PACK], identity[:])
 
         picked = late.tile([P, H + S], U8, name="picked", align_bytes=64, offset=9600)
         nc.vector.tensor_copy(picked[:, 0:H], d_scale_table[:].indirect(kidx_sb[:]))
@@ -70,10 +82,8 @@ def tile_picked_sigattn_sigmoid_p_kernel(
         w_rows = w1.rearrange("(p j) m -> p j m", j=PACK)
         w_raw = [late.tile([P, PACK, HALF], F32, name="w_raw%d" % h, align_bytes=64, offset=4160 * h) for h in range(2)]
         kb_sb = late.tile([P, PACK], F32, name="kb_sb", align_bytes=32, offset=4096)
-        gn_sb = late.tile([P, PACK], F32, name="gn_sb", align_bytes=32, offset=4128)
-        nc.sync.dma_start(w_raw[0][:], w_rows[:, :, 0:HALF])
         nc.sync.dma_start(kb_sb[:], kb.rearrange("(p t) o -> p (t o)", t=PACK))
-        nc.sync.dma_start(gn_sb[:], gn.rearrange("(p t) o -> p (t o)", t=PACK))
+        nc.sync.dma_start(w_raw[0][:], w_rows[:, :, 0:HALF])
         nc.sync.dma_start(w_raw[1][:], w_rows[:, :, HALF:N])
 
         keys = keep.tile([P, H], U32, name="keys", align_bytes=64)
@@ -86,34 +96,39 @@ def tile_picked_sigattn_sigmoid_p_kernel(
                 d_picked[h][:].rearrange("p (c i t) -> p c t i", t=PACK, i=RUN),
             )
 
-        queries = [
-            keep.tile([P, HALF], U32, name="queries0", align_bytes=64),
-            late.tile([P, HALF], U32, name="queries1", align_bytes=64, offset=10560),
-        ]
+        queries = {
+            0: keep.tile([P, CHUNK], U32, name="queries0", align_bytes=64),
+            CHUNK: late.tile([P, CHUNK], U32, name="queries1", align_bytes=64, offset=9600),
+            HALF: late.tile([P, HALF], U32, name="queries2", align_bytes=64, offset=10560),
+        }
+
+        def gather_queries(lo, width):
+            nc.vector.tensor_copy(queries[lo][:], x_table[:].indirect(offs_sb[:, lo // 16 : (lo + width) // 16]))
+
         key_scales = keep.tile([P, H], U8, name="key_scales", align_bytes=64)
-        nc.vector.tensor_copy(queries[0][:], x_table[:].indirect(offs_sb[:, 0:16]))
+        gather_queries(0, CHUNK)
         for tiles in (slice(0, 1), slice(1, PACK)):
             nc.vector.tensor_copy(
                 key_scales[:].rearrange("p (t m) -> p m t", t=PACK)[:, :, tiles],
                 rows[:, 0:H].rearrange("p (m t) -> p m t", t=PACK)[:, :, tiles],
             )
-        nc.vector.tensor_copy(queries[1][:], x_table[:].indirect(offs_sb[:, 16:32]))
+        gather_queries(CHUNK, CHUNK)
+        gather_queries(HALF, HALF)
 
         sig = {
-            0: late.tile([P, PACK, CHUNK], F32, name="sig0", align_bytes=64, offset=12544),
+            0: late.tile([P, PACK, CHUNK], F32, name="sig0", align_bytes=64, offset=24576),
             CHUNK: keep.tile([P, PACK, CHUNK], F32, name="sig1", align_bytes=64),
             HALF: keep.tile([P, PACK, HALF], F32, name="sig2", align_bytes=64),
         }
 
         def scores(lo, width):
-            moving = queries[lo // HALF][:, lo % HALF : lo % HALF + width]
             for t in range(PACK):
                 bank = psum.tile([P, width], F32, name="score", tag="bank", bufs=BANKS)
                 nc.tensor.matmul_mx(
                     out=bank[:],
                     lhsT=keys[:, t * P : (t + 1) * P].bitcast(FP8X4),
                     lhsT_scale=key_scales[:, t * P : (t + 1) * P],
-                    rhs=moving.bitcast(FP8X4),
+                    rhs=queries[lo][:].bitcast(FP8X4),
                     rhs_scale=rows[:, H + lo : H + lo + width],
                     start=True,
                     stop=True,
@@ -123,13 +138,24 @@ def tile_picked_sigattn_sigmoid_p_kernel(
         z_first = keep.tile([P, HALF * PACK], BF16, name="z_first", align_bytes=64)
         z_second = keep.tile([P, HALF * PACK], BF16, name="z_second", align_bytes=64)
         w_codes = keep.tile([P, N], U32, name="w_codes", align_bytes=64)
-        w_scales = keep.tile([P, N], U8, name="w_scales", align_bytes=64)
+        w_scales = late.tile([P, N], U8, name="w_scales", align_bytes=64, offset=24576)
         z_codes = keep.tile([P, S], U32, name="z_codes", align_bytes=64)
         z_scales = keep.tile([P, S], U8, name="z_scales", align_bytes=64)
 
         def cast(dst, a, copy):
             h, o = divmod(a * P, HALF)
             copy(dst[:].rearrange("p (c i j) -> p c j i", i=RUN, j=PACK), w_raw[h][:, :, o : o + P].rearrange("p j (c i) -> p c j i", i=RUN))
+
+        def pool_cast(dst, a):
+            h, o = divmod(a * P, HALF)
+            nc.gpsimd.tensor_scalar(
+                dst[:].rearrange("p (m j) -> p m j", j=PACK),
+                w_raw[h][:, :, o : o + P].rearrange("p j m -> p m j"),
+                1.0,
+                0.0,
+                MULT,
+                ADD,
+            )
 
         def quantise(codes, scales, lo, width, src):
             nc.vector.quantize_mx(out=codes[:, lo : lo + width].bitcast(FP8X4), scales=scales[:, lo : lo + width], in_=src)
@@ -140,7 +166,7 @@ def tile_picked_sigattn_sigmoid_p_kernel(
             nc.vector.tensor_tensor(
                 z[:, o * PACK : (o + width) * PACK].rearrange("p (c i t) -> p c t i", i=RUN, t=PACK),
                 sig[min(lo, HALF)][:, :, h * o : h * o + width].rearrange("p t (c i) -> p c t i", i=RUN),
-                gn_sb[:].unsqueeze(1).unsqueeze(3).broadcast_to([P, width // RUN, PACK, RUN]),
+                gn_bank[:, 0:PACK].unsqueeze(1).unsqueeze(3).broadcast_to([P, width // RUN, PACK, RUN]),
                 MULT,
             )
 
@@ -167,30 +193,31 @@ def tile_picked_sigattn_sigmoid_p_kernel(
 
         w_cast = [
             keep.tile([P, P * PACK], BF16, name="w_cast0", align_bytes=64),
-            keep.tile([P, P * PACK], BF16, name="w_cast1", align_bytes=64),
-            late.tile([P, P * PACK], BF16, name="w_cast2", align_bytes=64, offset=12544),
-            late.tile([P, P * PACK], BF16, name="w_cast3", align_bytes=64, offset=11520),
+            late.tile([P, P * PACK], BF16, name="w_cast1", align_bytes=64, offset=20672),
+            late.tile([P, P * PACK], BF16, name="w_cast2", align_bytes=64, offset=11520),
+            late.tile([P, P * PACK], BF16, name="w_cast3", align_bytes=64, offset=21632),
         ]
         scores(0, CHUNK)
         scores(CHUNK, CHUNK)
         scores(HALF, HALF)
-        cast(w_cast[3], 3, nc.scalar.copy)
+        cast(w_cast[2], 2, nc.scalar.copy)
 
-        for a in range(2):
-            cast(w_cast[a], a, nc.vector.tensor_copy)
-        for a in range(2):
-            quantise(w_codes, w_scales, a * P, P, w_cast[a][:])
+        cast(w_cast[0], 0, nc.vector.tensor_copy)
+        pool_cast(w_cast[1], 1)
         weigh(0, CHUNK)
         weigh(CHUNK, CHUNK)
-        cast(w_cast[2], 2, nc.vector.tensor_copy)
+        for a in range(2):
+            quantise(w_codes, w_scales, a * P, P, w_cast[a][:])
+        pool_cast(w_cast[3], 3)
         quantise(z_codes, z_scales, 0, HALF, z_first[:])
-        quantise(w_codes, w_scales, 2 * P, P, w_cast[2][:])
-        for a in range(3):
+        for a in range(2):
             finish(0, a, [product(a, 0, HALF)], nc.scalar.copy)
         weigh(HALF, CHUNK)
+        quantise(w_codes, w_scales, 2 * P, P, w_cast[2][:])
+        finish(0, 2, [product(2, 0, HALF)], nc.scalar.copy)
+        weigh(HALF + CHUNK, CHUNK)
         quantise(w_codes, w_scales, 3 * P, P, w_cast[3][:])
         finish(0, 3, [product(3, 0, HALF)], nc.scalar.copy)
-        weigh(HALF + CHUNK, CHUNK)
         banks = {}
         for o in (0, CHUNK):
             quantise(z_codes, z_scales, HALF + o, CHUNK, z_second[:, o * PACK : (o + CHUNK) * PACK])

@@ -40,10 +40,10 @@ def tile_picked_sigattn_sigmoid_p_kernel(
         offs_sb = keep.tile([P, S // 16], U16, name="offs_sb")
         d_table = keep.tile([P, G], U32, name="d_table", align_bytes=64)
         x_table = late.tile([P, T], U32, name="x_table", align_bytes=64, offset=12544)
-        d_scale_table = keep.tile([P, G], U8, name="d_scale_table", align_bytes=64)
-        x_scale_table = late.tile([P, T], U8, name="x_scale_table", align_bytes=64, offset=4032)
+        d_scale_table = late.tile([P, G], U8, name="d_scale_table", align_bytes=64, offset=4032)
+        x_scale_table = keep.tile([P, T], U8, name="x_scale_table", align_bytes=64)
         rows = keep.tile([P, H + S], U8, name="rows", align_bytes=64)
-        gn_row = keep.tile([P, H], F32, name="gn_row", align_bytes=64)
+        key_rows = keep.tile([P, H], F32, name="key_rows", align_bytes=64)
         identity = keep.tile([P, P], F32, name="identity", align_bytes=64)
         warm_in = keep.tile([P, 8], F32, name="warm_in")
         warm_out = keep.tile([P, 8], F32, name="warm_out")
@@ -51,38 +51,41 @@ def tile_picked_sigattn_sigmoid_p_kernel(
         nc.vector.memset(d_scale_table[:].bitcast(I32), 0)
         nc.vector.memset(x_scale_table[:].bitcast(I32), 0)
         nc.vector.memset(warm_in[:], 0.0)
-        nc.vector.memset(gn_row[:], 0.0)
+        nc.vector.memset(key_rows[:], 0.0)
         nc.vector.memset(rows[:].bitcast(I32), 0)
         nc.vector.memset(identity[:], 0.0)
         make_identity(nc, identity[:], nomemset=True)
 
         d_src = d_words[0].rearrange("p c r -> p (c r)").bitcast(I32)
-        nc.sync.dma_start(d_table[:, 0:LEAD].bitcast(I32), d_src[:, 0:LEAD])
         nc.sync.dma_start(kidx_sb[:], kidx)
+        nc.sync.dma_start(offs_sb[:], offs)
+        nc.sync.dma_start(d_table[:, 0:LEAD].bitcast(I32), d_src[:, 0:LEAD])
         nc.sync.dma_start(d_scale_table[0:P:8, :].bitcast(I32), d_scales[0].bitcast(I32))
         nc.sync.dma_start(d_table[:, LEAD:MID].bitcast(I32), d_src[:, LEAD:MID])
-        nc.sync.dma_start(offs_sb[:], offs)
         nc.sync.dma_start(x_scale_table[0:P:8, :].bitcast(I32), x_scales[0].bitcast(I32))
         nc.sync.dma_start(d_table[:, MID:G].bitcast(I32), d_src[:, MID:G])
-        nc.sync.dma_start(gn_row[0:1, :], gn.rearrange("h o -> o h"))
+        nc.sync.dma_start(key_rows[0:1, :], gn.rearrange("h o -> o h"))
+        nc.sync.dma_start(key_rows[1:2, :], kb.rearrange("h o -> o h"))
         nc.sync.dma_start(x_table[:].bitcast(I32), x_words[0].rearrange("p c r -> p (c r)").bitcast(I32))
         nc.scalar.activation(warm_out[:], warm_in[:], SIGMOID)
 
-        gn_bank = psum.tile([P, P + PACK], F32, name="gn_bank")
+        gn_bank = psum.tile([P, P + 2 * PACK], F32, name="gn_bank")
         for t in range(PACK):
-            nc.tensor.transpose(gn_bank[:, t : t + P], gn_row[:, t:H:PACK], identity[:])
+            nc.tensor.transpose(gn_bank[:, 2 * t : 2 * t + P], key_rows[:, t:H:PACK], identity[:])
+        kb_early = late.tile([P, PACK], F32, name="kb_early", align_bytes=64, offset=28672)
+        kb_last = keep.tile([P, PACK], F32, name="kb_last", align_bytes=64)
+        nc.scalar.copy(kb_early[:], gn_bank[:, 1 : 2 * PACK : 2])
+        nc.scalar.copy(kb_last[:], gn_bank[:, 1 : 2 * PACK : 2])
 
-        picked = late.tile([P, H + S], U8, name="picked", align_bytes=64, offset=9600)
+        picked = late.tile([P, H + HALF], U8, name="picked", align_bytes=64, offset=9856)
         nc.vector.tensor_copy(picked[:, 0:H], d_scale_table[:].indirect(kidx_sb[:]))
-        nc.vector.tensor_copy(picked[:, H : H + S], x_scale_table[:].indirect(offs_sb[:]))
+        nc.vector.tensor_copy(picked[:, H : H + HALF], x_scale_table[:].indirect(offs_sb[:, 0:16]))
         for r in range(4):
             queue = nc.scalar if r % 2 else nc.sync
-            queue.dma_start(rows[r:P:32, :].bitcast(I32), picked[8 * r : P : 32, :].bitcast(I32))
+            queue.dma_start(rows[r:P:32, 0 : H + HALF].bitcast(I32), picked[8 * r : P : 32, :].bitcast(I32))
 
         w_rows = w1.rearrange("(p j) m -> p j m", j=PACK)
         w_raw = [late.tile([P, PACK, HALF], F32, name="w_raw%d" % h, align_bytes=64, offset=4160 * h) for h in range(2)]
-        kb_sb = late.tile([P, PACK], F32, name="kb_sb", align_bytes=32, offset=4096)
-        nc.sync.dma_start(kb_sb[:], kb.rearrange("(p t) o -> p (t o)", t=PACK))
         nc.sync.dma_start(w_raw[0][:], w_rows[:, :, 0:HALF])
         nc.sync.dma_start(w_raw[1][:], w_rows[:, :, HALF:N])
 
@@ -96,9 +99,14 @@ def tile_picked_sigattn_sigmoid_p_kernel(
                 d_picked[h][:].rearrange("p (c i t) -> p c t i", t=PACK, i=RUN),
             )
 
+        picked_late = keep.tile([P, HALF], U8, name="picked_late", align_bytes=64)
+        nc.vector.tensor_copy(picked_late[:], x_scale_table[:].indirect(offs_sb[:, 16:32]))
+        for r in range(4):
+            nc.sync.dma_start(rows[r:P:32, H + HALF : H + S].bitcast(I32), picked_late[8 * r : P : 32, :].bitcast(I32))
+
         queries = {
             0: keep.tile([P, CHUNK], U32, name="queries0", align_bytes=64),
-            CHUNK: late.tile([P, CHUNK], U32, name="queries1", align_bytes=64, offset=9600),
+            CHUNK: late.tile([P, CHUNK], U32, name="queries1", align_bytes=64, offset=9856),
             HALF: late.tile([P, HALF], U32, name="queries2", align_bytes=64, offset=10560),
         }
 
@@ -118,24 +126,26 @@ def tile_picked_sigattn_sigmoid_p_kernel(
         sig = {
             0: late.tile([P, PACK, CHUNK], F32, name="sig0", align_bytes=64, offset=24576),
             CHUNK: keep.tile([P, PACK, CHUNK], F32, name="sig1", align_bytes=64),
-            HALF: keep.tile([P, PACK, HALF], F32, name="sig2", align_bytes=64),
+            HALF: keep.tile([P, PACK, CHUNK], F32, name="sig2", align_bytes=64),
+            HALF + CHUNK: keep.tile([P, PACK, CHUNK], F32, name="sig3", align_bytes=64),
         }
 
         def scores(lo, width):
+            kb_sb = kb_last if lo + width == S else kb_early
             for t in range(PACK):
                 bank = psum.tile([P, width], F32, name="score", tag="bank", bufs=BANKS)
                 nc.tensor.matmul_mx(
                     out=bank[:],
                     lhsT=keys[:, t * P : (t + 1) * P].bitcast(FP8X4),
                     lhsT_scale=key_scales[:, t * P : (t + 1) * P],
-                    rhs=queries[lo][:].bitcast(FP8X4),
+                    rhs=queries[min(lo, HALF)][:, lo - min(lo, HALF) : lo - min(lo, HALF) + width].bitcast(FP8X4),
                     rhs_scale=rows[:, H + lo : H + lo + width],
                     start=True,
                     stop=True,
                 )
                 nc.scalar.activation(sig[lo][:, t, :], bank[:], SIGMOID, bias=kb_sb[:, t : t + 1], scale=0.0625)
 
-        z_first = keep.tile([P, HALF * PACK], BF16, name="z_first", align_bytes=64)
+        z_first = late.tile([P, HALF * PACK], BF16, name="z_first", align_bytes=64, offset=26624)
         z_second = keep.tile([P, HALF * PACK], BF16, name="z_second", align_bytes=64)
         w_codes = keep.tile([P, N], U32, name="w_codes", align_bytes=64)
         w_scales = late.tile([P, N], U8, name="w_scales", align_bytes=64, offset=24576)
@@ -146,11 +156,11 @@ def tile_picked_sigattn_sigmoid_p_kernel(
             h, o = divmod(a * P, HALF)
             copy(dst[:].rearrange("p (c i j) -> p c j i", i=RUN, j=PACK), w_raw[h][:, :, o : o + P].rearrange("p j (c i) -> p c j i", i=RUN))
 
-        def pool_cast(dst, a):
-            h, o = divmod(a * P, HALF)
+        def pool_cast(dst, lo, width):
+            h, o = divmod(lo, HALF)
             nc.gpsimd.tensor_scalar(
                 dst[:].rearrange("p (m j) -> p m j", j=PACK),
-                w_raw[h][:, :, o : o + P].rearrange("p j m -> p m j"),
+                w_raw[h][:, :, o : o + width].rearrange("p j m -> p m j"),
                 1.0,
                 0.0,
                 MULT,
@@ -165,8 +175,8 @@ def tile_picked_sigattn_sigmoid_p_kernel(
             z = z_second if h else z_first
             nc.vector.tensor_tensor(
                 z[:, o * PACK : (o + width) * PACK].rearrange("p (c i t) -> p c t i", i=RUN, t=PACK),
-                sig[min(lo, HALF)][:, :, h * o : h * o + width].rearrange("p t (c i) -> p c t i", i=RUN),
-                gn_bank[:, 0:PACK].unsqueeze(1).unsqueeze(3).broadcast_to([P, width // RUN, PACK, RUN]),
+                sig[lo][:].rearrange("p t (c i) -> p c t i", i=RUN),
+                gn_bank[:, 0 : 2 * PACK : 2].unsqueeze(1).unsqueeze(3).broadcast_to([P, width // RUN, PACK, RUN]),
                 MULT,
             )
 
@@ -194,30 +204,35 @@ def tile_picked_sigattn_sigmoid_p_kernel(
         w_cast = [
             keep.tile([P, P * PACK], BF16, name="w_cast0", align_bytes=64),
             late.tile([P, P * PACK], BF16, name="w_cast1", align_bytes=64, offset=20672),
-            late.tile([P, P * PACK], BF16, name="w_cast2", align_bytes=64, offset=11520),
-            late.tile([P, P * PACK], BF16, name="w_cast3", align_bytes=64, offset=21632),
+            late.tile([P, P * PACK], BF16, name="w_cast2", align_bytes=64, offset=8896),
+        ]
+        w_last = [
+            keep.tile([P, 64 * PACK], BF16, name="w_last0", align_bytes=64),
+            late.tile([P, 64 * PACK], BF16, name="w_last1", align_bytes=64, offset=28416),
         ]
         scores(0, CHUNK)
         scores(CHUNK, CHUNK)
-        scores(HALF, HALF)
         cast(w_cast[2], 2, nc.scalar.copy)
+        scores(HALF, CHUNK)
+        scores(HALF + CHUNK, CHUNK)
 
         cast(w_cast[0], 0, nc.vector.tensor_copy)
-        pool_cast(w_cast[1], 1)
+        pool_cast(w_cast[1], P, P)
+        pool_cast(w_last[0], 3 * P, 64)
         weigh(0, CHUNK)
         weigh(CHUNK, CHUNK)
-        for a in range(2):
-            quantise(w_codes, w_scales, a * P, P, w_cast[a][:])
-        pool_cast(w_cast[3], 3)
+        quantise(w_codes, w_scales, 0, P, w_cast[0][:])
+        quantise(w_codes, w_scales, P, P, w_cast[1][:])
         quantise(z_codes, z_scales, 0, HALF, z_first[:])
-        for a in range(2):
+        pool_cast(w_last[1], 3 * P + 64, 64)
+        quantise(w_codes, w_scales, 2 * P, P, w_cast[2][:])
+        for a in range(3):
             finish(0, a, [product(a, 0, HALF)], nc.scalar.copy)
         weigh(HALF, CHUNK)
-        quantise(w_codes, w_scales, 2 * P, P, w_cast[2][:])
-        finish(0, 2, [product(2, 0, HALF)], nc.scalar.copy)
-        weigh(HALF + CHUNK, CHUNK)
-        quantise(w_codes, w_scales, 3 * P, P, w_cast[3][:])
+        for u in range(2):
+            quantise(w_codes, w_scales, 3 * P + 64 * u, 64, w_last[u][:])
         finish(0, 3, [product(3, 0, HALF)], nc.scalar.copy)
+        weigh(HALF + CHUNK, CHUNK)
         banks = {}
         for o in (0, CHUNK):
             quantise(z_codes, z_scales, HALF + o, CHUNK, z_second[:, o * PACK : (o + CHUNK) * PACK])

@@ -73,7 +73,7 @@ def tile_picked_sigattn_sigmoid_p_kernel(
         for t in range(PACK):
             nc.tensor.transpose(gn_bank[:, 2 * t : 2 * t + P], key_rows[:, t:H:PACK], identity[:])
         kb_early = late.tile([P, PACK], F32, name="kb_early", align_bytes=64, offset=28672)
-        kb_last = keep.tile([P, PACK], F32, name="kb_last", align_bytes=64)
+        kb_last = late.tile([P, PACK], F32, name="kb_last", align_bytes=64, offset=29696)
         nc.scalar.copy(kb_early[:], gn_bank[:, 1 : 2 * PACK : 2])
         nc.scalar.copy(kb_last[:], gn_bank[:, 1 : 2 * PACK : 2])
 
@@ -150,7 +150,10 @@ def tile_picked_sigattn_sigmoid_p_kernel(
         w_codes = keep.tile([P, N], U32, name="w_codes", align_bytes=64)
         w_scales = late.tile([P, N], U8, name="w_scales", align_bytes=64, offset=24576)
         z_codes = keep.tile([P, S], U32, name="z_codes", align_bytes=64)
-        z_scales = keep.tile([P, S], U8, name="z_scales", align_bytes=64)
+        z_scales = [
+            keep.tile([P, HALF], U8, name="z_scales0", align_bytes=64),
+            late.tile([P, HALF], U8, name="z_scales1", align_bytes=64, offset=29696),
+        ]
 
         def cast(dst, a, copy):
             h, o = divmod(a * P, HALF)
@@ -159,7 +162,7 @@ def tile_picked_sigattn_sigmoid_p_kernel(
         def pool_cast(dst, lo, width):
             h, o = divmod(lo, HALF)
             nc.gpsimd.tensor_scalar(
-                dst[:].rearrange("p (m j) -> p m j", j=PACK),
+                dst.rearrange("p (m j) -> p m j", j=PACK),
                 w_raw[h][:, :, o : o + width].rearrange("p j m -> p m j"),
                 1.0,
                 0.0,
@@ -169,6 +172,10 @@ def tile_picked_sigattn_sigmoid_p_kernel(
 
         def quantise(codes, scales, lo, width, src):
             nc.vector.quantize_mx(out=codes[:, lo : lo + width].bitcast(FP8X4), scales=scales[:, lo : lo + width], in_=src)
+
+        def quantise_z(lo, width, src):
+            h, o = divmod(lo, HALF)
+            nc.vector.quantize_mx(out=z_codes[:, lo : lo + width].bitcast(FP8X4), scales=z_scales[h][:, o : o + width], in_=src)
 
         def weigh(lo, width):
             h, o = divmod(lo, HALF)
@@ -188,7 +195,7 @@ def tile_picked_sigattn_sigmoid_p_kernel(
                 lhsT=w_codes[:, a * P : (a + 1) * P].bitcast(FP8X4),
                 lhsT_scale=w_scales[:, a * P : (a + 1) * P],
                 rhs=z_codes[:, cols].bitcast(FP8X4),
-                rhs_scale=z_scales[:, cols],
+                rhs_scale=z_scales[lo // HALF][:, lo % HALF : lo % HALF + width],
                 start=True,
                 stop=True,
             )
@@ -206,10 +213,7 @@ def tile_picked_sigattn_sigmoid_p_kernel(
             late.tile([P, P * PACK], BF16, name="w_cast1", align_bytes=64, offset=20672),
             late.tile([P, P * PACK], BF16, name="w_cast2", align_bytes=64, offset=8896),
         ]
-        w_last = [
-            keep.tile([P, 64 * PACK], BF16, name="w_last0", align_bytes=64),
-            late.tile([P, 64 * PACK], BF16, name="w_last1", align_bytes=64, offset=28416),
-        ]
+        w_last = late.tile([P, P * PACK], BF16, name="w_last", align_bytes=64, offset=28416)
         scores(0, CHUNK)
         scores(CHUNK, CHUNK)
         cast(w_cast[2], 2, nc.scalar.copy)
@@ -217,25 +221,27 @@ def tile_picked_sigattn_sigmoid_p_kernel(
         scores(HALF + CHUNK, CHUNK)
 
         cast(w_cast[0], 0, nc.vector.tensor_copy)
-        pool_cast(w_cast[1], P, P)
-        pool_cast(w_last[0], 3 * P, 64)
+        pool_cast(w_cast[1][:], P, P)
         weigh(0, CHUNK)
         weigh(CHUNK, CHUNK)
         quantise(w_codes, w_scales, 0, P, w_cast[0][:])
         quantise(w_codes, w_scales, P, P, w_cast[1][:])
-        quantise(z_codes, z_scales, 0, HALF, z_first[:])
-        pool_cast(w_last[1], 3 * P + 64, 64)
+        quantise_z(0, HALF, z_first[:])
+        pool_cast(w_last[:, 64 * PACK :], 3 * P + 64, 64)
+        nc.scalar.copy(
+            w_last[:, 0 : 64 * PACK].rearrange("p (c i j) -> p c j i", i=RUN, j=PACK),
+            w_raw[1][:, :, P : P + 64].rearrange("p j (c i) -> p c j i", i=RUN),
+        )
         quantise(w_codes, w_scales, 2 * P, P, w_cast[2][:])
         for a in range(3):
             finish(0, a, [product(a, 0, HALF)], nc.scalar.copy)
         weigh(HALF, CHUNK)
-        for u in range(2):
-            quantise(w_codes, w_scales, 3 * P + 64 * u, 64, w_last[u][:])
-        finish(0, 3, [product(3, 0, HALF)], nc.scalar.copy)
         weigh(HALF + CHUNK, CHUNK)
+        quantise(w_codes, w_scales, 3 * P, P, w_last[:])
+        finish(0, 3, [product(3, 0, HALF)], nc.scalar.copy)
         banks = {}
         for o in (0, CHUNK):
-            quantise(z_codes, z_scales, HALF + o, CHUNK, z_second[:, o * PACK : (o + CHUNK) * PACK])
+            quantise_z(HALF + o, CHUNK, z_second[:, o * PACK : (o + CHUNK) * PACK])
             for a in range(2):
                 banks[a, o] = product(a, HALF + o, CHUNK)
         for a in range(4):

@@ -72,10 +72,10 @@ def tile_picked_sigattn_sigmoid_p_kernel(
         gn_bank = psum.tile([P, P + 2 * PACK], F32, name="gn_bank")
         for t in range(PACK):
             nc.tensor.transpose(gn_bank[:, 2 * t : 2 * t + P], key_rows[:, t:H:PACK], identity[:])
-        kb_early = late.tile([P, PACK], F32, name="kb_early", align_bytes=64, offset=28672)
-        kb_last = late.tile([P, PACK], F32, name="kb_last", align_bytes=64, offset=29696)
-        nc.scalar.copy(kb_early[:], gn_bank[:, 1 : 2 * PACK : 2])
-        nc.scalar.copy(kb_last[:], gn_bank[:, 1 : 2 * PACK : 2])
+        kb_sb = late.tile([P, PACK], F32, name="kb_sb", align_bytes=64, offset=28672)
+        kb_third = late.tile([P, PACK], F32, name="kb_third", align_bytes=64, offset=28992)
+        nc.scalar.copy(kb_sb[:], gn_bank[:, 1 : 2 * PACK : 2])
+        nc.scalar.copy(kb_third[:], gn_bank[:, 1 : 2 * PACK : 2])
 
         picked = late.tile([P, H + HALF], U8, name="picked", align_bytes=64, offset=9856)
         nc.vector.tensor_copy(picked[:, 0:H], d_scale_table[:].indirect(kidx_sb[:]))
@@ -130,8 +130,8 @@ def tile_picked_sigattn_sigmoid_p_kernel(
             HALF + CHUNK: keep.tile([P, PACK, CHUNK], F32, name="sig3", align_bytes=64),
         }
 
-        def scores(lo, width):
-            kb_sb = kb_last if lo + width == S else kb_early
+        def passes(lo, width):
+            banks = []
             for t in range(PACK):
                 bank = psum.tile([P, width], F32, name="score", tag="bank", bufs=BANKS)
                 nc.tensor.matmul_mx(
@@ -143,16 +143,26 @@ def tile_picked_sigattn_sigmoid_p_kernel(
                     start=True,
                     stop=True,
                 )
-                nc.scalar.activation(sig[lo][:, t, :], bank[:], SIGMOID, bias=kb_sb[:, t : t + 1], scale=0.0625)
+                banks.append(bank)
+            return banks
 
-        z_first = late.tile([P, HALF * PACK], BF16, name="z_first", align_bytes=64, offset=26624)
+        def sigmoids(lo, banks):
+            bias = kb_third if lo == HALF else kb_sb
+            for t in range(PACK):
+                nc.scalar.activation(sig[lo][:, t, :], banks[t][:], SIGMOID, bias=bias[:, t : t + 1], scale=0.0625)
+
+        def scores(lo, width):
+            sigmoids(lo, passes(lo, width))
+
+        z_first = keep.tile([P, HALF * PACK], BF16, name="z_first", align_bytes=64)
         z_second = keep.tile([P, HALF * PACK], BF16, name="z_second", align_bytes=64)
         w_codes = keep.tile([P, N], U32, name="w_codes", align_bytes=64)
-        w_scales = late.tile([P, N], U8, name="w_scales", align_bytes=64, offset=24576)
+        w_scales = late.tile([P, HALF], U8, name="w_scales", align_bytes=64, offset=24576)
+        last_scales = late.tile([P, 2 * P], U8, name="last_scales", align_bytes=64, offset=28992)
         z_codes = keep.tile([P, S], U32, name="z_codes", align_bytes=64)
         z_scales = [
             keep.tile([P, HALF], U8, name="z_scales0", align_bytes=64),
-            late.tile([P, HALF], U8, name="z_scales1", align_bytes=64, offset=29696),
+            late.tile([P, HALF], U8, name="z_scales1", align_bytes=64, offset=28672),
         ]
 
         def cast(dst, a, copy):
@@ -193,7 +203,7 @@ def tile_picked_sigattn_sigmoid_p_kernel(
             nc.tensor.matmul_mx(
                 out=bank[:],
                 lhsT=w_codes[:, a * P : (a + 1) * P].bitcast(FP8X4),
-                lhsT_scale=w_scales[:, a * P : (a + 1) * P],
+                lhsT_scale=w_scales[:, a * P : (a + 1) * P] if a < 2 else last_scales[:, (a - 2) * P : (a - 1) * P],
                 rhs=z_codes[:, cols].bitcast(FP8X4),
                 rhs_scale=z_scales[lo // HALF][:, lo % HALF : lo % HALF + width],
                 start=True,
@@ -211,34 +221,37 @@ def tile_picked_sigattn_sigmoid_p_kernel(
         w_cast = [
             keep.tile([P, P * PACK], BF16, name="w_cast0", align_bytes=64),
             late.tile([P, P * PACK], BF16, name="w_cast1", align_bytes=64, offset=20672),
-            late.tile([P, P * PACK], BF16, name="w_cast2", align_bytes=64, offset=8896),
+            keep.tile([P, P * PACK], BF16, name="w_cast2", align_bytes=64),
         ]
-        w_last = late.tile([P, P * PACK], BF16, name="w_last", align_bytes=64, offset=28416)
+        w_half = late.tile([P, 64 * PACK], BF16, name="w_half", align_bytes=64, offset=11520)
+        w_last = late.tile([P, 64 * PACK], BF16, name="w_last", align_bytes=64, offset=21632)
         scores(0, CHUNK)
         scores(CHUNK, CHUNK)
         cast(w_cast[2], 2, nc.scalar.copy)
         scores(HALF, CHUNK)
-        scores(HALF + CHUNK, CHUNK)
 
         cast(w_cast[0], 0, nc.vector.tensor_copy)
         pool_cast(w_cast[1][:], P, P)
         weigh(0, CHUNK)
         weigh(CHUNK, CHUNK)
-        quantise(w_codes, w_scales, 0, P, w_cast[0][:])
-        quantise(w_codes, w_scales, P, P, w_cast[1][:])
-        quantise_z(0, HALF, z_first[:])
-        pool_cast(w_last[:, 64 * PACK :], 3 * P + 64, 64)
+        for a in range(2):
+            quantise(w_codes, w_scales, a * P, P, w_cast[a][:])
+        pool_cast(w_last[:], 3 * P + 64, 64)
+        last = passes(HALF + CHUNK, CHUNK)
         nc.scalar.copy(
-            w_last[:, 0 : 64 * PACK].rearrange("p (c i j) -> p c j i", i=RUN, j=PACK),
+            w_half[:].rearrange("p (c i j) -> p c j i", i=RUN, j=PACK),
             w_raw[1][:, :, P : P + 64].rearrange("p j (c i) -> p c j i", i=RUN),
         )
-        quantise(w_codes, w_scales, 2 * P, P, w_cast[2][:])
-        for a in range(3):
-            finish(0, a, [product(a, 0, HALF)], nc.scalar.copy)
+        sigmoids(HALF + CHUNK, last)
+        quantise_z(0, HALF, z_first[:])
         weigh(HALF, CHUNK)
+        for lo, width, src in ((0, P, w_cast[2]), (P, 64, w_half), (P + 64, 64, w_last)):
+            nc.vector.quantize_mx(
+                out=w_codes[:, HALF + lo : HALF + lo + width].bitcast(FP8X4), scales=last_scales[:, lo : lo + width], in_=src[:]
+            )
         weigh(HALF + CHUNK, CHUNK)
-        quantise(w_codes, w_scales, 3 * P, P, w_last[:])
-        finish(0, 3, [product(3, 0, HALF)], nc.scalar.copy)
+        for a in range(4):
+            finish(0, a, [product(a, 0, HALF)], nc.scalar.copy)
         banks = {}
         for o in (0, CHUNK):
             quantise_z(HALF + o, CHUNK, z_second[:, o * PACK : (o + CHUNK) * PACK])

@@ -64,8 +64,8 @@ def tile_picked_sigattn_sigmoid_p_kernel(
         nc.sync.dma_start(d_table[:, LEAD:MID].bitcast(I32), d_src[:, LEAD:MID])
         nc.sync.dma_start(x_scale_table[0:P:8, :].bitcast(I32), x_scales[0].bitcast(I32))
         nc.sync.dma_start(d_table[:, MID:G].bitcast(I32), d_src[:, MID:G])
-        nc.sync.dma_start(key_rows[0:1, :], gn.rearrange("h o -> o h"))
-        nc.sync.dma_start(key_rows[1:2, :], kb.rearrange("h o -> o h"))
+        nc.scalar.dma_start(key_rows[0:1, :], gn.rearrange("h o -> o h"))
+        nc.scalar.dma_start(key_rows[1:2, :], kb.rearrange("h o -> o h"))
         nc.sync.dma_start(x_table[:].bitcast(I32), x_words[0].rearrange("p c r -> p (c r)").bitcast(I32))
         nc.scalar.activation(warm_out[:], warm_in[:], SIGMOID)
 

@@ -22,9 +22,12 @@ PACK = 4
 RUN = 4
 CHUNK = 128
 HALF = 256
+PIECE = 64
 LEAD = 448
 MID = 960
 BANKS = 7
+GN_ROW = P - 2
+KB_ROW = P - 1
 
 
 def tile_picked_sigattn_sigmoid_p_kernel(
@@ -39,24 +42,28 @@ def tile_picked_sigattn_sigmoid_p_kernel(
         kidx_sb = keep.tile([P, H // 16], U16, name="kidx_sb")
         offs_sb = keep.tile([P, S // 16], U16, name="offs_sb")
         d_table = keep.tile([P, G], U32, name="d_table", align_bytes=64)
-        x_table = late.tile([P, T], U32, name="x_table", align_bytes=64, offset=12544)
-        d_scale_table = late.tile([P, G], U8, name="d_scale_table", align_bytes=64, offset=4032)
-        x_scale_table = keep.tile([P, T], U8, name="x_scale_table", align_bytes=64)
+        x_table = keep.tile([P, T], U32, name="x_table", align_bytes=64)
+        d_scale_table = keep.tile([P, G], U8, name="d_scale_table", align_bytes=64)
+        x_scale_table = late.tile([P, T], U8, name="x_scale_table", align_bytes=64, offset=4032)
         rows = keep.tile([P, H + S], U8, name="rows", align_bytes=64)
         key_rows = keep.tile([P, H], F32, name="key_rows", align_bytes=64)
         identity = keep.tile([P, P], F32, name="identity", align_bytes=64)
+        unit = late.tile([P, 1], F32, name="unit", align_bytes=64, offset=16384)
         warm_in = keep.tile([P, 8], F32, name="warm_in")
         warm_out = keep.tile([P, 8], F32, name="warm_out")
 
         nc.vector.memset(d_scale_table[:].bitcast(I32), 0)
         nc.vector.memset(x_scale_table[:].bitcast(I32), 0)
         nc.vector.memset(warm_in[:], 0.0)
-        nc.vector.memset(key_rows[:], 0.0)
+        nc.vector.memset(key_rows[0:GN_ROW, :], 0.0)
         nc.vector.memset(rows[:].bitcast(I32), 0)
+        nc.vector.memset(unit[:], 1.0)
         nc.vector.memset(identity[:], 0.0)
         make_identity(nc, identity[:], nomemset=True)
 
         d_src = d_words[0].rearrange("p c r -> p (c r)").bitcast(I32)
+        nc.scalar.dma_start(key_rows[GN_ROW : GN_ROW + 1, :], gn.rearrange("h o -> o h"))
+        nc.scalar.dma_start(key_rows[KB_ROW : KB_ROW + 1, :], kb.rearrange("h o -> o h"))
         nc.sync.dma_start(kidx_sb[:], kidx)
         nc.sync.dma_start(offs_sb[:], offs)
         nc.sync.dma_start(d_table[:, 0:LEAD].bitcast(I32), d_src[:, 0:LEAD])
@@ -64,25 +71,26 @@ def tile_picked_sigattn_sigmoid_p_kernel(
         nc.sync.dma_start(d_table[:, LEAD:MID].bitcast(I32), d_src[:, LEAD:MID])
         nc.sync.dma_start(x_scale_table[0:P:8, :].bitcast(I32), x_scales[0].bitcast(I32))
         nc.sync.dma_start(d_table[:, MID:G].bitcast(I32), d_src[:, MID:G])
-        nc.scalar.dma_start(key_rows[0:1, :], gn.rearrange("h o -> o h"))
-        nc.scalar.dma_start(key_rows[1:2, :], kb.rearrange("h o -> o h"))
         nc.sync.dma_start(x_table[:].bitcast(I32), x_words[0].rearrange("p c r -> p (c r)").bitcast(I32))
         nc.scalar.activation(warm_out[:], warm_in[:], SIGMOID)
 
         gn_bank = psum.tile([P, P + 2 * PACK], F32, name="gn_bank")
-        for t in range(PACK):
+        for t in reversed(range(PACK)):
             nc.tensor.transpose(gn_bank[:, 2 * t : 2 * t + P], key_rows[:, t:H:PACK], identity[:])
         kb_sb = late.tile([P, PACK], F32, name="kb_sb", align_bytes=64, offset=28672)
-        kb_third = late.tile([P, PACK], F32, name="kb_third", align_bytes=64, offset=28992)
-        nc.scalar.copy(kb_sb[:], gn_bank[:, 1 : 2 * PACK : 2])
-        nc.scalar.copy(kb_third[:], gn_bank[:, 1 : 2 * PACK : 2])
+        kb_early = late.tile([P, PACK], F32, name="kb_early", align_bytes=64, offset=24576)
+        nc.scalar.copy(kb_early[:], gn_bank[:, KB_ROW : KB_ROW + 2 * PACK - 1 : 2])
+        nc.scalar.copy(kb_sb[:], gn_bank[:, KB_ROW : KB_ROW + 2 * PACK - 1 : 2])
 
-        picked = late.tile([P, H + HALF], U8, name="picked", align_bytes=64, offset=9856)
+        picked = late.tile([P, H + HALF], U8, name="picked", align_bytes=64, offset=10688)
+        picked_late = keep.tile([P, HALF], U8, name="picked_late", align_bytes=64)
         nc.vector.tensor_copy(picked[:, 0:H], d_scale_table[:].indirect(kidx_sb[:]))
         nc.vector.tensor_copy(picked[:, H : H + HALF], x_scale_table[:].indirect(offs_sb[:, 0:16]))
+        nc.vector.tensor_copy(picked_late[:], x_scale_table[:].indirect(offs_sb[:, 16:32]))
         for r in range(4):
-            queue = nc.scalar if r % 2 else nc.sync
-            queue.dma_start(rows[r:P:32, 0 : H + HALF].bitcast(I32), picked[8 * r : P : 32, :].bitcast(I32))
+            nc.scalar.dma_start(rows[r:P:32, 0 : H + HALF].bitcast(I32), picked[8 * r : P : 32, :].bitcast(I32))
+        for r in range(4):
+            nc.scalar.dma_start(rows[r:P:32, H + HALF : H + S].bitcast(I32), picked_late[8 * r : P : 32, :].bitcast(I32))
 
         w_rows = w1.rearrange("(p j) m -> p j m", j=PACK)
         w_raw = [late.tile([P, PACK, HALF], F32, name="w_raw%d" % h, align_bytes=64, offset=4160 * h) for h in range(2)]
@@ -99,47 +107,37 @@ def tile_picked_sigattn_sigmoid_p_kernel(
                 d_picked[h][:].rearrange("p (c i t) -> p c t i", t=PACK, i=RUN),
             )
 
-        picked_late = keep.tile([P, HALF], U8, name="picked_late", align_bytes=64)
-        nc.vector.tensor_copy(picked_late[:], x_scale_table[:].indirect(offs_sb[:, 16:32]))
-        for r in range(4):
-            nc.sync.dma_start(rows[r:P:32, H + HALF : H + S].bitcast(I32), picked_late[8 * r : P : 32, :].bitcast(I32))
-
+        key_scales = keep.tile([P, H], U8, name="key_scales", align_bytes=64)
+        nc.vector.tensor_copy(
+            key_scales[:].rearrange("p (t m) -> p m t", t=PACK),
+            rows[:, 0:H].rearrange("p (m t) -> p m t", t=PACK),
+        )
         queries = {
-            0: keep.tile([P, CHUNK], U32, name="queries0", align_bytes=64),
-            CHUNK: late.tile([P, CHUNK], U32, name="queries1", align_bytes=64, offset=9856),
-            HALF: late.tile([P, HALF], U32, name="queries2", align_bytes=64, offset=10560),
+            0: late.tile([P, CHUNK], U32, name="queries0", align_bytes=64, offset=10240),
+            CHUNK: late.tile([P, CHUNK], U32, name="queries1", align_bytes=64, offset=10752),
+            HALF: late.tile([P, HALF], U32, name="queries2", align_bytes=64, offset=11264),
         }
-
-        def gather_queries(lo, width):
+        for lo, width in ((0, CHUNK), (CHUNK, CHUNK), (HALF, HALF)):
             nc.vector.tensor_copy(queries[lo][:], x_table[:].indirect(offs_sb[:, lo // 16 : (lo + width) // 16]))
 
-        key_scales = keep.tile([P, H], U8, name="key_scales", align_bytes=64)
-        gather_queries(0, CHUNK)
-        for tiles in (slice(0, 1), slice(1, PACK)):
-            nc.vector.tensor_copy(
-                key_scales[:].rearrange("p (t m) -> p m t", t=PACK)[:, :, tiles],
-                rows[:, 0:H].rearrange("p (m t) -> p m t", t=PACK)[:, :, tiles],
-            )
-        gather_queries(CHUNK, CHUNK)
-        gather_queries(HALF, HALF)
-
         sig = {
-            0: late.tile([P, PACK, CHUNK], F32, name="sig0", align_bytes=64, offset=24576),
+            0: keep.tile([P, PACK, CHUNK], F32, name="sig0", align_bytes=64),
             CHUNK: keep.tile([P, PACK, CHUNK], F32, name="sig1", align_bytes=64),
             HALF: keep.tile([P, PACK, CHUNK], F32, name="sig2", align_bytes=64),
             HALF + CHUNK: keep.tile([P, PACK, CHUNK], F32, name="sig3", align_bytes=64),
         }
 
-        def passes(lo, width):
+        def passes(lo):
             banks = []
+            first = min(lo, HALF)
             for t in range(PACK):
-                bank = psum.tile([P, width], F32, name="score", tag="bank", bufs=BANKS)
+                bank = psum.tile([P, CHUNK], F32, name="score", tag="bank", bufs=BANKS)
                 nc.tensor.matmul_mx(
                     out=bank[:],
                     lhsT=keys[:, t * P : (t + 1) * P].bitcast(FP8X4),
                     lhsT_scale=key_scales[:, t * P : (t + 1) * P],
-                    rhs=queries[min(lo, HALF)][:, lo - min(lo, HALF) : lo - min(lo, HALF) + width].bitcast(FP8X4),
-                    rhs_scale=rows[:, H + lo : H + lo + width],
+                    rhs=queries[first][:, lo - first : lo - first + CHUNK].bitcast(FP8X4),
+                    rhs_scale=rows[:, H + lo : H + lo + CHUNK],
                     start=True,
                     stop=True,
                 )
@@ -147,27 +145,27 @@ def tile_picked_sigattn_sigmoid_p_kernel(
             return banks
 
         def sigmoids(lo, banks):
-            bias = kb_third if lo == HALF else kb_sb
+            bias = kb_early if lo < HALF else kb_sb
             for t in range(PACK):
                 nc.scalar.activation(sig[lo][:, t, :], banks[t][:], SIGMOID, bias=bias[:, t : t + 1], scale=0.0625)
-
-        def scores(lo, width):
-            sigmoids(lo, passes(lo, width))
 
         z_first = keep.tile([P, HALF * PACK], BF16, name="z_first", align_bytes=64)
         z_second = keep.tile([P, HALF * PACK], BF16, name="z_second", align_bytes=64)
         w_codes = keep.tile([P, N], U32, name="w_codes", align_bytes=64)
         w_scales = late.tile([P, HALF], U8, name="w_scales", align_bytes=64, offset=24576)
-        last_scales = late.tile([P, 2 * P], U8, name="last_scales", align_bytes=64, offset=28992)
+        last_scales = keep.tile([P, HALF], U8, name="last_scales", align_bytes=64)
         z_codes = keep.tile([P, S], U32, name="z_codes", align_bytes=64)
         z_scales = [
             keep.tile([P, HALF], U8, name="z_scales0", align_bytes=64),
             late.tile([P, HALF], U8, name="z_scales1", align_bytes=64, offset=28672),
         ]
 
-        def cast(dst, a, copy):
-            h, o = divmod(a * P, HALF)
-            copy(dst[:].rearrange("p (c i j) -> p c j i", i=RUN, j=PACK), w_raw[h][:, :, o : o + P].rearrange("p j (c i) -> p c j i", i=RUN))
+        def woven(dst, lo, width):
+            h, o = divmod(lo, HALF)
+            return (
+                dst.rearrange("p (c i j) -> p c j i", i=RUN, j=PACK),
+                w_raw[h][:, :, o : o + width].rearrange("p j (c i) -> p c j i", i=RUN),
+            )
 
         def pool_cast(dst, lo, width):
             h, o = divmod(lo, HALF)
@@ -180,31 +178,34 @@ def tile_picked_sigattn_sigmoid_p_kernel(
                 ADD,
             )
 
-        def quantise(codes, scales, lo, width, src):
-            nc.vector.quantize_mx(out=codes[:, lo : lo + width].bitcast(FP8X4), scales=scales[:, lo : lo + width], in_=src)
+        def quantise_w(a, src):
+            scales = w_scales if a < 2 else last_scales
+            nc.vector.quantize_mx(
+                out=w_codes[:, a * P : (a + 1) * P].bitcast(FP8X4), scales=scales[:, a % 2 * P : (a % 2 + 1) * P], in_=src[:]
+            )
 
         def quantise_z(lo, width, src):
             h, o = divmod(lo, HALF)
             nc.vector.quantize_mx(out=z_codes[:, lo : lo + width].bitcast(FP8X4), scales=z_scales[h][:, o : o + width], in_=src)
 
-        def weigh(lo, width):
+        def weigh(lo):
             h, o = divmod(lo, HALF)
             z = z_second if h else z_first
             nc.vector.tensor_tensor(
-                z[:, o * PACK : (o + width) * PACK].rearrange("p (c i t) -> p c t i", i=RUN, t=PACK),
+                z[:, o * PACK : (o + CHUNK) * PACK].rearrange("p (c i t) -> p c t i", i=RUN, t=PACK),
                 sig[lo][:].rearrange("p t (c i) -> p c t i", i=RUN),
-                gn_bank[:, 0 : 2 * PACK : 2].unsqueeze(1).unsqueeze(3).broadcast_to([P, width // RUN, PACK, RUN]),
+                gn_bank[:, GN_ROW : GN_ROW + 2 * PACK : 2].unsqueeze(1).unsqueeze(3).broadcast_to([P, CHUNK // RUN, PACK, RUN]),
                 MULT,
             )
 
         def product(a, lo, width):
-            cols = slice(lo, lo + width)
             bank = psum.tile([P, width], F32, name="acc", tag="bank", bufs=BANKS)
+            scales = w_scales if a < 2 else last_scales
             nc.tensor.matmul_mx(
                 out=bank[:],
                 lhsT=w_codes[:, a * P : (a + 1) * P].bitcast(FP8X4),
-                lhsT_scale=w_scales[:, a * P : (a + 1) * P] if a < 2 else last_scales[:, (a - 2) * P : (a - 1) * P],
-                rhs=z_codes[:, cols].bitcast(FP8X4),
+                lhsT_scale=scales[:, a % 2 * P : (a % 2 + 1) * P],
+                rhs=z_codes[:, lo : lo + width].bitcast(FP8X4),
                 rhs_scale=z_scales[lo // HALF][:, lo % HALF : lo % HALF + width],
                 start=True,
                 stop=True,
@@ -219,37 +220,32 @@ def tile_picked_sigattn_sigmoid_p_kernel(
             nc.sync.dma_start(out[a * P : (a + 1) * P, lo : lo + HALF], res[:])
 
         w_cast = [
-            keep.tile([P, P * PACK], BF16, name="w_cast0", align_bytes=64),
-            late.tile([P, P * PACK], BF16, name="w_cast1", align_bytes=64, offset=20672),
-            keep.tile([P, P * PACK], BF16, name="w_cast2", align_bytes=64),
+            late.tile([P, P * PACK], BF16, name="w_cast0", align_bytes=64, offset=9280),
+            late.tile([P, P * PACK], BF16, name="w_cast1", align_bytes=64, offset=16384),
+            late.tile([P, P * PACK], BF16, name="w_cast2", align_bytes=64, offset=12224),
+            late.tile([P, P * PACK], BF16, name="w_cast3", align_bytes=64, offset=17344),
         ]
-        w_half = late.tile([P, 64 * PACK], BF16, name="w_half", align_bytes=64, offset=11520)
-        w_last = late.tile([P, 64 * PACK], BF16, name="w_last", align_bytes=64, offset=21632)
-        scores(0, CHUNK)
-        scores(CHUNK, CHUNK)
-        cast(w_cast[2], 2, nc.scalar.copy)
-        scores(HALF, CHUNK)
+        for lo in (0, CHUNK, HALF):
+            sigmoids(lo, passes(lo))
+        last = passes(HALF + CHUNK)
 
-        cast(w_cast[0], 0, nc.vector.tensor_copy)
+        dst, src = woven(w_cast[0][:, 0 : PIECE * PACK], 0, PIECE)
+        nc.vector.tensor_scalar(dst, src, unit[:], None, MULT)
+        nc.vector.tensor_copy(*woven(w_cast[0][:, PIECE * PACK : P * PACK], PIECE, PIECE))
         pool_cast(w_cast[1][:], P, P)
-        weigh(0, CHUNK)
-        weigh(CHUNK, CHUNK)
+        weigh(0)
+        weigh(CHUNK)
         for a in range(2):
-            quantise(w_codes, w_scales, a * P, P, w_cast[a][:])
-        pool_cast(w_last[:], 3 * P + 64, 64)
-        last = passes(HALF + CHUNK, CHUNK)
-        nc.scalar.copy(
-            w_half[:].rearrange("p (c i j) -> p c j i", i=RUN, j=PACK),
-            w_raw[1][:, :, P : P + 64].rearrange("p j (c i) -> p c j i", i=RUN),
-        )
+            quantise_w(a, w_cast[a])
+        nc.scalar.copy(*woven(w_cast[2][:], 2 * P, P))
+        nc.scalar.copy(*woven(w_cast[3][:, 0 : PIECE * PACK], 3 * P, PIECE))
+        pool_cast(w_cast[3][:, PIECE * PACK : P * PACK], 3 * P + PIECE, PIECE)
         sigmoids(HALF + CHUNK, last)
         quantise_z(0, HALF, z_first[:])
-        weigh(HALF, CHUNK)
-        for lo, width, src in ((0, P, w_cast[2]), (P, 64, w_half), (P + 64, 64, w_last)):
-            nc.vector.quantize_mx(
-                out=w_codes[:, HALF + lo : HALF + lo + width].bitcast(FP8X4), scales=last_scales[:, lo : lo + width], in_=src[:]
-            )
-        weigh(HALF + CHUNK, CHUNK)
+        weigh(HALF)
+        for a in range(2, 4):
+            quantise_w(a, w_cast[a])
+        weigh(HALF + CHUNK)
         for a in range(4):
             finish(0, a, [product(a, 0, HALF)], nc.scalar.copy)
         banks = {}

@@ -82,15 +82,12 @@ def tile_picked_sigattn_sigmoid_p_kernel(
         nc.scalar.copy(kb_early[:], gn_bank[:, KB_ROW : KB_ROW + 2 * PACK - 1 : 2])
         nc.scalar.copy(kb_sb[:], gn_bank[:, KB_ROW : KB_ROW + 2 * PACK - 1 : 2])
 
-        picked = late.tile([P, H + HALF], U8, name="picked", align_bytes=64, offset=10688)
-        picked_late = keep.tile([P, HALF], U8, name="picked_late", align_bytes=64)
+        picked = late.tile([P, H + S], U8, name="picked", align_bytes=64, offset=10752)
         nc.vector.tensor_copy(picked[:, 0:H], d_scale_table[:].indirect(kidx_sb[:]))
-        nc.vector.tensor_copy(picked[:, H : H + HALF], x_scale_table[:].indirect(offs_sb[:, 0:16]))
-        nc.vector.tensor_copy(picked_late[:], x_scale_table[:].indirect(offs_sb[:, 16:32]))
+        nc.vector.tensor_copy(picked[:, H : H + S], x_scale_table[:].indirect(offs_sb[:]))
         for r in range(4):
-            nc.scalar.dma_start(rows[r:P:32, 0 : H + HALF].bitcast(I32), picked[8 * r : P : 32, :].bitcast(I32))
-        for r in range(4):
-            nc.scalar.dma_start(rows[r:P:32, H + HALF : H + S].bitcast(I32), picked_late[8 * r : P : 32, :].bitcast(I32))
+            queue = nc.scalar if r % 2 else nc.sync
+            queue.dma_start(rows[r:P:32, :].bitcast(I32), picked[8 * r : P : 32, :].bitcast(I32))
 
         w_rows = w1.rearrange("(p j) m -> p j m", j=PACK)
         w_raw = [late.tile([P, PACK, HALF], F32, name="w_raw%d" % h, align_bytes=64, offset=4160 * h) for h in range(2)]
@@ -107,18 +104,24 @@ def tile_picked_sigattn_sigmoid_p_kernel(
                 d_picked[h][:].rearrange("p (c i t) -> p c t i", t=PACK, i=RUN),
             )
 
-        key_scales = keep.tile([P, H], U8, name="key_scales", align_bytes=64)
-        nc.vector.tensor_copy(
-            key_scales[:].rearrange("p (t m) -> p m t", t=PACK),
-            rows[:, 0:H].rearrange("p (m t) -> p m t", t=PACK),
-        )
         queries = {
             0: late.tile([P, CHUNK], U32, name="queries0", align_bytes=64, offset=10240),
             CHUNK: late.tile([P, CHUNK], U32, name="queries1", align_bytes=64, offset=10752),
             HALF: late.tile([P, HALF], U32, name="queries2", align_bytes=64, offset=11264),
         }
-        for lo, width in ((0, CHUNK), (CHUNK, CHUNK), (HALF, HALF)):
+
+        def gather_queries(lo, width):
             nc.vector.tensor_copy(queries[lo][:], x_table[:].indirect(offs_sb[:, lo // 16 : (lo + width) // 16]))
+
+        key_scales = keep.tile([P, H], U8, name="key_scales", align_bytes=64)
+        gather_queries(0, CHUNK)
+        for tiles in (slice(0, 1), slice(1, PACK)):
+            nc.vector.tensor_copy(
+                key_scales[:].rearrange("p (t m) -> p m t", t=PACK)[:, :, tiles],
+                rows[:, 0:H].rearrange("p (m t) -> p m t", t=PACK)[:, :, tiles],
+            )
+        gather_queries(CHUNK, CHUNK)
+        gather_queries(HALF, HALF)
 
         sig = {
             0: keep.tile([P, PACK, CHUNK], F32, name="sig0", align_bytes=64),

@@ -23,8 +23,7 @@ RUN = 4
 CHUNK = 128
 HALF = 256
 PIECE = 64
-LEAD = 448
-MID = 960
+LEAD = 640
 BANKS = 7
 GN_ROW = P - 2
 KB_ROW = P - 1
@@ -63,14 +62,13 @@ def tile_picked_sigattn_sigmoid_p_kernel(
 
         d_src = d_words[0].rearrange("p c r -> p (c r)").bitcast(I32)
         nc.scalar.dma_start(key_rows[GN_ROW : GN_ROW + 1, :], gn.rearrange("h o -> o h"))
+        nc.sync.dma_start(d_table[:, 0:LEAD].bitcast(I32), d_src[:, 0:LEAD])
         nc.scalar.dma_start(key_rows[KB_ROW : KB_ROW + 1, :], kb.rearrange("h o -> o h"))
         nc.sync.dma_start(kidx_sb[:], kidx)
         nc.sync.dma_start(offs_sb[:], offs)
-        nc.sync.dma_start(d_table[:, 0:LEAD].bitcast(I32), d_src[:, 0:LEAD])
         nc.sync.dma_start(d_scale_table[0:P:8, :].bitcast(I32), d_scales[0].bitcast(I32))
-        nc.sync.dma_start(d_table[:, LEAD:MID].bitcast(I32), d_src[:, LEAD:MID])
         nc.sync.dma_start(x_scale_table[0:P:8, :].bitcast(I32), x_scales[0].bitcast(I32))
-        nc.sync.dma_start(d_table[:, MID:G].bitcast(I32), d_src[:, MID:G])
+        nc.sync.dma_start(d_table[:, LEAD:G].bitcast(I32), d_src[:, LEAD:G])
         nc.sync.dma_start(x_table[:].bitcast(I32), x_words[0].rearrange("p c r -> p (c r)").bitcast(I32))
         nc.scalar.activation(warm_out[:], warm_in[:], SIGMOID)
 

@@ -38,14 +38,14 @@ def tile_picked_sigattn_sigmoid_p_kernel(
         late = ctx.enter_context(tc.tile_pool(name="late", bufs=1))
         psum = ctx.enter_context(tc.psum_pool(name="psum", bufs=1))
 
-        kidx_sb = keep.tile([P, H // 16], U16, name="kidx_sb")
-        offs_sb = keep.tile([P, S // 16], U16, name="offs_sb")
-        d_table = keep.tile([P, G], U32, name="d_table", align_bytes=64)
-        x_table = keep.tile([P, T], U32, name="x_table", align_bytes=64)
-        d_scale_table = keep.tile([P, G], U8, name="d_scale_table", align_bytes=64)
-        x_scale_table = late.tile([P, T], U8, name="x_scale_table", align_bytes=64, offset=4032)
-        rows = keep.tile([P, H + S], U8, name="rows", align_bytes=64)
-        key_rows = keep.tile([P, H], F32, name="key_rows", align_bytes=64)
+        kidx_sb = keep.tile([P, H // 16], U16, name="kidx_sb", align_bytes=64)
+        offs_sb = keep.tile([P, S // 16], U16, name="offs_sb", align_bytes=64)
+        d_table = keep.tile([P, G], U32, name="d_table", align_bytes=256)
+        x_table = keep.tile([P, T], U32, name="x_table", align_bytes=256)
+        d_scale_table = keep.tile([P, G], U8, name="d_scale_table", align_bytes=256)
+        x_scale_table = late.tile([P, T], U8, name="x_scale_table", align_bytes=256, offset=3072)
+        rows = keep.tile([P, H + S], U8, name="rows", align_bytes=256)
+        key_rows = keep.tile([P, H], F32, name="key_rows", align_bytes=256)
         identity = keep.tile([P, P], F32, name="identity", align_bytes=64)
         unit = late.tile([P, 1], F32, name="unit", align_bytes=64, offset=16384)
         warm_in = keep.tile([P, 8], F32, name="warm_in")
@@ -80,7 +80,7 @@ def tile_picked_sigattn_sigmoid_p_kernel(
         nc.scalar.copy(kb_early[:], gn_bank[:, KB_ROW : KB_ROW + 2 * PACK - 1 : 2])
         nc.scalar.copy(kb_sb[:], gn_bank[:, KB_ROW : KB_ROW + 2 * PACK - 1 : 2])
 
-        picked = late.tile([P, H + S], U8, name="picked", align_bytes=64, offset=10752)
+        picked = late.tile([P, H + S], U8, name="picked", align_bytes=256, offset=10752)
         nc.vector.tensor_copy(picked[:, 0:H], d_scale_table[:].indirect(kidx_sb[:]))
         nc.vector.tensor_copy(picked[:, H : H + S], x_scale_table[:].indirect(offs_sb[:]))
         for r in range(4):
@@ -88,7 +88,7 @@ def tile_picked_sigattn_sigmoid_p_kernel(
             queue.dma_start(rows[r:P:32, :].bitcast(I32), picked[8 * r : P : 32, :].bitcast(I32))
 
         w_rows = w1.rearrange("(p j) m -> p j m", j=PACK)
-        w_raw = [late.tile([P, PACK, HALF], F32, name="w_raw%d" % h, align_bytes=64, offset=4160 * h) for h in range(2)]
+        w_raw = [late.tile([P, PACK, HALF], F32, name="w_raw%d" % h, align_bytes=256, offset=4096 * h) for h in range(2)]
         nc.sync.dma_start(w_raw[0][:], w_rows[:, :, 0:HALF])
         nc.sync.dma_start(w_raw[1][:], w_rows[:, :, HALF:N])
 
@@ -214,7 +214,7 @@ def tile_picked_sigattn_sigmoid_p_kernel(
             return bank
 
         def finish(lo, a, banks, copy):
-            res = keep.tile([P, HALF], F32, name="res%d_%d" % (lo, a), align_bytes=64)
+            res = keep.tile([P, HALF], F32, name="res%d_%d" % (lo, a), align_bytes=256)
             width = HALF // len(banks)
             for u, bank in enumerate(banks):
                 copy(res[:, u * width : (u + 1) * width], bank[:])

@@ -213,12 +213,10 @@ def tile_picked_sigattn_sigmoid_p_kernel(
             )
             return bank
 
-        def finish(lo, a, banks, copy):
-            res = keep.tile([P, HALF], F32, name="res%d_%d" % (lo, a), align_bytes=256)
-            width = HALF // len(banks)
-            for u, bank in enumerate(banks):
-                copy(res[:, u * width : (u + 1) * width], bank[:])
-            nc.sync.dma_start(out[a * P : (a + 1) * P, lo : lo + HALF], res[:])
+        def finish(lo, a, bank, width, copy):
+            res = keep.tile([P, width], F32, name="res%d_%d" % (lo, a), align_bytes=256)
+            copy(res[:], bank[:])
+            nc.sync.dma_start(out[a * P : (a + 1) * P, lo : lo + width], res[:])
 
         w_cast = [
             late.tile([P, P * PACK], BF16, name="w_cast0", align_bytes=64, offset=9280),
@@ -248,12 +246,13 @@ def tile_picked_sigattn_sigmoid_p_kernel(
             quantise_w(a, w_cast[a])
         weigh(HALF + CHUNK)
         for a in range(4):
-            finish(0, a, [product(a, 0, HALF)], nc.scalar.copy)
-        banks = {}
+            finish(0, a, product(a, 0, HALF), HALF, nc.scalar.copy)
+        out_tiles = out.rearrange("(a p) m -> p a m", p=P)
         for o in (0, CHUNK):
             quantise_z(HALF + o, CHUNK, z_second[:, o * PACK : (o + CHUNK) * PACK])
-            for a in range(2):
-                banks[a, o] = product(a, HALF + o, CHUNK)
-        for a in range(4):
-            parts = [banks[a, 0], banks[a, CHUNK]] if a < 2 else [product(a, HALF, HALF)]
-            finish(HALF, a, parts, nc.scalar.copy if a % 2 else nc.vector.tensor_copy)
+            pair = keep.tile([P, 2, CHUNK], F32, name="pair%d" % o, align_bytes=256)
+            for a, copy in enumerate((nc.vector.tensor_copy, nc.scalar.copy)):
+                copy(pair[:, a, :], product(a, HALF + o, CHUNK)[:])
+            nc.sync.dma_start(out_tiles[:, 0:2, HALF + o : HALF + o + CHUNK], pair[:])
+        for a in range(2, 4):
+            finish(HALF, a, product(a, HALF, HALF), HALF, nc.scalar.copy if a % 2 else nc.vector.tensor_copy)

@@ -23,7 +23,7 @@ RUN = 4
 CHUNK = 128
 HALF = 256
 PIECE = 64
-LEAD = 640
+LEAD = 512
 BANKS = 7
 GN_ROW = P - 2
 KB_ROW = P - 1
@@ -54,11 +54,11 @@ def tile_picked_sigattn_sigmoid_p_kernel(
         nc.vector.memset(d_scale_table[:].bitcast(I32), 0)
         nc.vector.memset(x_scale_table[:].bitcast(I32), 0)
         nc.vector.memset(warm_in[:], 0.0)
+        nc.vector.memset(identity[:], 0.0)
+        make_identity(nc, identity[:], nomemset=True)
         nc.vector.memset(key_rows[0:GN_ROW, :], 0.0)
         nc.vector.memset(rows[:].bitcast(I32), 0)
         nc.vector.memset(unit[:], 1.0)
-        nc.vector.memset(identity[:], 0.0)
-        make_identity(nc, identity[:], nomemset=True)
 
         d_src = d_words[0].rearrange("p c r -> p (c r)").bitcast(I32)
         nc.scalar.dma_start(key_rows[GN_ROW : GN_ROW + 1, :], gn.rearrange("h o -> o h"))

from contextlib import ExitStack

import concourse.mybir as mybir
from concourse.masks import make_identity

K, T, S, N, G, H = 512, 2048, 512, 512, 2048, 512
FLOPS = 2 * K * H * S + 2 * H * N * S

F32 = mybir.dt.float32
BF16 = mybir.dt.bfloat16
U32 = mybir.dt.uint32
I32 = mybir.dt.int32
U16 = mybir.dt.uint16
U8 = mybir.dt.uint8
FP8X4 = mybir.dt.float8_e4m3fn_x4
SIGMOID = mybir.ActivationFunctionType.Sigmoid
MULT = mybir.AluOpType.mult
ADD = mybir.AluOpType.add

P = 128
PACK = 4
RUN = 4
CHUNK = 128
HALF = 256
PIECE = 64
LEAD = 512
BANKS = 7
GN_ROW = P - 2
KB_ROW = P - 1


def tile_picked_sigattn_sigmoid_p_kernel(
    tc, x_words, x_scales, d_words, d_scales, kb, gn, w1, offs, kidx, out
):
    nc = tc.nc
    with ExitStack() as ctx:
        keep = ctx.enter_context(tc.tile_pool(name="keep", bufs=1))
        late = ctx.enter_context(tc.tile_pool(name="late", bufs=1))
        psum = ctx.enter_context(tc.psum_pool(name="psum", bufs=1))

        kidx_sb = keep.tile([P, H // 16], U16, name="kidx_sb", align_bytes=64)
        offs_sb = keep.tile([P, S // 16], U16, name="offs_sb", align_bytes=64)
        d_table = keep.tile([P, G], U32, name="d_table", align_bytes=256)
        x_table = keep.tile([P, T], U32, name="x_table", align_bytes=256)
        d_scale_table = keep.tile([P, G], U8, name="d_scale_table", align_bytes=256)
        x_scale_table = late.tile([P, T], U8, name="x_scale_table", align_bytes=256, offset=3072)
        rows = keep.tile([P, H + S], U8, name="rows", align_bytes=256)
        key_rows = keep.tile([P, H], F32, name="key_rows", align_bytes=256)
        identity = keep.tile([P, P], F32, name="identity", align_bytes=64)
        unit = late.tile([P, 1], F32, name="unit", align_bytes=64, offset=16384)
        warm_in = keep.tile([P, 8], F32, name="warm_in")
        warm_out = keep.tile([P, 8], F32, name="warm_out")

        nc.vector.memset(d_scale_table[:].bitcast(I32), 0)
        nc.vector.memset(x_scale_table[:].bitcast(I32), 0)
        nc.vector.memset(warm_in[:], 0.0)
        nc.vector.memset(identity[:], 0.0)
        make_identity(nc, identity[:], nomemset=True)
        nc.vector.memset(key_rows[0:GN_ROW, :], 0.0)
        nc.vector.memset(rows[:].bitcast(I32), 0)
        nc.vector.memset(unit[:], 1.0)

        d_src = d_words[0].rearrange("p c r -> p (c r)").bitcast(I32)
        nc.scalar.dma_start(key_rows[GN_ROW : GN_ROW + 1, :], gn.rearrange("h o -> o h"))
        nc.sync.dma_start(d_table[:, 0:LEAD].bitcast(I32), d_src[:, 0:LEAD])
        nc.scalar.dma_start(key_rows[KB_ROW : KB_ROW + 1, :], kb.rearrange("h o -> o h"))
        nc.sync.dma_start(kidx_sb[:], kidx)
        nc.sync.dma_start(offs_sb[:], offs)
        nc.sync.dma_start(d_scale_table[0:P:8, :].bitcast(I32), d_scales[0].bitcast(I32))
        nc.sync.dma_start(x_scale_table[0:P:8, :].bitcast(I32), x_scales[0].bitcast(I32))
        nc.sync.dma_start(d_table[:, LEAD:G].bitcast(I32), d_src[:, LEAD:G])
        nc.sync.dma_start(x_table[:].bitcast(I32), x_words[0].rearrange("p c r -> p (c r)").bitcast(I32))
        nc.scalar.activation(warm_out[:], warm_in[:], SIGMOID)

        gn_bank = psum.tile([P, P + 2 * PACK], F32, name="gn_bank")
        for t in reversed(range(PACK)):
            nc.tensor.transpose(gn_bank[:, 2 * t : 2 * t + P], key_rows[:, t:H:PACK], identity[:])
        kb_sb = late.tile([P, PACK], F32, name="kb_sb", align_bytes=64, offset=28672)
        kb_early = late.tile([P, PACK], F32, name="kb_early", align_bytes=64, offset=24576)
        nc.scalar.copy(kb_early[:], gn_bank[:, KB_ROW : KB_ROW + 2 * PACK - 1 : 2])
        nc.scalar.copy(kb_sb[:], gn_bank[:, KB_ROW : KB_ROW + 2 * PACK - 1 : 2])

        picked = late.tile([P, H + S], U8, name="picked", align_bytes=256, offset=10752)
        nc.vector.tensor_copy(picked[:, 0:H], d_scale_table[:].indirect(kidx_sb[:]))
        nc.vector.tensor_copy(picked[:, H : H + S], x_scale_table[:].indirect(offs_sb[:]))
        for r in range(4):
            queue = nc.scalar if r % 2 else nc.sync
            queue.dma_start(rows[r:P:32, :].bitcast(I32), picked[8 * r : P : 32, :].bitcast(I32))

        w_rows = w1.rearrange("(p j) m -> p j m", j=PACK)
        w_raw = [late.tile([P, PACK, HALF], F32, name="w_raw%d" % h, align_bytes=256, offset=4096 * h) for h in range(2)]
        nc.sync.dma_start(w_raw[0][:], w_rows[:, :, 0:HALF])
        nc.sync.dma_start(w_raw[1][:], w_rows[:, :, HALF:N])

        keys = keep.tile([P, H], U32, name="keys", align_bytes=64)
        d_picked = [keep.tile([P, HALF], U32, name="d_picked%d" % h, align_bytes=64) for h in range(2)]
        for h in range(2):
            nc.vector.tensor_copy(d_picked[h][:], d_table[:].indirect(kidx_sb[:, h * 16 : (h + 1) * 16]))
        for h in range(2):
            nc.vector.tensor_copy(
                keys[:].rearrange("p (t g c i) -> p g c t i", t=PACK, g=2, i=RUN)[:, h],
                d_picked[h][:].rearrange("p (c i t) -> p c t i", t=PACK, i=RUN),
            )

        queries = {
            0: late.tile([P, CHUNK], U32, name="queries0", align_bytes=64, offset=10240),
            CHUNK: late.tile([P, CHUNK], U32, name="queries1", align_bytes=64, offset=10752),
            HALF: late.tile([P, HALF], U32, name="queries2", align_bytes=64, offset=11264),
        }

        def gather_queries(lo, width):
            nc.vector.tensor_copy(queries[lo][:], x_table[:].indirect(offs_sb[:, lo // 16 : (lo + width) // 16]))

        key_scales = keep.tile([P, H], U8, name="key_scales", align_bytes=64)
        gather_queries(0, CHUNK)
        for tiles in (slice(0, 1), slice(1, PACK)):
            nc.vector.tensor_copy(
                key_scales[:].rearrange("p (t m) -> p m t", t=PACK)[:, :, tiles],
                rows[:, 0:H].rearrange("p (m t) -> p m t", t=PACK)[:, :, tiles],
            )
        gather_queries(CHUNK, CHUNK)
        gather_queries(HALF, HALF)

        sig = {
            0: keep.tile([P, PACK, CHUNK], F32, name="sig0", align_bytes=64),
            CHUNK: keep.tile([P, PACK, CHUNK], F32, name="sig1", align_bytes=64),
            HALF: keep.tile([P, PACK, CHUNK], F32, name="sig2", align_bytes=64),
            HALF + CHUNK: keep.tile([P, PACK, CHUNK], F32, name="sig3", align_bytes=64),
        }

        def passes(lo):
            banks = []
            first = min(lo, HALF)
            for t in range(PACK):
                bank = psum.tile([P, CHUNK], F32, name="score", tag="bank", bufs=BANKS)
                nc.tensor.matmul_mx(
                    out=bank[:],
                    lhsT=keys[:, t * P : (t + 1) * P].bitcast(FP8X4),
                    lhsT_scale=key_scales[:, t * P : (t + 1) * P],
                    rhs=queries[first][:, lo - first : lo - first + CHUNK].bitcast(FP8X4),
                    rhs_scale=rows[:, H + lo : H + lo + CHUNK],
                    start=True,
                    stop=True,
                )
                banks.append(bank)
            return banks

        def sigmoids(lo, banks):
            bias = kb_early if lo < HALF else kb_sb
            for t in range(PACK):
                nc.scalar.activation(sig[lo][:, t, :], banks[t][:], SIGMOID, bias=bias[:, t : t + 1], scale=0.0625)

        z_first = keep.tile([P, HALF * PACK], BF16, name="z_first", align_bytes=64)
        z_second = keep.tile([P, HALF * PACK], BF16, name="z_second", align_bytes=64)
        w_codes = keep.tile([P, N], U32, name="w_codes", align_bytes=64)
        w_scales = late.tile([P, HALF], U8, name="w_scales", align_bytes=64, offset=24576)
        last_scales = keep.tile([P, HALF], U8, name="last_scales", align_bytes=64)
        z_codes = keep.tile([P, S], U32, name="z_codes", align_bytes=64)
        z_scales = [
            keep.tile([P, HALF], U8, name="z_scales0", align_bytes=64),
            late.tile([P, HALF], U8, name="z_scales1", align_bytes=64, offset=28672),
        ]

        def woven(dst, lo, width):
            h, o = divmod(lo, HALF)
            return (
                dst.rearrange("p (c i j) -> p c j i", i=RUN, j=PACK),
                w_raw[h][:, :, o : o + width].rearrange("p j (c i) -> p c j i", i=RUN),
            )

        def pool_cast(dst, lo, width):
            h, o = divmod(lo, HALF)
            nc.gpsimd.tensor_scalar(
                dst.rearrange("p (m j) -> p m j", j=PACK),
                w_raw[h][:, :, o : o + width].rearrange("p j m -> p m j"),
                1.0,
                0.0,
                MULT,
                ADD,
            )

        def quantise_w(a, src):
            scales = w_scales if a < 2 else last_scales
            nc.vector.quantize_mx(
                out=w_codes[:, a * P : (a + 1) * P].bitcast(FP8X4), scales=scales[:, a % 2 * P : (a % 2 + 1) * P], in_=src[:]
            )

        def quantise_z(lo, width, src):
            h, o = divmod(lo, HALF)
            nc.vector.quantize_mx(out=z_codes[:, lo : lo + width].bitcast(FP8X4), scales=z_scales[h][:, o : o + width], in_=src)

        def weigh(lo):
            h, o = divmod(lo, HALF)
            z = z_second if h else z_first
            nc.vector.tensor_tensor(
                z[:, o * PACK : (o + CHUNK) * PACK].rearrange("p (c i t) -> p c t i", i=RUN, t=PACK),
                sig[lo][:].rearrange("p t (c i) -> p c t i", i=RUN),
                gn_bank[:, GN_ROW : GN_ROW + 2 * PACK : 2].unsqueeze(1).unsqueeze(3).broadcast_to([P, CHUNK // RUN, PACK, RUN]),
                MULT,
            )

        def product(a, lo, width):
            bank = psum.tile([P, width], F32, name="acc", tag="bank", bufs=BANKS)
            scales = w_scales if a < 2 else last_scales
            nc.tensor.matmul_mx(
                out=bank[:],
                lhsT=w_codes[:, a * P : (a + 1) * P].bitcast(FP8X4),
                lhsT_scale=scales[:, a % 2 * P : (a % 2 + 1) * P],
                rhs=z_codes[:, lo : lo + width].bitcast(FP8X4),
                rhs_scale=z_scales[lo // HALF][:, lo % HALF : lo % HALF + width],
                start=True,
                stop=True,
            )
            return bank

        def finish(lo, a, bank, width, copy):
            res = keep.tile([P, width], F32, name="res%d_%d" % (lo, a), align_bytes=256)
            copy(res[:], bank[:])
            nc.sync.dma_start(out[a * P : (a + 1) * P, lo : lo + width], res[:])

        w_cast = [
            late.tile([P, P * PACK], BF16, name="w_cast0", align_bytes=64, offset=9280),
            late.tile([P, P * PACK], BF16, name="w_cast1", align_bytes=64, offset=16384),
            late.tile([P, P * PACK], BF16, name="w_cast2", align_bytes=64, offset=12224),
            late.tile([P, P * PACK], BF16, name="w_cast3", align_bytes=64, offset=17344),
        ]
        for lo in (0, CHUNK, HALF):
            sigmoids(lo, passes(lo))
        last = passes(HALF + CHUNK)

        dst, src = woven(w_cast[0][:, 0 : PIECE * PACK], 0, PIECE)
        nc.vector.tensor_scalar(dst, src, unit[:], None, MULT)
        nc.vector.tensor_copy(*woven(w_cast[0][:, PIECE * PACK : P * PACK], PIECE, PIECE))
        pool_cast(w_cast[1][:], P, P)
        weigh(0)
        weigh(CHUNK)
        for a in range(2):
            quantise_w(a, w_cast[a])
        nc.scalar.copy(*woven(w_cast[2][:], 2 * P, P))
        nc.scalar.copy(*woven(w_cast[3][:, 0 : PIECE * PACK], 3 * P, PIECE))
        pool_cast(w_cast[3][:, PIECE * PACK : P * PACK], 3 * P + PIECE, PIECE)
        sigmoids(HALF + CHUNK, last)
        quantise_z(0, HALF, z_first[:])
        weigh(HALF)
        for a in range(2, 4):
            quantise_w(a, w_cast[a])
        weigh(HALF + CHUNK)
        for a in range(4):
            finish(0, a, product(a, 0, HALF), HALF, nc.scalar.copy)
        out_tiles = out.rearrange("(a p) m -> p a m", p=P)
        for o in (0, CHUNK):
            quantise_z(HALF + o, CHUNK, z_second[:, o * PACK : (o + CHUNK) * PACK])
            pair = keep.tile([P, 2, CHUNK], F32, name="pair%d" % o, align_bytes=256)
            for a, copy in enumerate((nc.vector.tensor_copy, nc.scalar.copy)):
                copy(pair[:, a, :], product(a, HALF + o, CHUNK)[:])
            nc.sync.dma_start(out_tiles[:, 0:2, HALF + o : HALF + o + CHUNK], pair[:])
        for a in range(2, 4):
            finish(HALF, a, product(a, HALF, HALF), HALF, nc.scalar.copy if a % 2 else nc.vector.tensor_copy)
